import numpy as np, ml_dtypes
CORES = [6,15,38,47]
N = 4
BF = ml_dtypes.bfloat16
def gentries(a):
    return np.ascontiguousarray(a.reshape(8, 16, -1).transpose(0, 2, 1)).reshape(8, -1)
def gtable(e):
    e = np.asarray(e); return np.ascontiguousarray(e.reshape(8, -1, 16).transpose(0, 2, 1)).reshape(128, -1).astype(np.int32)
def f(rng, *shape):
    return (rng.standard_normal(shape, dtype=np.float32) * np.exp2(rng.integers(-2, 3, shape[:-1] + (1,)))).astype(BF)
def wide(rng, *shape):
    v = f(rng, *shape).astype(np.float32); k = shape[:-2] + (1, shape[-1])
    return (v * np.exp2(rng.integers(-6, 7, k)) * (rng.random(k) > 0.0625)).astype(BF)
V, B, CAP, RO, HI, LO, M = 960, 64, 256, 6, 9, 4, 4096
FP = (N - 1) * B
def face(x, y, fs):
    p = np.zeros(4 * V, np.int64); p[x] = y; p[y] = x; p[fs] = 4 * V + np.arange(FP)
    return p
def mate(rng, a):
    a = rng.permutation(a); x, y = a[0::2].copy(), a[1::2].copy()
    for i in np.flatnonzero(x >> 2 == y >> 2):
        if x[i] >> 2 != y[i] >> 2: continue
        j = rng.choice(np.flatnonzero((x >> 2 != x[i] >> 2) & (y >> 2 != x[i] >> 2)))
        y[i], y[j] = int(y[j]), int(y[i])
    return x, y
def wire(rng, half=None, px=(), py=(), must=(), cell=0):
    px, py, must = np.array(px, np.int64), np.array(py, np.int64), np.array(must, np.int64)
    free = np.ones(4 * V, bool); free[px] = False; free[py] = False; free[must] = False
    a = np.flatnonzero(free); a = a[(a >> 2) >= cell]
    if half is None: fs = rng.permutation(a)[:FP - len(must)]
    else:
        h = half[a >> 2]; n = FP // 2 - len(must) // 2
        fs = np.concatenate([rng.permutation(a[h])[:n], rng.permutation(a[~h])[:n]])
    fs = np.concatenate([must[:1], rng.permutation(fs), must[1:]]); free[fs] = False; a = np.flatnonzero(free)
    if half is None: x, y = mate(rng, a)
    else:
        h = half[a >> 2]; c = (a >> 2) < cell
        x = np.concatenate([a[h & c], a[h & ~c]]); y = np.concatenate([rng.permutation(a[~h & c]), rng.permutation(a[~h & ~c])])
    return face(np.concatenate([x, px]), np.concatenate([y, py]), fs), fs
def seeds(rng, m):
    o = rng.permutation(V); st = np.sort(o[:m]); w = np.sort(o[m:]); give = np.zeros(V - m, bool)
    if m > 0:
        give[0] = True; give[1 + rng.permutation(V - m - 1)[:m - 1]] = True
    j = np.flatnonzero(~give); j = j[j > 0]
    px = np.concatenate([4 * rng.permutation(st) + 1, 4 * w[j - 1] + 1]); py = np.concatenate([4 * w[give], 4 * w[j]])
    free = np.ones(4 * V, bool); free[px] = False; free[py] = False
    s = np.flatnonzero(free); first = np.isin(s >> 2, st); a = s[first]; b = rng.permutation(s[~first])
    if m == 0: b = np.concatenate([np.zeros(1, np.int64), b[b != 0]])
    fs = rng.permutation(b[:FP]); b = b[FP:]; x, y = mate(rng, b[len(a):])
    return face(np.concatenate([px, a, x]), np.concatenate([py, b[:len(a)], y]), fs), fs, st
def knit(rng, px, py, fo, st):
    z = rng.integers(0, 2, (FP // 2, 1)); fs = (4 * fo[:, None] + 2 + np.concatenate([z, 1 - z], axis=1)).reshape(-1)
    free = np.ones(4 * V, bool); free[px] = False; free[py] = False; free[fs] = False
    s = np.flatnonzero(free); first = np.isin(s >> 2, st); a = s[first]; b = rng.permutation(s[~first]); x, y = mate(rng, b[len(a):])
    return face(np.concatenate([px, a, x]), np.concatenate([py, b[:len(a)], y]), fs), fs
def chain(rng, st, fo):
    m = len(st); w = np.setdiff1d(np.arange(V), st); give = np.zeros(V - m, bool); give[0] = True; give[1 + rng.permutation(V - m - 1)[:m - 1]] = True
    j = np.flatnonzero(~give)
    return knit(rng, np.concatenate([4 * rng.permutation(st) + 1, 4 * w[j - 1] + 1]), np.concatenate([4 * w[give], 4 * w[j]]), fo, st)
def blank():
    return np.zeros((N, 8, 4 * V), np.int64), np.zeros((N, 8, FP), np.int64), np.zeros((N, 8, V), np.int64), np.ones((N, 8, V), np.int64)
def mixed(rng):
    port, rim, t, d = blank()
    for r in range(N):
        k = rng.permutation(8)
        for g in range(8):
            if k[g] < 4:
                port[r, g], rim[r, g] = wire(rng); t[r, g] = rng.integers(0, 4, V); d[r, g] = 2 ** rng.integers(0, 3, V)
            else:
                half = np.zeros(V, bool); half[rng.permutation(V)[:V // 2]] = True
                port[r, g], rim[r, g] = wire(rng, half)
                t[r, g] = np.where(half, rng.integers(0, 2, V), rng.integers(2, 4, V)); d[r, g] = np.where(half, 2 ** rng.integers(0, 2, V), 2 ** rng.integers(0, 3, V))
    return port, rim, t, d
def limit(x, m):
    return np.clip(np.asarray(x).astype(np.float32), -m, m)
def gates(rng, q):
    z = np.std(q.reshape(N, 8, 16, V), axis=3, keepdims=True) * rng.uniform(0.4, 1.1, (N, 8, 1, 1))
    return np.clip(z, 0.0625, 4)
def sized(x):
    x = np.ascontiguousarray(np.reshape(x, (N, 128, V))).astype(np.float32)
    return np.where(np.abs(x) < np.float32(2.0 ** -40), np.float32(0), x).astype(BF)
def pack(q, v, h, t, d, port, rim):
    return {"q0": sized(q), "q1": sized(v),
            "th": np.ascontiguousarray(np.reshape(h, (N, 128, 1))).astype(np.float32), "t0": t.astype(np.int32), "d0": d.astype(np.int32),
            "port": np.stack([gtable(a) for a in port]), "rim": np.stack([gtable(a) for a in rim])}
def setup_inputs(rng):
    port, rim, t, d = mixed(rng); q = limit(f(rng, N, 128, V), 4); v = limit(0.25 * f(rng, N, 128, V).astype(np.float32), 1)
    return pack(q, v, gates(rng, q), t, d, port, rim)
def setup_inputs_spread(rng):
    port, rim, t, d = mixed(rng); q = limit(wide(rng, N, 128, V), 4); v = limit(0.25 * wide(rng, N, 128, V).astype(np.float32), 1)
    q = np.where(q == 0, np.float32(2.0 ** -12), q)
    h = np.clip(np.exp2(rng.uniform(-4, 2, (N, 8, 16, 1))), 0.0625, 4)
    t = np.minimum((4 * rng.random((N, 8, V)) ** 3).astype(np.int64), 3); d = 2 ** np.minimum((3 * rng.random((N, 8, V)) ** 0.5).astype(np.int64), 2)
    return pack(q, v, h, t, d, port, rim)
def setup_inputs_ends(rng):
    port, rim, t, d = blank(); t = 3 * rng.integers(0, 2, (N, 8, V)); d = 1 + 3 * rng.integers(0, 2, (N, 8, V))
    q = 8 * rng.integers(0, 2, (N, 8, 16, V)) - 4; v = 2 * rng.integers(0, 2, (N, 8, 16, V)) - 1
    h = np.where(rng.random((N, 8, 16, 1)) < 0.5, 0.0625, 4.0); half = np.arange(V) < V // 2
    for r in range(N):
        k = rng.permutation(8)
        if r == N - 1:
            i = int(np.flatnonzero(k == 4)[0]); k[i], k[7] = int(k[7]), 4
        for g in range(8):
            odd = (r + g) % 2 == 1
            px, py, must = ((), (), (0, 4 * V - 1)) if odd else ((0,), (4 * V - 1,), ())
            if k[g] < 4:
                low = rng.permutation(16) < (0, LO, LO + 1, HI - 1)[k[g]]
                h[r, g, :, 0] = np.where(low, 0.0625, 4.0); q[r, g] = np.where(low[:, None], q[r, g], np.where(half, -4, 4)[None, :])
                port[r, g], rim[r, g] = wire(rng, half, px, py, must)
            else:
                if k[g] == 4: h[r, g] = 0.0625
                port[r, g], rim[r, g] = wire(rng, None, px, py, must)
            late = (r + g) % 2 == (N + 6) % 2
            t[r, g, V - 2:] = (0, 3) if late else (3, 0); d[r, g, V - 2:] = (1, 4) if late else (4, 1)
    return pack(q, v, h, t, d, port, rim)
def setup_inputs_corners(rng):
    port, rim, t, d = blank(); most = (2 * V - FP) // 4 - 4
    for r in range(N):
        k = rng.permutation(np.array([1, CAP - 1, CAP, CAP, CAP + 1, CAP + 1, most])); k = np.concatenate([k[:5], np.zeros(1, np.int64), k[5:]])
        for g in range(8):
            port[r, g], rim[r, g], st = seeds(rng, int(k[g]))
            i = rng.integers(0, 3, V); t[r, g] = np.array([0, 2, 3])[i]; d[r, g] = np.array([4, 2, 1])[i]
            t[r, g, st] = 0; d[r, g, st] = 1
            if k[g] == 0: t[r, g] = 3; d[r, g] = 4
    q = limit(f(rng, N, 128, V), 4); v = limit(0.25 * f(rng, N, 128, V).astype(np.float32), 1)
    return pack(q, v, gates(rng, q), t, d, port, rim)
def setup_inputs_calm(rng):
    port, rim, t, d = blank(); e = np.arange(V); half = (e < CAP // 2) | ((e >= CAP) & (e < CAP + (V - CAP) // 2))
    q = np.zeros((N, 8, 16, V), np.float32); v = np.zeros((N, 8, 16, V), np.float32); h = np.zeros((N, 8, 16, 1), np.float32)
    kinds = ((LO, 3, 4), (LO, 2, 4), (LO, 0, 4), (HI, 0, 1), (HI, 1, 1), (HI - 1, 0, 2), (LO + 1, 3, 2), (HI - 1, 2, 2))
    for r in range(N):
        k = rng.permutation(8)
        for g in range(8):
            n, a, b = kinds[k[g]]; low = (rng.permutation(16) < n)[:, None]
            z = (0.5 + 2.5 * rng.random((16, 1))).astype(np.float32).astype(BF).astype(np.float32); sg = np.where(half, -1, 1)[None, :]
            any_ = 2 * rng.integers(0, 2, (16, V)) - 1
            q[r, g] = np.where(low, any_ * (1 + 2 * rng.random((16, V))), sg * z)
            v[r, g] = np.where(low, 2 * rng.random((16, V)) - 1, sg * rng.random((16, V)))
            h[r, g] = np.where(low, 0.0625, z); t[r, g] = a; d[r, g] = b
            port[r, g], rim[r, g] = wire(rng, half, (), (), (), CAP)
    return pack(q, v, h, t, d, port, rim)
def setup_inputs_knots(rng):
    port, rim, t, d = blank(); q = limit(f(rng, N, 128, V), 4).reshape(N, 8, 16, V); v = limit(0.25 * f(rng, N, 128, V).astype(np.float32), 1).reshape(N, 8, 16, V)
    h = gates(rng, q); tm = rng.permutation(16)[:2]; nt = np.setdiff1d(np.arange(16), tm); sg = 2 * rng.integers(0, 2, (N, 8, 2, V)) - 1
    q[:, :, tm] = sg * np.exp2(rng.integers(-40, -33, sg.shape).astype(np.float64)) * (1 + 0.0078125 * rng.integers(0, 128, sg.shape))
    v[:, :, tm] = sg * np.exp2(rng.integers(-40, -35, sg.shape).astype(np.float64))
    off = int(rng.integers(0, 2)); ne = (V - FP // 4) // 2; none = np.zeros(0, np.int64)
    for r in range(N):
        k = rng.permutation(4)
        for g in range(8):
            kind = int(k[g // 2])
            if (g + off) % 2 == 0:
                fo = rng.permutation(V)[:FP // 2]; st = np.sort(fo); port[r, g], rim[r, g] = chain(rng, st, fo)
                i = rng.integers(0, 3, V); t[r, g] = np.array([0, 2, 3])[i]; d[r, g] = np.array([4, 2, 1])[i]
                t[r, g, st] = rng.integers(0, 2, FP // 2); d[r, g, st] = 2 - t[r, g, st]
            elif kind == 0:
                fo = rng.permutation(V)[:FP // 2]; i = int(rng.integers(0, FP // 2)); st = fo[i:i + 1]; port[r, g], rim[r, g] = chain(rng, st, fo)
                t[r, g] = 3; d[r, g] = 4; t[r, g, st] = 0; d[r, g, st] = 1; q[r, g] = np.clip(q[r, g], -3, 3); h[r, g] = 4
            elif kind == 1:
                o = 1 + rng.permutation(V - 2); n = FP // 2; fo = o[:n]
                ea = np.concatenate([np.array([0]), o[n:n + 15]]); eb = np.concatenate([np.array([V - 1]), o[n + 15:n + 30]])
                px = (4 * ea[:, None] + np.arange(4)).reshape(-1); py = (4 * eb[:, None] + np.argsort(rng.random((16, 4)), axis=1)).reshape(-1)
                port[r, g], rim[r, g] = knit(rng, px, py, fo, none)
                t[r, g] = rng.integers(0, 4, V); d[r, g] = 2 ** rng.integers(0, 3, V); t[r, g, fo] = rng.integers(0, 2, n); d[r, g, fo] = 4
                t[r, g, ea] = 0; t[r, g, eb] = 0; d[r, g, ea] = 2 ** rng.integers(0, 3, 16); d[r, g, eb] = d[r, g, ea]
            else:
                up = kind == 2; e = np.arange(V); first = (e >= V - ne) if up else (e < ne); s = 1 if up else -1
                fo = rng.permutation(np.flatnonzero(~first))[:FP // 2]; port[r, g], rim[r, g] = knit(rng, none, none, fo, np.flatnonzero(first))
                t[r, g] = 0; d[r, g] = np.where(first, 2, 4)
                o = rng.permutation(nt); n = (LO, HI - 1)[(r + kind) % 2]; lo, ex = o[:n], o[n:]
                z = (1 + 0.9 * rng.random((len(ex), 1))).astype(np.float32).astype(BF).astype(np.float32)
                q[r, g][ex] = s * np.where(first[None, :], z, 2.0 ** -8 * (0.75 + 0.6 * rng.random((len(ex), V))))
                v[r, g][ex] = s * np.where(first[None, :], rng.random((len(ex), V)), 0); h[r, g][ex] = z
                q[r, g][lo] = (2 * rng.integers(0, 2, (n, V)) - 1) * (1 + 2 * rng.random((n, V))); h[r, g][lo] = 0.0625
    return pack(q, v, h, t, d, port, rim)
def check_inputs(d):
    bad = []
    for k, lo, hi in (("q0", -4, 4), ("q1", -1, 1), ("th", 0.0625, 4), ("t0", 0, 3), ("d0", 1, 4), ("port", 0, 4 * V + FP - 1), ("rim", 0, 4 * V - 1)):
        x = np.asarray(d[k]).astype(np.float64)
        if not np.all((x >= lo) & (x <= hi)): bad.append("range of " + k)
        if k in ("q0", "q1") and np.any((x != 0) & (np.abs(x) < 2.0 ** -40)): bad.append(k + " is under 2**-40 in size somewhere and not 0")
    if np.any(np.asarray(d["d0"]) == 3): bad.append("d0 is 3 somewhere")
    if bad: return bad
    p = np.stack([gentries(a) for a in d["port"]]).astype(np.int64); m = np.stack([gentries(a) for a in d["rim"]]).astype(np.int64)
    s = np.arange(4 * V); own = p < 4 * V; back = np.take_along_axis(p, np.where(own, p, 0), 2)
    if np.any(own & (back != s)): bad.append("port: facing slots don't face each other")
    if np.any(own & ((p >> 2) == (s >> 2))): bad.append("port: an element faces itself")
    if np.any(np.add.reduce((~own).astype(np.int64), axis=2) != FP) or np.any(np.take_along_axis(p, m, 2) != 4 * V + np.arange(FP)): bad.append("port and rim: foreign ports")
    return bad
def swap(x):
    y = np.zeros_like(x)
    for r in range(N):
        for d in range(1, N):
            s = (r + d) % N; gs = (np.arange(8) + (1 if r < s else 7)) % 8
            y[r][..., (d - 1) * B:d * B] = x[s][gs][..., (N - d - 1) * B:(N - d) * B]
    return y
def around(x, e):
    b = np.take_along_axis(x, e[:, :, None, :], 3) if x.ndim == 4 else np.take_along_axis(x, e, 2)
    return np.concatenate([x, swap(b)], axis=-1)
def overlap(x0, x1, a, b, tau):
    u = (b - a).astype(np.float32) * x0
    w = (np.float32(0.5) * ((b - tau) ** 2 - (a - tau) ** 2).astype(np.float32)) * x1
    return np.float32(0.03125) * (u + w)
def reference(q0, q1, th, t0, d0, port, rim):
    s0 = q0.astype(np.float32).reshape(N, 8, 16, V); s1 = q1.astype(np.float32).reshape(N, 8, 16, V); h = th.astype(np.float32).reshape(N, 8, 16, 1)
    t = t0.astype(np.int64); dt = d0.astype(np.int64)
    p = np.stack([gentries(a) for a in port]).astype(np.int64); m = np.stack([gentries(a) for a in rim]).astype(np.int64)
    col = np.where(p < 4 * V, p >> 2, p - 3 * V); e = m >> 2
    num = np.zeros((N, 8, V), np.int64) + np.arange(N)[:, None, None] * V + np.arange(V); nx = around(num, e)
    fm = np.zeros((N, 8, 16, 4 * V + FP), np.float32); inv = np.array([0, 1, 0.5, 0, 0.25], np.float32)
    for rnd in range(RO):
        key = M * (t + dt) + num; kn = np.take_along_axis(around(key, e), col, 2).reshape(N, 8, V, 4)
        can = np.all(key[..., None] < kn, axis=3); act = can & (np.add.accumulate(can.astype(np.int64), axis=2) <= CAP)
        x0, x1, tx = around(s0, e), around(s1, e), around(t, e)
        for r in range(N):
            for g in range(8):
                a = np.flatnonzero(act[r, g]); sl = 4 * a[:, None] + np.arange(4); c = p[r, g][sl]; n = col[r, g][sl]
                te = tx[r, g][a][:, None]; tn = tx[r, g][n]; de = dt[r, g][a]; tb = te + de[:, None]; ta = np.minimum(np.maximum(te, tn), tb)
                old = x0[r, g][:, a]
                ie = overlap(old[:, :, None], x1[r, g][:, a][:, :, None], ta, tb, te); ni = overlap(x0[r, g][:, n], x1[r, g][:, n], ta, tb, tn)
                left = nx[r, g][a][:, None] < nx[r, g][n]
                up = np.maximum(np.where(left, ie, ni), np.float32(0)); dn = np.minimum(np.where(left, ni, ie), np.float32(0))
                ph = np.float32(0.5) * (up * up + dn * dn); own = np.where(left, -ph, ph)
                new = old
                for i in range(4): new = new + (fm[r, g][:, sl[:, i]] + own[:, :, i])
                fm[r, g][:, sl] = 0
                fm[r, g][:, c] = fm[r, g][:, c] - own
                s0[r, g][:, a] = new; s1[r, g][:, a] = (new - old) * inv[de]
                cnt = np.add.reduce((np.abs(new) > h[r, g]).astype(np.int64), axis=0)
                t[r, g][a] = tb[:, 0]; dt[r, g][a] = np.where(cnt >= HI, 1, np.where(cnt <= LO, 4, 2))
        come = swap(fm[..., 4 * V:])
        for r in range(N):
            for g in range(8): fm[r, g][:, m[r, g]] = fm[r, g][:, m[r, g]] + come[r, g]
        fm[..., 4 * V:] = 0
    k = fm[..., :4 * V].reshape(N, 8, 16, V, 4)
    ym = ((k[..., 0] + k[..., 1]) + k[..., 2]) + k[..., 3]
    return {"y0": s0.reshape(N, 128, V), "y1": s1.reshape(N, 128, V), "ym": np.ascontiguousarray(ym).reshape(N, 128, V), "yt": np.concatenate([t, dt], axis=2).astype(np.float32)}

@@ -1,0 +1,681 @@
+from concourse.bass import DstId, RemoteDMATransfer
+from concourse.mybir import AluOpType as ALU, ActivationFunctionType as AF
+
+V, B, FP, CAP, RO = 960, 64, 192, 256, 6
+W = 1408
+R = 1216
+LOG = 2 * W
+QLW = LOG + R * RO + 704
+SPL = 32
+F32, BF, I32, U16 = "float32", "bfloat16", "int32", "uint16"
+
+
+def _sb(n, d=F32):
+    return ("sbuf", [128, n], d)
+
+
+SCRATCH = {
+    "PD": ("psum", [128, 1024], F32), "PN": ("psum", [128, 1024], F32), "PF": ("psum", [128, 1024], F32),
+    "P6": ("psum", [128, 512], F32), "P7": ("psum", [128, 512], F32),
+    "QL": _sb(QLW), "WM": _sb(W, BF), "LW": _sb(W, BF), "SW": _sb(W, BF), "GG": _sb(3840, BF),
+    "TI": _sb(V, I32), "TB": _sb(V, BF), "thr": _sb(8),
+    "pt": _sb(240, I32), "rm": _sb(16, I32), "i1": _sb(240, I32), "i2": _sb(240, I32), "i3": _sb(240, I32), "i4": _sb(16, I32),
+    "f1": _sb(240), "f2": _sb(240), "b1": _sb(240, BF), "b2": _sb(240, BF), "FW": _sb(960, BF),
+    "colw": _sb(240, U16), "leftb": _sb(240, BF),
+    "pc": _sb(8, I32), "cc": _sb(64), "rowj": _sb(256), "j16": _sb(256), "QG": _sb(256), "QP": _sb(256), "OH": _sb(16), "OQ": _sb(4),
+    "lohi": _sb(16), "J2": _sb(256), "JM": _sb(256, BF), "MT": _sb(144 * 40, BF), "BI": _sb(2048, BF),
+    "yrow": _sb(256, BF), "yfor": _sb(192, BF), "eperm": _sb(V), "dneg": _sb(64), "R16": _sb(256), "R4": _sb(240),
+    "ones": _sb(64), "dum": _sb(256), "c16": _sb(240),
+    "rime": _sb(16, U16), "krim": _sb(16, BF), "slist": _sb(48, U16), "glist": _sb(16, U16),
+    "mn": _sb(240), "ncn": _sb(64), "inl": _sb(64, BF), "x1": _sb(64), "x2": _sb(64), "pos": _sb(64, U16),
+    "CW": _sb(1216), "CX": _sb(1216), "sc": _sb(512), "el": _sb(16, U16), "nl": _sb(64, U16), "mo": _sb(256, U16),
+    "dyn": _sb(256, BF), "sta": _sb(256, BF), "qe": _sb(512), "sm": _sb(512), "fb": _sb(256, BF),
+    "qn": _sb(2048), "ue": _sb(1024), "un": _sb(1024), "ie": _sb(1024), "inn": _sb(1024), "mm": _sb(1024), "oo": _sb(1024),
+    "qa": _sb(1024), "ab": _sb(256), "bits": _sb(256, BF), "nm": _sb(256, BF), "inv": _sb(512), "dq": _sb(256),
+    "sa": _sb(192 * 7, BF), "la": _sb(192 * 7, BF), "sb": _sb(384 * 6), "lb": _sb(384 * 6), "sg": _sb(192 * 7), "lg": _sb(192 * 7),
+    "MM": _sb(3840), "ymo": _sb(V), "yto": _sb(V), "ml": _sb(240, U16),
+}
+NDMA = 16
+SEMAPHORES = (["cV", "cA", "cP", "cG"] + ["d%d" % i for i in range(NDMA)]
+              + ["%s%d" % (s, r) for s in ("ra", "rb", "rg", "ta", "tb", "tg") for r in range(RO + 1)])
+PSUM = ("PD", "PN", "PF", "P6", "P7")
+
+
+def _builder(g, T):
+    ops, acc, bank = [], {}, {}
+    queue = {"V": g.vector, "A": g.scalar, "P": g.tensor, "G": g, "S": g.sync}
+    ndma = [0]
+
+    def add(eng, fn, reads, writes, sem=None):
+        me = len(ops)
+        deps = set()
+        for lst, wr in ((reads, False), (writes, True)):
+            for x in lst:
+                name, lo, hi = x[0], x[1], x[2]
+                st = x[3] if len(x) > 3 else 1
+                for (l2, h2, w2, o2, s2) in acc.get(name, ()):
+                    if l2 < hi and lo < h2 and (wr or w2):
+                        if eng == "P" and ops[o2][0] == "P":
+                            continue
+                        if st > 1 and s2 == st and (lo - l2) % st != 0 and ops[o2][0] == eng:
+                            continue
+                        deps.add(o2)
+                if name in PSUM:
+                    for b in range(lo // 512, (hi - 1) // 512 + 1):
+                        d = bank.setdefault((name, b), {})
+                        for e2 in d:
+                            if e2 != eng:
+                                deps.add(d[e2])
+                        d[eng] = me
+        for lst, wr in ((reads, False), (writes, True)):
+            for y in lst:
+                name, lo, hi = y[0], y[1], y[2]
+                st = y[3] if len(y) > 3 else 1
+                a = acc.setdefault(name, [])
+                if wr and st == 1:
+                    a[:] = [x for x in a if not (lo <= x[0] and x[1] <= hi)]
+                a.append((lo, hi, wr, me, st))
+        ops.append((eng, fn, deps, sem))
+        return me
+
+    def dma(eng, out, in_, reads, writes):
+        name = "d%d" % ndma[0]
+        ndma[0] += 1
+        return add(eng, lambda: queue[eng].dma_start(out, in_).then_inc(T.sem[name], 16), reads, writes, (name, 16))
+
+    def emit():
+        need, upto = set(), {}
+        for i, (eng, fn, deps, sem) in enumerate(ops):
+            last, keep = {}, set()
+            for d in deps:
+                if ops[d][3] is None:
+                    last[ops[d][0]] = max(last.get(ops[d][0], -1), d)
+                else:
+                    keep.add(d)
+            for e in last:
+                if upto.get((eng, e), -1) < last[e]:
+                    upto[(eng, e)] = last[e]
+                    keep.add(last[e])
+            ops[i] = (eng, fn, keep if eng != "X" else set(), sem)
+            need |= ops[i][2]
+        cnt = {"V": 0, "A": 0, "P": 0, "G": 0}
+        token, seen, final = {}, {}, {}
+        for i, (eng, fn, deps, sem) in enumerate(ops):
+            if eng != "X":
+                want = {}
+                for d in deps:
+                    s, v = token[d]
+                    want[s] = max(want.get(s, 0), v)
+                for s in sorted(want):
+                    if seen.get((eng, s), 0) < want[s]:
+                        queue[eng].wait_ge(T.sem[s], want[s])
+                        seen[(eng, s)] = want[s]
+            if sem is not None:
+                if fn is not None:
+                    fn()
+                token[i] = sem
+                final[sem[0]] = sem[1]
+            else:
+                ins = fn()
+                if i in need:
+                    cnt[eng] += 1
+                    ins.then_inc(T.sem["c" + eng], 1)
+                    token[i] = ("c" + eng, cnt[eng])
+                    final["c" + eng] = cnt[eng]
+        for s in sorted(final):
+            if max([seen.get((e, s), 0) for e in queue]) < final[s]:
+                g.wait_ge(T.sem[s], final[s])
+
+    return add, dma, emit
+
+
+def rank_program(g, core, T, topo):
+    rank = T.rank_of(core)
+    if rank is None:
+        return
+    N = len(T.cores)
+    add, dma, emit = _builder(g, T)
+
+    def a(name, lo=0, hi=None, step=1):
+        if hi is None:
+            hi = T[name].shape[1]
+        if step == 1:
+            return (T[name][:, lo:hi], (name, lo, hi))
+        last = lo + (hi - lo - 1) // step * step
+        return (T[name][:, lo:last + 1:step], (name, lo, last + 1, step))
+
+    def ind(win, off):
+        return (win[0].indirect(off[0]), win[1], off[1])
+
+    def rd(*xs):
+        out = []
+        for x in xs:
+            if isinstance(x, tuple):
+                out += list(x[1:])
+        return out
+
+    def val(x):
+        return x[0] if isinstance(x, tuple) else x
+
+    def io(out, *ins):
+        if len(out) == 3:
+            return rd(*ins) + [out[1], out[2]], [out[1]]
+        return rd(*ins), [out[1]]
+
+    def cp(out, in_, extra=()):
+        r, w = io(out, in_)
+        add("V", lambda: g.vector.tensor_copy(out[0], in_[0]), r + list(extra), w)
+
+    def tt(out, x, y, op):
+        r, w = io(out, x, y)
+        add("V", lambda: g.vector.tensor_tensor(out[0], x[0], y[0], op), r, w)
+
+    def ts(out, x, s1, op0, s2=None, op1=None):
+        r, w = io(out, x, s1, s2)
+        if op1 is None:
+            add("V", lambda: g.vector.tensor_scalar(out[0], x[0], val(s1), None, op0), r, w)
+        else:
+            add("V", lambda: g.vector.tensor_scalar(out[0], x[0], val(s1), val(s2), op0, op1), r, w)
+
+    def scan(out, d0, d1, op0, op1):
+        r, w = io(out, d0, d1)
+        add("V", lambda: g.vector.tensor_tensor_scan(out[0], d0[0], d1[0], 0.0, op0, op1), r, w)
+
+    def ms(out, c):
+        add("V", lambda: g.vector.memset(out[0], c), [], [out[1]])
+
+    def act(out, in_, func=AF.Copy, bias=None, scale=None):
+        r, w = io(out, in_, bias, scale)
+        kw = {}
+        if bias is not None:
+            kw["bias"] = val(bias)
+        if scale is not None:
+            kw["scale"] = val(scale)
+        add("A", lambda: g.scalar.activation(out[0], in_[0], func, **kw), r, w)
+
+    def take(eng, out, in_):
+        if eng == "V":
+            cp(out, in_)
+        else:
+            act(out, in_)
+
+    def mm(out, lhsT, rhs, start=True, stop=True):
+        add("P", lambda: g.tensor.matmul(out[0], lhsT[0], rhs[0], start, stop), rd(lhsT, rhs), [out[1]])
+
+    def group(out, terms):
+        for i, (l, r) in enumerate(terms):
+            mm(out, l, r, i == 0, i == len(terms) - 1)
+
+    def iota(out, pattern, base, cm, small=True):
+        if small:
+            add("G", lambda: g.iota(out[0], pattern, base, cm, allow_small_or_imprecise_dtypes=True), [], [out[1]])
+        else:
+            add("G", lambda: g.iota(out[0], pattern, base, cm), [], [out[1]])
+
+    ADD, SUB, MUL, MAX, MIN = ALU.add, ALU.subtract, ALU.mult, ALU.max, ALU.min
+    EQ, GT, LE, LT = ALU.is_equal, ALU.is_gt, ALU.is_le, ALU.is_lt
+    SHR, AND = ALU.arith_shift_right, ALU.bitwise_and
+
+    def split(src):
+        peers = [(src + d) % N for d in range(1, N)]
+        eng = [e for e in topo.engines(T.cores[src], T.cores[peers[0]])
+               if all([e in topo.engines(T.cores[src], T.cores[p]) for p in peers])]
+        q = len(eng) // 4
+        parts = [eng[0:q], eng[q:3 * q], eng[3 * q:4 * q]]
+        return {p: parts[i] for i, p in enumerate(peers)}
+
+    def send(kind, r, width, c0, c1):
+        sbuf, lbuf = "s" + kind, "l" + kind
+        base = r * 3 * width
+        mine = split(rank)
+        trs, n = [], 0
+        for d in range(1, N):
+            p = (rank + d) % N
+            rid, pid, _ = topo.addr(T.cores[p])
+            mask = 0
+            for e in mine[p]:
+                mask |= 1 << e
+            n += len(mine[p])
+            so = base + (d - 1) * width
+            do = base + (N - d - 1) * width
+            trs.append(RemoteDMATransfer(dst_ids=[DstId(rid=rid, pnc=pid)], dma_engine_mask=mask,
+                                         remote_sem=T.sem["r%s%d" % (kind, r)],
+                                         src=T[sbuf][:, so + c0:so + c1], dst=T[lbuf][:, do + c0:do + c1]))
+        ls = "t%s%d" % (kind, r)
+        add("G", lambda: g.remote_dma_fused(trs, local_sem=T.sem[ls]), [(sbuf, base, base + 3 * width)], [], (ls, n))
+        got = sum([len(split(s)[rank]) for s in range(N) if s != rank])
+        add("X", None, [], [(lbuf, base, base + 3 * width)], ("r%s%d" % (kind, r), got))
+
+    def shift(name, d):
+        return a(name, 16, 144) if rank < (rank + d) % N else a(name, 112, 240)
+
+    col = {}
+
+    def c(name):
+        if name not in col:
+            col[name] = len(col)
+        return a("cc", col[name], col[name] + 1)
+
+    mat = {}
+
+    def m(name, lo=0, n=144):
+        if name not in mat:
+            mat[name] = len(mat)
+        return a("MT", mat[name] * 144 + lo, mat[name] * 144 + lo + n)
+
+    def sl(name, lo=0):
+        return m(name, lo, 128)
+
+    def oh(j):
+        return a("OH", j, j + 1)
+
+    def oq(j):
+        return a("OQ", j, j + 1)
+
+    def weights(*chains):
+        for i in range(max([len(ch[2]) for ch in chains])):
+            for (name, first, terms) in chains:
+                if i < len(terms):
+                    act(c(name), terms[i][0], AF.Identity, first if i == 0 else c(name), float(terms[i][1]))
+
+    def scaled(out, base, w):
+        act(out, base, AF.Copy, None, w)
+
+    def take_meta(r):
+        for d in range(1, N):
+            o = 64 * (d - 1)
+            group(a("P7", o, o + 64), [(shift("JM", d), a("la", 192 * r + o, 192 * r + o + 64)),
+                                       (sl("NY"), a("yfor", o, o + 64))])
+        act(a("WM", V, V + FP), a("P7", 0, 192))
+
+    def take_data(r):
+        for f in range(2):
+            for d in range(1, N):
+                s = 384 * r + 128 * (d - 1) + 64 * f
+                mm(a("PN", 192 * f + 64 * (d - 1), 192 * f + 64 * d), shift("J2", d), a("lb", s, s + 64))
+
+    def put_data():
+        for f in range(2):
+            act(a("QL", W * f + V, W * f + V + FP), a("PN", 192 * f, 192 * f + 192))
+
+    def take_gifts(r, P="P7"):
+        for d in range(1, N):
+            s = 192 * r + 64 * (d - 1)
+            mm(a(P, 64 * (d - 1), 64 * d), shift("J2", d), a("lg", s, s + 64))
+
+    def put_gifts(r, P="P7"):
+        act(a("QL", LOG + R * r + 512, LOG + R * r + 704), a(P, 0, 192))
+
+    def chunk(eng, j):
+        take(eng, a("GG", 480 * j, 480 * j + 480), ind(a("WM"), a("colw", 30 * j, 30 * j + 30)))
+
+    def zterm(j, start, stop):
+        for i in (2 * j, 2 * j + 1):
+            mm(a("P6", 0, 240), sl("E", 15 - i), a("GG", 240 * i, 240 * i + 240), start and i == 2 * j, stop and i > 2 * j)
+
+    def lterm(j):
+        o = 512 * (j // 4) + 120 * (j % 4)
+        group(a("PF", o, o + 120), [(sl("LK", 3 - k), a("GG", 480 * j + k, 480 * j + 480, 4)) for k in range(4)]
+              + [(sl("LO"), a("WM", 120 * j, 120 * j + 120))])
+
+    def quad(out, terms):
+        group(out, [(sl(nme, 12 - 4 * j), a(src, j, 256, 4)) for (nme, src) in terms for j in range(4)])
+
+    def spread(dst, h, f):
+        for i in range(16):
+            mm(a(dst, 512 * h + i, 512 * h + 512, 16), a("BI", 128 * i, 128 * i + 128),
+               a("fb", 64 * f + 32 * h, 64 * f + 32 * h + 32))
+
+    TIT = [("TI1", 0, 1), ("TI2", 0, 1)]
+    add("V", lambda: g.vector.memset(T.TI[:], 0), [], [("TI", 0, V)] + TIT)
+    dma("S", T.rm[:, 0:12], T.rim[:], [], [("rm", 0, 12)])
+    dma("S", T.pt[:], T.port[:], [], [("pt", 0, 240)])
+    dma("S", T.TI[0:128:16, :], T.t0[:], [], [("TI", 0, V)])
+    dma("A", T.TI[1:128:16, :], T.d0[:], [], [TIT[0]])
+    dma("S", T.TI[2:128:16, :], T.d0[:], [], [TIT[1]])
+    dma("S", T.thr[:, 0:1], T.th[:], [], [("thr", 0, 1)])
+    iota(a("pc", 0, 1), [[0, 1]], 0, 1, False)
+    iota(a("rowj"), [[1, 256]], 0, 0)
+    dma("G", T.QL[:, 0:V], T.q0[:], [], [("QL", 0, V)])
+    dma("G", T.QL[:, W:W + V], T.q1[:], [], [("QL", W, W + V)])
+    iota(a("yfor"), [[1, 48], [0, 4]], 128, 0)
+    iota(a("QL", V, W), [[0, W - V]], 0, 0)
+    ts(a("pc", 1, 2), a("pc", 0, 1), 15, AND)
+    ts(a("pc", 2, 3), a("pc", 0, 1), 3, AND)
+    ts(a("pc", 3, 4), a("pc", 0, 1), 12, AND)
+    for nme in ("p", "lane", "k", "q4"):
+        c(nme)
+    cp(a("cc", 0, 4), a("pc", 0, 4))
+    ms(a("WM", V, W), 0.0)
+    ts(a("OH"), a("rowj", 0, 16), c("lane"), EQ)
+    ts(a("OQ"), a("rowj", 0, 16, 4), c("q4"), EQ)
+    ts(a("QP"), a("rowj"), c("p"), SUB)
+    ts(c("k12"), c("k"), 12.0, ADD)
+    weights(("ia", -1.0, [(oh(0), 2)]), ("ib", 0.0, [(oh(1), 7), (oh(2), 10)]),
+            ("lo", 0.0, [(oh(1), 4), (oh(2), 8), (oh(3), 1), (oh(8), -128)]),
+            ("hi", 0.0, [(oh(0), 99), (oh(1), 5), (oh(2), 9), (oh(3), 1), (oh(8), 200)]),
+            ("n8", 1.0, [(oh(8), -1)]), ("wd", 0.0, [(oh(1), -2), (oh(2), -1), (oh(3), 20)]),
+            ("wA", 0.0, [(oh(4), R), (oh(8), 4)]), ("wL", 0.0, [(oh(0), -1), (oh(4), 1), (oh(8), 1)]))
+    weights(("wb", c("wd"), [(oh(0), 1)]), ("l3", 3.0, [(c("lane"), 1)]), ("l60", 1216.0, [(c("lane"), -60)]))
+    ts(a("QG"), a("QP"), c("lane"), ADD)
+    ts(a("J2", 0, 128), a("QP", 0, 128), 0.0, EQ)
+    ts(a("J2", 128, 256), a("QP", 0, 128), 0.0, EQ)
+    ts(a("i4", 0, 12), a("rm", 0, 12), 2, SHR)
+    ts(m("C15"), a("QG", 0, 144), 15.0, EQ)
+    cp(a("rime", 0, 12), a("i4", 0, 12))
+    ts(m("P4"), a("QG", 0, 144), c("k12"), EQ)
+    ts(a("lohi", 0, 7), a("rowj", 0, 7), oh(4), MUL, c("lo"), ADD)
+    ts(a("lohi", 8, 15), a("rowj", 0, 7), oh(4), MUL, c("hi"), ADD)
+    ts(m("NY"), a("QG", 0, 144), 8.0, EQ, oh(0), MUL)
+    cp(a("f2", 0, 192), ind(a("TI"), a("rime", 0, 12)), TIT)
+    ts(a("i1"), a("pt"), 2, SHR)
+    ts(a("b1", 0, 192), a("f2", 0, 192), c("ia"), MUL, c("ib"), ADD)
+    ts(a("i2"), a("pt"), -2880.0, ADD)
+    ts(a("sa", 0, 192), a("b1", 0, 192), a("lohi", 0, 1), MAX, a("lohi", 8, 9), MIN)
+    send("a", 0, 64, 0, 64)
+    for d in range(3):
+        cp(a("slist", 8 * d, 8 * d + 4), a("i4", 4 * d, 4 * d + 4))
+        ts(a("slist", 8 * d + 4, 8 * d + 8), a("i4", 4 * d, 4 * d + 4), float(W), ADD)
+    scaled(a("JM"), a("J2"), c("n8"))
+    scaled(m("E"), m("C15"), c("wb"))
+    for j in range(4):
+        scaled(m("T%d" % j), m("P4"), oq(j))
+    act(a("c16"), a("rowj", 0, 240), AF.Identity, c("lane"), 16.0)
+    act(a("sb", 0, 384), ind(a("QL", 0, W + V), a("slist", 0, 24)))
+    iota(a("j16"), [[0, 16], [1, 16]], 0, 0)
+    send("b", 0, 128, 0, 128)
+    iota(a("eperm"), [[1, 60], [60, 16]], 64, 0)
+    iota(a("QL", W + V, LOG + 704), [[0, LOG + 704 - W - V]], 0, 0)
+    tt(a("i1"), a("i1"), a("i2"), MAX)
+    ts(a("b1"), a("pt"), float(4 * V + B * (N - 1 - rank)), LT, 4.0, MUL)
+    tt(a("b2"), a("pt"), a("c16"), GT)
+    cp(a("FW", 0, 240), a("i1"))
+    tt(a("b1"), a("b1"), a("b2"), MUL)
+    ts(a("i3"), a("pt"), 3, AND)
+    ts(a("FW", 480, 720), a("b1"), -2.0, ADD)
+    tt(a("FW", 240, 480), a("i1"), a("FW", 0, 240), SUB)
+    ts(a("FW", 720, 960), a("i3"), c("k"), SUB)
+    for h in range(2):
+        for j in range(4):
+            group(a("PD", 512 * h + j, 512 * h + 480, 4),
+                  [(sl("T%d" % j, 12 - 4 * f), a("FW", 240 * f + 120 * h, 240 * f + 120 * h + 120)) for f in range(4)])
+    ts(a("TB"), a("TI"), c("ia"), MUL, c("ib"), ADD)
+    cp(a("colw"), a("i1"))
+    ts(a("WM", 0, V), a("TB"), a("lohi", 0, 1), MAX, a("lohi", 8, 9), MIN)
+    cp(a("SW", 0, 480), a("PD", 0, 480))
+    ts(m("x"), a("QG", 0, 144), 15.5, LT)
+    ts(sl("BD"), a("QG", 0, 128), -0.5, GT)
+    cp(a("SW", 480, 960), a("PD", 512, 992))
+    ts(m("Q"), a("QG", 0, 144), 11.5, GT)
+    tt(sl("BD"), sl("BD"), sl("x"), MUL)
+    tt(m("Q"), m("Q"), m("x"), MUL)
+    for i in range(16):
+        bi = a("BI", 128 * i, 128 * i + 128)
+        add("G", lambda bi=bi, i=i: g.affine_select(bi[0], sl("BD")[0], [[-16, 8], [0, 16]], EQ, 0.0, -i, 1),
+            rd(sl("BD")), [bi[1]])
+    weights(("wzd", oq(0), [(oh(12), -1)]), ("wdl", oq(1), [(oh(13), -1)]), ("wnd", oh(13), [(oq(1), -1)]),
+            ("wan", 0.0, [(oq(1), R), (oq(2), 4)]), ("wae", 0.0, [(oh(13), R), (oh(14), 4)]),
+            ("wnl", oq(0), [(oq(1), 1)]), ("whd", 0.0, [(oh(12), -0.5)]))
+    for k in range(4):
+        scaled(m("K%d" % k), m("C15"), oh(8 + k))
+    act(a("dum"), a("rowj"), AF.Silu, 1216.0)
+    take_meta(0)
+    group(a("P6", 240, 300), [(sl("E", 15 - i), a("WM", 60 * i, 60 * i + 60)) for i in range(16)])
+    for k in range(4):
+        group(a("PN", k, 240, 4), [(sl("K%d" % k, 15 - i), a("SW", 60 * i, 60 * i + 60)) for i in range(16)])
+    ts(m("y"), m("Q"), oq(3), MUL)
+    cp(m("I", 0, 128), a("J2", 0, 128))
+    tt(m("U"), m("P4"), m("y"), MAX)
+    ms(a("R4"), 0.0)
+    ms(a("ones"), 1.0)
+    ts(sl("TR"), a("QG", 0, 128), c("lane"), GT)
+    ms(a("R4", 0, 240, 4), 1000.0)
+    ts(m("LK"), a("QG", 0, 144), c("l3"), EQ, c("wL"), MUL)
+    tt(sl("TR"), sl("TR"), sl("x"), MUL)
+    ms(sl("LO"), 0.0)
+    ts(a("x1", 0, 8), a("QG", 0, 128, 16), 0.0, EQ)
+    for j, wv in ((0, "wb"), (1, "wb"), (2, "wb"), (3, "wb"), (15, "wb"), (12, "wd"), (13, 4), (14, 8)):
+        lo = mat["LO"] * 144
+        ts(a("MT", lo + j, lo + 128, 16), a("x1", 0, 8), c(wv) if isinstance(wv, str) else oh(wv), MUL)
+    ts(a("R16"), a("j16"), c("lane"), EQ, 1.0e6, MUL)
+    ms(a("SW", V, W), 0.0)
+    ms(a("LW", V, W), 0.0)
+    ts(a("dneg", 0, 60), a("rowj", 0, 60), -1.0, MUL, c("l60"), ADD)
+
+    def late_constants():
+        act(a("CW", 0, 256), a("dum"))
+        act(a("CX", 0, 256), a("dum"))
+        scaled(m("NL"), m("P4"), c("wnl"))
+        for nme, wv in (("Z", oq(0)), ("ZD", c("wzd")), ("DT", oh(12))):
+            scaled(m(nme), m("U"), wv)
+
+    def last_constants():
+        ts(sl("NC"), a("QG", 0, 128), 0.5, GT)
+        ts(sl("y"), a("QG", 0, 128), 2.5, LT)
+        ts(sl("NM"), a("QG", 0, 128), 0.0, EQ, oh(15), MUL)
+        tt(sl("NC"), sl("NC"), sl("y"), MUL)
+        ts(a("i4", 0, 12), a("rm", 0, 12), 3, AND)
+        ts(sl("DB"), sl("BD"), c("whd"), MUL)
+        ts(a("yrow"), a("rowj"), -128.0, ADD)
+        cp(a("krim", 0, 12), a("i4", 0, 12))
+
+    def second_constants():
+        for nme, wv in (("DL", c("wdl")), ("ND", c("wnd")), ("AN", c("wan")), ("AE", c("wae"))):
+            scaled(m(nme), m("U"), wv)
+        scaled(m("A"), m("C15"), c("wA"))
+
+    for r in range(1, RO + 1):
+        if r == 1:
+            plan = (("A", 0), ("A", 1), ("A", 2), ("A", 3), ("A", 4), ("A", 5), ("V", 7), ("A", 6))
+        else:
+            group(a("P6", 240, 300), [(sl("E", 15 - i), a("WM", 60 * i, 60 * i + 60)) for i in range(16)])
+            take_meta(r - 1)
+            plan = (("A", 0), ("V", 1), ("A", 2), ("V", 3), ("A", 4), ("V", 5), ("A", 6), ("V", 7))
+        todo = list(range(8))
+        for n, (e, j) in enumerate(plan):
+            chunk(e, j)
+            zterm(j, n == 0, n == 7)
+            if r > 1 and n in (1, 3, 5):
+                lterm(todo.pop(0))
+            if r == 1 and n == 4:
+                ts(a("leftb"), a("PN", 0, 240), 0.25, MUL)
+            if n == 5:
+                mm(a("P6", 0, 240), sl("I"), a("leftb"), False, False)
+        if r == 1:
+            late_constants()
+        scan(a("mn"), a("R4"), a("P6", 0, 240), MAX, MIN)
+        tt(a("ncn", 0, 60), a("mn", 3, 240, 4), a("P6", 240, 300), LE)
+        scan(a("inl", 0, 60), a("ones", 0, 60), a("ncn", 0, 60), ADD, SUB)
+        lterm(todo.pop(0))
+        if r > 1:
+            act(a("LW", 0, 480), a("PF", 0, 480))
+        mm(a("P7", 300, 301), sl("TR"), a("inl", 59, 60))
+        for j in todo:
+            lterm(j)
+        take_data(r - 1)
+        tt(a("x1", 0, 60), a("ncn", 0, 60), a("dneg", 0, 60), MUL)
+        tt(a("x2", 0, 60), a("x1", 0, 60), a("inl", 0, 60), ADD)
+        ts(a("pos", 0, 60), a("x2", 0, 60), a("P7", 300, 301), ADD, -1.0, ADD)
+        cp(ind(a("CW"), a("pos", 0, SPL)), a("eperm", 0, 16 * SPL))
+        act(ind(a("CX"), a("pos", SPL, 60)), a("eperm", 16 * SPL, V), AF.Silu)
+        for h in range(0 if r == 1 else 1, 2):
+            act(a("LW", 480 * h, 480 * h + 480), a("PF", 512 * h, 512 * h + 480))
+        scan(a("sc", 256, 512), a("R16"), a("CX", 0, 256), MAX, MIN)
+        scan(a("sc", 0, 256), a("R16"), a("CW", 0, 256), MAX, MIN)
+        tt(a("x1", 0, 16), a("sc", 15, 256, 16), a("sc", 271, 512, 16), MIN)
+        ts(a("el"), a("x1", 0, 16), -63.75, ADD)
+        el = a("el")
+        act(a("sta"), ind(a("SW"), el))
+        cp(a("dyn"), ind(a("LW"), el))
+        quad(a("P7", 0, 64), [("NL", "sta")])
+        quad(a("P6", 0, 64), [("Z", "dyn")])
+        quad(a("P6", 64, 128), [("ZD", "dyn")])
+        quad(a("P6", 128, 192), [("T2", "sta")])
+        quad(a("P6", 192, 256), [("DT", "dyn")])
+        cp(a("qe", 0, 256), ind(a("QL", 0, W), el))
+        cp(a("nl"), a("P7", 0, 64))
+        act(a("qe", 256, 512), ind(a("QL", W, 2 * W), el))
+        put_data()
+        if r > 1:
+            quad(a("P7", 0, 64), [("DL", "dyn")])
+            quad(a("P7", 64, 128), [("ND", "dyn")])
+            quad(a("P7", 128, 192), [("AN", "dyn"), ("T3", "sta")])
+            quad(a("P7", 192, 256), [("AE", "dyn")])
+        for h in range(2):
+            act(a("qn", 512 * h, 512 * h + 512), ind(a("QL", 0, W), a("nl", 32 * h, 32 * h + 32)))
+            act(a("qn", 1024 + 512 * h, 1536 + 512 * h), ind(a("QL", W, 2 * W), a("nl", 32 * h, 32 * h + 32)))
+        ts(a("sm", 0, 128), a("P6", 0, 128), 0.0, MAX, 0.5, MUL)
+        tt(a("sm", 128, 192), a("sm", 0, 64), a("sm", 64, 128), SUB)
+        tt(a("fb", 0, 64), a("sm", 128, 192), a("P6", 128, 192), MUL)
+        tt(a("sm", 192, 256), a("P6", 192, 256), a("sm", 128, 192), SUB)
+        tt(a("sm", 256, 320), a("P6", 0, 64), a("sm", 128, 192), SUB)
+        spread("PD", 0, 0)
+        tt(a("fb", 64, 128), a("sm", 192, 256), a("fb", 0, 64), MUL)
+        tt(a("fb", 128, 192), a("sm", 256, 320), a("fb", 0, 64), MUL)
+        ts(a("fb", 192, 256), a("P6", 128, 192), 0.25, MUL)
+        spread("PF", 0, 1)
+        spread("PD", 1, 0)
+        spread("PF", 1, 1)
+        spread("PN", 0, 2)
+        spread("PN", 1, 2)
+        if r > 1:
+            ts(a("sm", 320, 448), a("P7", 0, 128), 0.0, GT)
+            tt(a("sm", 0, 128), a("sm", 320, 448), a("P7", 128, 256), MUL)
+            ts(a("mo", 0, 128), a("sm", 0, 128), c("k"), ADD)
+        else:
+            last_constants()
+        if r > 1:
+            take_gifts(r - 1)
+        mm(a("P6", 256, 512), sl("NM"), a("dyn"), True, False)
+        mm(a("P6", 256, 512), sl("NY"), a("yrow"), False, False)
+        logw = a("QL", LOG, LOG + R * r - 512)
+        for h in range(2):
+            lo, hi = 512 * h, 512 * h + 512
+            for k in range(4):
+                tt(a("ue", lo + k, hi, 4), a("qe", 128 * h, 128 * h + 128), a("PD", lo + k, hi, 4), MUL)
+            for k in range(4):
+                tt(a("PF", lo + k, hi, 4), a("qe", 256 + 128 * h, 384 + 128 * h), a("PF", lo + k, hi, 4), MUL)
+            tt(a("ie", lo, hi), a("ue", lo, hi), a("PF", lo, hi), ADD)
+            act(a("ie", lo, hi), a("ie", lo, hi), AF.Relu, None, 0.03125)
+            act(a("ue", lo, hi), a("ie", lo, hi), AF.Square)
+        for h in range(2):
+            lo, hi = 512 * h, 512 * h + 512
+            tt(a("un", lo, hi), a("qn", lo, hi), a("PD", lo, hi), MUL)
+            tt(a("PN", lo, hi), a("qn", 1024 + lo, 1024 + hi), a("PN", lo, hi), MUL)
+            spread("PD", h, 3)
+            tt(a("inn", lo, hi), a("un", lo, hi), a("PN", lo, hi), ADD)
+            act(a("inn", lo, hi), a("inn", lo, hi), AF.Relu, None, -0.03125)
+            act(a("PN", lo, hi), a("inn", lo, hi), AF.Square)
+            if r > 1:
+                if h == 0:
+                    put_gifts(r - 1)
+                act(a("mm", lo, hi), ind(logw, a("mo", 32 * h, 32 * h + 32)))
+        for h in range(2):
+            lo, hi = 512 * h, 512 * h + 512
+            tt(a("un", lo, hi), a("ue", lo, hi), a("PN", lo, hi), ADD)
+            tt(a("PD", lo, hi), a("un", lo, hi), a("PD", lo, hi), MUL)
+            if r > 1:
+                tt(a("PF", lo, hi), a("mm", lo, hi), a("PD", lo, hi), SUB)
+        mm(a("P7", 256, 512), sl("DB"), a("dyn"))
+        if r > 1:
+            act(a("oo"), ind(logw, a("mo", 64, 128)))
+        else:
+            second_constants()
+        for k in range(4):
+            tt(a("qa", 256 * k, 256 * k + 256), a("qe", 0, 256) if k == 0 else a("qa", 256 * k - 256, 256 * k),
+               a("PF" if r > 1 else "PD", k, 1024, 4), ADD if r > 1 else SUB)
+        qnew = a("qa", 768, 1024)
+        act(a("ab"), qnew, AF.Abs)
+        tt(a("dq", 0, 128), a("qa", 768, 896), a("qe", 0, 128), SUB)
+        ts(a("bits"), a("ab"), a("thr", 0, 1), GT)
+        tt(a("dq", 128, 256), a("qa", 896, 1024), a("qe", 128, 256), SUB)
+        mm(a("P6", 256, 512), sl("NC"), a("bits"), False, True)
+        act(a("inv", 0, 256), a("P7", 256, 512), AF.Relu, 1.25)
+        act(a("inv", 256, 512), a("inv", 0, 256), AF.Identity, 0.25)
+        ts(a("nm"), a("P6", 256, 512), a("lohi", r, r + 1), MAX, a("lohi", 8 + r, 9 + r), MIN)
+        cp(ind(a("WM"), el), a("nm"))
+        new = a("QL", LOG + R * r - 512, LOG + R * r + 512)
+        if r == 1:
+            act(new, a("PD"))
+        act(a("sa", 192 * r, 192 * r + 192), ind(a("WM"), a("rime", 0, 12)))
+        send("a", r, 64, 0, 64)
+        group(a("P7", 192, 204), [(sl("I"), a("krim", 0, 12))]
+              + [(sl("A", 15 - i), a("sa", 192 * r + i, 192 * r + 192, 16)) for i in range(16)])
+        if r < RO:
+            cp(ind(a("QL", 0, W), el), qnew)
+            tt(ind(a("QL", W, 2 * W), el), a("dq"), a("inv", 256, 512), MUL)
+            act(a("CW", 0, 256), a("dum"))
+            act(a("CX", 0, 256), a("dum"))
+            act(a("sb", 384 * r, 384 * r + 384), ind(a("QL", 0, W + V), a("slist", 0, 24)))
+            send("b", r, 128, 0, 128)
+        if r > 1:
+            tt(new, a("oo"), a("PD"), ADD)
+        cp(a("glist", 0, 12), a("P7", 192, 204))
+        cp(a("sg", 192 * r, 192 * r + 192), ind(a("QL", LOG, LOG + R * r + 512), a("glist", 0, 12)))
+        send("g", r, 64, 0, 64)
+        if r == RO:
+            cp(ind(a("QL", 0, W), el), qnew)
+            tt(ind(a("QL", W, 2 * W), el), a("dq"), a("inv", 256, 512), MUL)
+        if r == 1:
+            scaled(m("QA"), m("Q"), c("wA"))
+            ts(sl("x"), a("QG", 0, 128), 0.0, EQ, oh(0), MUL)
+            ts(sl("YT"), a("QG", 0, 128), 1.0, EQ, c("wd"), MUL)
+            tt(sl("YT"), sl("YT"), sl("x"), ADD)
+
+    dma("S", T.y0[:], T.QL[:, 0:V], [("QL", 0, V)], [])
+    dma("S", T.y1[:], T.QL[:, W:W + V], [("QL", W, W + V)], [])
+    group(a("P6", 0, 240), [(sl("QA", 12 - 4 * j), a("WM", j, V, 4)) for j in range(4)])
+    act(a("f1"), a("P6", 0, 240))
+    for h in range(2):
+        mm(a("PF", 512 * h, 512 * h + 480), sl("YT"), a("WM", 480 * h, 480 * h + 480))
+        act(a("yto", 480 * h, 480 * h + 480), a("PF", 512 * h, 512 * h + 480))
+    take_meta(RO)
+    dma("S", T.yt[:, 0:V], T.yto[0:128:16, :], [("yto", 0, V)], [])
+    dma("S", T.yt[:, V:2 * V], T.yto[1:128:16, :], [("yto", 0, V)], [])
+    logw = a("QL", LOG, QLW)
+
+    def address(q):
+        P, lo, hi = ("P6", "P7")[q % 2], 60 * q, 60 * q + 60
+        group(a(P, 256, 316), [(sl("I"), a("FW", 720 + lo, 720 + hi))]
+              + [(sl("A", 15 - i), a("GG", 960 * q + i, 960 * q + 960, 16)) for i in range(16)])
+
+    def lists(q):
+        P, lo, hi = ("P6", "P7")[q % 2], 60 * q, 60 * q + 60
+        tt(a("f2", lo, hi), a(P, 256, 316), a("f1", lo, hi), GT)
+        tt(a("mn", lo, hi), a(P, 256, 316), a("f2", lo, hi), MUL)
+        ts(a("ml", lo, hi), a("mn", lo, hi), c("k"), ADD)
+
+    def fetch(eng, j):
+        take(eng, a("MM", 480 * j, 480 * j + 480), ind(logw, a("ml", 30 * j, 30 * j + 30)))
+
+    def total(q):
+        P = a("PD" if q < 2 else "PF", 512 * (q % 2), 512 * (q % 2) + 240)
+        o = 960 * q
+        tt(P, a("MM", o, o + 960, 4), a("MM", o + 1, o + 960, 4), ADD)
+        tt(P, a("MM", o + 2, o + 960, 4), P, ADD)
+        tt(a("ymo", 240 * q, 240 * q + 240), a("MM", o + 3, o + 960, 4), P, ADD)
+        dma("S", T.ym[:, 240 * q:240 * q + 240], T.ymo[:, 240 * q:240 * q + 240], [("ymo", 240 * q, 240 * q + 240)], [])
+
+    for q in range(4):
+        chunk("A", 2 * q)
+        chunk("V", 2 * q + 1)
+        address(q)
+        if q == 2:
+            take_gifts(RO, "PN")
+            put_gifts(RO, "PN")
+        if q > 0:
+            lists(q - 1)
+    fetch("A", 0)
+    fetch("A", 1)
+    lists(3)
+    fetch("V", 2)
+    fetch("A", 3)
+    total(0)
+    fetch("A", 4)
+    total(1)
+    fetch("A", 5)
+    fetch("V", 6)
+    fetch("A", 7)
+    total(2)
+    total(3)
+    emit()

@@ -7,6 +7,10 @@ R = 1216
 LOG = 2 * W
 QLW = LOG + R * RO + 704
 SPL = 32
+DQ = False
+CUT = 22
+TAIL = "x"
+ORDER = "ue0 v0 we0 v1 ue1 v2 ie0 gifts0 m0 re0 se0 we1 un0 ie1 re1 se1 wn0 un1 in0 rn0 sn0 wn1 in1 rn1 sn1 m1 pg0 s0 g0 s1 own0 g1 own1"
 F32, BF, I32, U16 = "float32", "bfloat16", "int32", "uint16"
 
 
@@ -17,8 +21,9 @@ def _sb(n, d=F32):
 SCRATCH = {
     "PD": ("psum", [128, 1024], F32), "PN": ("psum", [128, 1024], F32), "PF": ("psum", [128, 1024], F32),
     "P6": ("psum", [128, 512], F32), "P7": ("psum", [128, 512], F32),
-    "QL": _sb(QLW), "WM": _sb(W, BF), "LW": _sb(W, BF), "SW": _sb(W, BF), "GG": _sb(3840, BF),
-    "TI": _sb(V, I32), "TB": _sb(V, BF), "thr": _sb(8),
+    "QL": _sb(QLW), "WN": _sb(W + CAP, BF), "PR": _sb(V, BF), "PG": _sb(192, BF), "pm": _sb(64, BF), "cst": _sb(8, BF),
+    "erim": _sb(16), "rl": _sb(48), "alist": _sb(16, U16), "LW": _sb(W, BF), "SW": _sb(W, BF), "GG": _sb(3840, BF),
+    "TI": _sb(V, I32), "TB": _sb(V, BF), "qb": _sb(2 * V, BF), "thr": _sb(8),
     "pt": _sb(240, I32), "rm": _sb(16, I32), "i1": _sb(240, I32), "i2": _sb(240, I32), "i3": _sb(240, I32), "i4": _sb(16, I32),
     "f1": _sb(240), "f2": _sb(240), "b1": _sb(240, BF), "b2": _sb(240, BF), "FW": _sb(960, BF),
     "colw": _sb(240, U16), "leftb": _sb(240, BF),
@@ -31,11 +36,11 @@ SCRATCH = {
     "CW": _sb(1216), "CX": _sb(1216), "sc": _sb(512), "el": _sb(16, U16), "nl": _sb(64, U16), "mo": _sb(256, U16),
     "dyn": _sb(256, BF), "sta": _sb(256, BF), "qe": _sb(512), "sm": _sb(512), "fb": _sb(256, BF),
     "qn": _sb(2048), "ue": _sb(1024), "un": _sb(1024), "ie": _sb(1024), "inn": _sb(1024), "mm": _sb(1024), "oo": _sb(1024),
-    "qa": _sb(1024), "ab": _sb(256), "bits": _sb(256, BF), "nm": _sb(256, BF), "inv": _sb(512), "dq": _sb(256),
-    "sa": _sb(192 * 7, BF), "la": _sb(192 * 7, BF), "sb": _sb(384 * 6), "lb": _sb(384 * 6), "sg": _sb(192 * 7), "lg": _sb(192 * 7),
+    "qa": _sb(1024), "ab": _sb(256), "bits": _sb(512, BF), "inv": _sb(512), "dq": _sb(256),
+    "sa": _sb(192 * 7, BF), "la": _sb(576 * 7, BF), "sb": _sb(384 * 6), "lb": _sb(384 * 6), "sg": _sb(192 * 7), "lg": _sb(192 * 7),
     "MM": _sb(3840), "ymo": _sb(V), "yto": _sb(V), "ml": _sb(240, U16),
 }
-NDMA = 16
+NDMA = 20
 SEMAPHORES = (["cV", "cA", "cP", "cG"] + ["d%d" % i for i in range(NDMA)]
               + ["%s%d" % (s, r) for s in ("ra", "rb", "rg", "ta", "tb", "tg") for r in range(RO + 1)])
 PSUM = ("PD", "PN", "PF", "P6", "P7")
@@ -78,9 +83,11 @@ def _builder(g, T):
         ops.append((eng, fn, deps, sem))
         return me
 
-    def dma(eng, out, in_, reads, writes):
+    def dma(eng, out, in_, reads, writes, adding=False):
         name = "d%d" % ndma[0]
         ndma[0] += 1
+        if adding:
+            return add(eng, lambda: g.dma_start(out, in_, accum_op=ALU.add).then_inc(T.sem[name], 16), reads, writes, (name, 16))
         return add(eng, lambda: queue[eng].dma_start(out, in_).then_inc(T.sem[name], 16), reads, writes, (name, 16))
 
     def emit():
@@ -137,6 +144,8 @@ def rank_program(g, core, T, topo):
     add, dma, emit = _builder(g, T)
 
     def a(name, lo=0, hi=None, step=1):
+        if name == "WM":
+            name, lo, hi = "WN", lo + CAP, (W if hi is None else hi) + CAP
         if hi is None:
             hi = T[name].shape[1]
         if step == 1:
@@ -228,6 +237,24 @@ def rank_program(g, core, T, topo):
         sbuf, lbuf = "s" + kind, "l" + kind
         base = r * 3 * width
         mine = split(rank)
+        if kind == "a":
+            mask, n = 0, 0
+            for p in mine:
+                for e in mine[p]:
+                    mask |= 1 << e
+                    n += 1
+            ids, dsts = [], []
+            for d in range(1, N):
+                rid, pid, _ = topo.addr(T.cores[(rank + d) % N])
+                ids.append(DstId(rid=rid, pnc=pid))
+                do = 3 * base + (N - d - 1) * 192
+                dsts.append(T.la[:, do:do + 192])
+            tr = RemoteDMATransfer(dst_ids=ids, dma_engine_mask=mask, remote_sem=T.sem["ra%d" % r],
+                                   srcs=[T.sa[:, base:base + 192]], dsts=dsts)
+            add("G", lambda: g.remote_dma_fused([tr], local_sem=T.sem["ta%d" % r]), [("sa", base, base + 192)], [], ("ta%d" % r, n))
+            got = sum([sum([len(x) for x in split(s).values()]) for s in range(N) if s != rank])
+            add("X", None, [], [("la", 3 * base, 3 * base + 576)], ("ra%d" % r, got))
+            return
         trs, n = [], 0
         for d in range(1, N):
             p = (rank + d) % N
@@ -284,7 +311,8 @@ def rank_program(g, core, T, topo):
     def take_meta(r):
         for d in range(1, N):
             o = 64 * (d - 1)
-            group(a("P7", o, o + 64), [(shift("JM", d), a("la", 192 * r + o, 192 * r + o + 64)),
+            s = 576 * r + 192 * (d - 1) + 64 * (N - d - 1)
+            group(a("P7", o, o + 64), [(shift("JM", d), a("la", s, s + 64)),
                                        (sl("NY"), a("yfor", o, o + 64))])
         act(a("WM", V, V + FP), a("P7", 0, 192))
 
@@ -298,13 +326,17 @@ def rank_program(g, core, T, topo):
         for f in range(2):
             act(a("QL", W * f + V, W * f + V + FP), a("PN", 192 * f, 192 * f + 192))
 
-    def take_gifts(r, P="P7"):
+    def take_gifts(r, P="P6"):
         for d in range(1, N):
             s = 192 * r + 64 * (d - 1)
             mm(a(P, 64 * (d - 1), 64 * d), shift("J2", d), a("lg", s, s + 64))
 
-    def put_gifts(r, P="P7"):
+    def put_gifts(r, P="P6"):
         act(a("QL", LOG + R * r + 512, LOG + R * r + 704), a(P, 0, 192))
+
+    def give(eng, r):
+        take(eng, a("sg", 192 * r, 192 * r + 192), ind(a("QL", LOG, LOG + R * r + 512), a("glist", 0, 12)))
+        send("g", r, 64, 0, 64)
 
     def chunk(eng, j):
         take(eng, a("GG", 480 * j, 480 * j + 480), ind(a("WM"), a("colw", 30 * j, 30 * j + 30)))
@@ -336,8 +368,8 @@ def rank_program(g, core, T, topo):
     dma("S", T.thr[:, 0:1], T.th[:], [], [("thr", 0, 1)])
     iota(a("pc", 0, 1), [[0, 1]], 0, 1, False)
     iota(a("rowj"), [[1, 256]], 0, 0)
-    dma("G", T.QL[:, 0:V], T.q0[:], [], [("QL", 0, V)])
-    dma("G", T.QL[:, W:W + V], T.q1[:], [], [("QL", W, W + V)])
+    dma("S", T.qb[:, 0:V], T.q0[:], [], [("qb", 0, V)])
+    dma("S", T.qb[:, V:2 * V], T.q1[:], [], [("qb", V, 2 * V)])
     iota(a("yfor"), [[1, 48], [0, 4]], 128, 0)
     iota(a("QL", V, W), [[0, W - V]], 0, 0)
     ts(a("pc", 1, 2), a("pc", 0, 1), 15, AND)
@@ -381,6 +413,8 @@ def rank_program(g, core, T, topo):
     for j in range(4):
         scaled(m("T%d" % j), m("P4"), oq(j))
     act(a("c16"), a("rowj", 0, 240), AF.Identity, c("lane"), 16.0)
+    act(a("QL", 0, V), a("qb", 0, V))
+    act(a("QL", W, W + V), a("qb", V, 2 * V))
     act(a("sb", 0, 384), ind(a("QL", 0, W + V), a("slist", 0, 24)))
     iota(a("j16"), [[0, 16], [1, 16]], 0, 0)
     send("b", 0, 128, 0, 128)
@@ -428,6 +462,8 @@ def rank_program(g, core, T, topo):
     tt(m("U"), m("P4"), m("y"), MAX)
     ms(a("R4"), 0.0)
     ms(a("ones"), 1.0)
+    ms(a("cst"), -129.0)
+    cp(a("erim", 0, 12), a("i4", 0, 12))
     ts(sl("TR"), a("QG", 0, 128), c("lane"), GT)
     ms(a("R4", 0, 240, 4), 1000.0)
     ts(m("LK"), a("QG", 0, 144), c("l3"), EQ, c("wL"), MUL)
@@ -456,6 +492,7 @@ def rank_program(g, core, T, topo):
         tt(sl("NC"), sl("NC"), sl("y"), MUL)
         ts(a("i4", 0, 12), a("rm", 0, 12), 3, AND)
         ts(sl("DB"), sl("BD"), c("whd"), MUL)
+        ts(c("nth"), a("thr", 0, 1), -1.0, MUL)
         ts(a("yrow"), a("rowj"), -128.0, ADD)
         cp(a("krim", 0, 12), a("i4", 0, 12))
 
@@ -470,12 +507,16 @@ def rank_program(g, core, T, topo):
         else:
             group(a("P6", 240, 300), [(sl("E", 15 - i), a("WM", 60 * i, 60 * i + 60)) for i in range(16)])
             take_meta(r - 1)
-            plan = (("A", 0), ("V", 1), ("A", 2), ("V", 3), ("A", 4), ("V", 5), ("A", 6), ("V", 7))
+            plan = (("A", 0), ("A", 1), ("V", 4), ("A", 2), ("V", 5), ("A", 3), ("V", 6), ("V", 7))
         todo = list(range(8))
         for n, (e, j) in enumerate(plan):
-            chunk(e, j)
+            if r > 1 and n == 7:
+                act(a("GG", 3360, 3360 + 16 * CUT), ind(a("WM"), a("colw", 210, 210 + CUT)))
+                cp(a("GG", 3360 + 16 * CUT, 3840), ind(a("WM"), a("colw", 210 + CUT, 240)))
+            else:
+                chunk(e, j)
             zterm(j, n == 0, n == 7)
-            if r > 1 and n in (1, 3, 5):
+            if r > 1 and n in (0, 1, 3):
                 lterm(todo.pop(0))
             if r == 1 and n == 4:
                 ts(a("leftb"), a("PN", 0, 240), 0.25, MUL)
@@ -483,23 +524,31 @@ def rank_program(g, core, T, topo):
                 mm(a("P6", 0, 240), sl("I"), a("leftb"), False, False)
         if r == 1:
             late_constants()
+        else:
+            give("A", r - 1)
         scan(a("mn"), a("R4"), a("P6", 0, 240), MAX, MIN)
         tt(a("ncn", 0, 60), a("mn", 3, 240, 4), a("P6", 240, 300), LE)
         scan(a("inl", 0, 60), a("ones", 0, 60), a("ncn", 0, 60), ADD, SUB)
         lterm(todo.pop(0))
         if r > 1:
             act(a("LW", 0, 480), a("PF", 0, 480))
-        mm(a("P7", 300, 301), sl("TR"), a("inl", 59, 60))
+        group(a("P7", 300, 301), [(sl("I"), a("cst", 0, 1)), (sl("TR"), a("inl", 59, 60))])
         for j in todo:
             lterm(j)
-        take_data(r - 1)
         tt(a("x1", 0, 60), a("ncn", 0, 60), a("dneg", 0, 60), MUL)
         tt(a("x2", 0, 60), a("x1", 0, 60), a("inl", 0, 60), ADD)
-        ts(a("pos", 0, 60), a("x2", 0, 60), a("P7", 300, 301), ADD, -1.0, ADD)
+        ts(a("pos", 0, 60), a("x2", 0, 60), a("P7", 300, 301), ADD, 128.0, ADD)
+        ts(a("pm", 0, 60), a("x2", 0, 60), a("P7", 300, 301), ADD, 128.0, MIN)
+        for i in range(16):
+            o = 512 * (i // 8) + 60 * (i % 8)
+            mm(a("PD", o, o + 60), a("BI", 128 * i, 128 * i + 128), a("pm", 0, 60))
+        take_data(r - 1)
         cp(ind(a("CW"), a("pos", 0, SPL)), a("eperm", 0, 16 * SPL))
         act(ind(a("CX"), a("pos", SPL, 60)), a("eperm", 16 * SPL, V), AF.Silu)
         for h in range(0 if r == 1 else 1, 2):
             act(a("LW", 480 * h, 480 * h + 480), a("PF", 512 * h, 512 * h + 480))
+        for h in range(2):
+            act(a("PR", 480 * h, 480 * h + 480), a("PD", 512 * h, 512 * h + 480))
         scan(a("sc", 256, 512), a("R16"), a("CX", 0, 256), MAX, MIN)
         scan(a("sc", 0, 256), a("R16"), a("CW", 0, 256), MAX, MIN)
         tt(a("x1", 0, 16), a("sc", 15, 256, 16), a("sc", 271, 512, 16), MIN)
@@ -536,84 +585,126 @@ def rank_program(g, core, T, topo):
         spread("PF", 0, 1)
         spread("PD", 1, 0)
         spread("PF", 1, 1)
-        spread("PN", 0, 2)
-        spread("PN", 1, 2)
-        if r > 1:
-            ts(a("sm", 320, 448), a("P7", 0, 128), 0.0, GT)
-            tt(a("sm", 0, 128), a("sm", 320, 448), a("P7", 128, 256), MUL)
-            ts(a("mo", 0, 128), a("sm", 0, 128), c("k"), ADD)
-        else:
-            last_constants()
         if r > 1:
             take_gifts(r - 1)
+        spread("PN", 0, 2)
+        spread("PN", 1, 2)
+        if r == 1:
+            last_constants()
+        logw = a("QL", LOG, LOG + R * r - 512)
+        def hf(name, h, o=0):
+            return a(name, o + 512 * h, o + 512 * h + 512)
+
+        def step(name, h):
+            lo, hi = 512 * h, 512 * h + 512
+            if name == "ue":
+                for k in range(4):
+                    tt(a("ue", lo + k, hi, 4), a("qe", 128 * h, 128 * h + 128), a("PD", lo + k, hi, 4), MUL)
+            elif name == "we":
+                for k in range(4):
+                    tt(a("PF", lo + k, hi, 4), a("qe", 256 + 128 * h, 384 + 128 * h), a("PF", lo + k, hi, 4), MUL)
+            elif name == "ie":
+                tt(hf("ie", h), hf("ue", h), hf("PF", h), ADD)
+            elif name == "re":
+                act(hf("ie", h), hf("ie", h), AF.Relu, None, 0.03125)
+            elif name == "se":
+                act(hf("ue", h), hf("ie", h), AF.Square)
+            elif name == "un":
+                tt(hf("un", h), hf("qn", h), hf("PD", h), MUL)
+                spread("PD", h, 3)
+            elif name == "wn":
+                tt(hf("PN", h), hf("qn", h, 1024), hf("PN", h), MUL)
+            elif name == "in":
+                tt(hf("inn", h), hf("un", h), hf("PN", h), ADD)
+            elif name == "rn":
+                act(hf("inn", h), hf("inn", h), AF.Relu, None, -0.03125)
+            elif name == "sn":
+                act(hf("PN", h), hf("inn", h), AF.Square)
+            elif name == "s":
+                tt(hf("un", h), hf("ue", h), hf("PN", h), ADD)
+            elif name == "g":
+                tt(hf("PD", h), hf("un", h), hf("PD", h), MUL)
+            elif name == "pg":
+                act(a("PG"), ind(a("PR"), a("rime", 0, 12)))
+                group(a("P7", 208, 220), [(sl("K0", 15 - i), a("PG", i, 192, 16)) for i in range(16)])
+            elif name == "l":
+                if h == 0:
+                    ts(a("rl", 0, 12), a("P7", 208, 220), 128.0, EQ)
+                elif h == 1:
+                    tt(a("rl", 16, 28), a("rl", 0, 12), a("erim", 0, 12), MUL)
+                elif h == 2:
+                    tt(a("rl", 32, 44), a("rl", 16, 28), a("P7", 208, 220), ADD)
+                else:
+                    ts(a("alist", 0, 12), a("rl", 32, 44), 128.0, ADD)
+            elif r == 1:
+                pass
+            elif name == "v":
+                if h == 0:
+                    ts(a("sm", 320, 448), a("P7", 0, 128), 0.0, GT)
+                elif h == 1:
+                    tt(a("sm", 0, 128), a("sm", 320, 448), a("P7", 128, 256), MUL)
+                else:
+                    ts(a("mo", 0, 128), a("sm", 0, 128), c("k"), ADD)
+            elif name == "gifts":
+                put_gifts(r - 1)
+            elif name == "m":
+                act(hf("mm", h), ind(logw, a("mo", 32 * h, 32 * h + 32)))
+            elif name == "own":
+                tt(hf("PF", h), hf("mm", h), hf("PD", h), SUB)
+
+        def chain(h, k):
+            o = 256 * k + 128 * h
+            tt(a("qa", o, o + 128), a("qe", 128 * h, 128 * h + 128) if k == 0 else a("qa", o - 256, o - 128),
+               a("PF" if r > 1 else "PD", 512 * h + k, 512 * h + 512, 4), ADD if r > 1 else SUB)
+
+        for x in ORDER.split():
+            step(x[:-1], int(x[-1]))
         mm(a("P6", 256, 512), sl("NM"), a("dyn"), True, False)
         mm(a("P6", 256, 512), sl("NY"), a("yrow"), False, False)
-        logw = a("QL", LOG, LOG + R * r - 512)
-        for h in range(2):
-            lo, hi = 512 * h, 512 * h + 512
-            for k in range(4):
-                tt(a("ue", lo + k, hi, 4), a("qe", 128 * h, 128 * h + 128), a("PD", lo + k, hi, 4), MUL)
-            for k in range(4):
-                tt(a("PF", lo + k, hi, 4), a("qe", 256 + 128 * h, 384 + 128 * h), a("PF", lo + k, hi, 4), MUL)
-            tt(a("ie", lo, hi), a("ue", lo, hi), a("PF", lo, hi), ADD)
-            act(a("ie", lo, hi), a("ie", lo, hi), AF.Relu, None, 0.03125)
-            act(a("ue", lo, hi), a("ie", lo, hi), AF.Square)
-        for h in range(2):
-            lo, hi = 512 * h, 512 * h + 512
-            tt(a("un", lo, hi), a("qn", lo, hi), a("PD", lo, hi), MUL)
-            tt(a("PN", lo, hi), a("qn", 1024 + lo, 1024 + hi), a("PN", lo, hi), MUL)
-            spread("PD", h, 3)
-            tt(a("inn", lo, hi), a("un", lo, hi), a("PN", lo, hi), ADD)
-            act(a("inn", lo, hi), a("inn", lo, hi), AF.Relu, None, -0.03125)
-            act(a("PN", lo, hi), a("inn", lo, hi), AF.Square)
-            if r > 1:
-                if h == 0:
-                    put_gifts(r - 1)
-                act(a("mm", lo, hi), ind(logw, a("mo", 32 * h, 32 * h + 32)))
-        for h in range(2):
-            lo, hi = 512 * h, 512 * h + 512
-            tt(a("un", lo, hi), a("ue", lo, hi), a("PN", lo, hi), ADD)
-            tt(a("PD", lo, hi), a("un", lo, hi), a("PD", lo, hi), MUL)
-            if r > 1:
-                tt(a("PF", lo, hi), a("mm", lo, hi), a("PD", lo, hi), SUB)
         mm(a("P7", 256, 512), sl("DB"), a("dyn"))
         if r > 1:
             act(a("oo"), ind(logw, a("mo", 64, 128)))
         else:
             second_constants()
         for k in range(4):
-            tt(a("qa", 256 * k, 256 * k + 256), a("qe", 0, 256) if k == 0 else a("qa", 256 * k - 256, 256 * k),
-               a("PF" if r > 1 else "PD", k, 1024, 4), ADD if r > 1 else SUB)
+            chain(0, k)
+            chain(1, k)
+            if TAIL:
+                step("l", k)
         qnew = a("qa", 768, 1024)
-        act(a("ab"), qnew, AF.Abs)
+        ts(a("bits", 0, 128), a("qa", 768, 896), a("thr", 0, 1), GT)
+        ts(a("bits", 128, 256), a("qa", 896, 1024), a("thr", 0, 1), GT)
+        ts(a("bits", 256, 512), qnew, c("nth"), LT)
+        mm(a("P6", 256, 512), sl("NC"), a("bits", 0, 256), False, False)
+        mm(a("P6", 256, 512), sl("NC"), a("bits", 256, 512), False, True)
         tt(a("dq", 0, 128), a("qa", 768, 896), a("qe", 0, 128), SUB)
-        ts(a("bits"), a("ab"), a("thr", 0, 1), GT)
-        tt(a("dq", 128, 256), a("qa", 896, 1024), a("qe", 128, 256), SUB)
-        mm(a("P6", 256, 512), sl("NC"), a("bits"), False, True)
         act(a("inv", 0, 256), a("P7", 256, 512), AF.Relu, 1.25)
         act(a("inv", 256, 512), a("inv", 0, 256), AF.Identity, 0.25)
-        ts(a("nm"), a("P6", 256, 512), a("lohi", r, r + 1), MAX, a("lohi", 8 + r, 9 + r), MIN)
-        cp(ind(a("WM"), el), a("nm"))
-        new = a("QL", LOG + R * r - 512, LOG + R * r + 512)
-        if r == 1:
-            act(new, a("PD"))
-        act(a("sa", 192 * r, 192 * r + 192), ind(a("WM"), a("rime", 0, 12)))
+        ts(a("WN", 0, CAP), a("P6", 256, 512), a("lohi", r, r + 1), MAX, a("lohi", 8 + r, 9 + r), MIN)
+        tt(a("dq", 128, 256), a("qa", 896, 1024), a("qe", 128, 256), SUB) if DQ else None
+        cp(a("sa", 192 * r, 192 * r + 192), ind(a("WN", 0, CAP + V), a("alist", 0, 12)))
         send("a", r, 64, 0, 64)
+        cp(ind(a("WM"), el), a("WN", 0, CAP))
+        tt(a("dq", 128, 256), a("qa", 896, 1024), a("qe", 128, 256), SUB) if not DQ else None
+        new = a("QL", LOG + R * r - 512, LOG + R * r + 512)
+        if r < RO:
+            act(new, a("PD"))
+        if 1 < r < RO:
+            dma("G", new[0], T.oo[:], [("oo", 0, 1024), new[1]], [new[1]], True)
         group(a("P7", 192, 204), [(sl("I"), a("krim", 0, 12))]
               + [(sl("A", 15 - i), a("sa", 192 * r + i, 192 * r + 192, 16)) for i in range(16)])
+        cp(a("glist", 0, 12), a("P7", 192, 204))
         if r < RO:
             cp(ind(a("QL", 0, W), el), qnew)
             tt(ind(a("QL", W, 2 * W), el), a("dq"), a("inv", 256, 512), MUL)
             act(a("CW", 0, 256), a("dum"))
             act(a("CX", 0, 256), a("dum"))
-            act(a("sb", 384 * r, 384 * r + 384), ind(a("QL", 0, W + V), a("slist", 0, 24)))
+            cp(a("sb", 384 * r, 384 * r + 384), ind(a("QL", 0, W + V), a("slist", 0, 24)))
             send("b", r, 128, 0, 128)
-        if r > 1:
+        else:
             tt(new, a("oo"), a("PD"), ADD)
-        cp(a("glist", 0, 12), a("P7", 192, 204))
-        cp(a("sg", 192 * r, 192 * r + 192), ind(a("QL", LOG, LOG + R * r + 512), a("glist", 0, 12)))
-        send("g", r, 64, 0, 64)
         if r == RO:
+            give("V", r)
             cp(ind(a("QL", 0, W), el), qnew)
             tt(ind(a("QL", W, 2 * W), el), a("dq"), a("inv", 256, 512), MUL)
         if r == 1:

@@ -3,14 +3,19 @@ from concourse.mybir import AluOpType as ALU, ActivationFunctionType as AF
 
 V, B, FP, CAP, RO = 960, 64, 192, 256, 6
 W = 1408
+S = CAP + W
 R = 1216
-LOG = 2 * W
+LOG = 2 * S
 QLW = LOG + R * RO + 704
 SPL = 32
-DQ = False
-CUT = 22
-TAIL = "x"
-ORDER = "ue0 v0 we0 v1 ue1 v2 ie0 gifts0 m0 re0 se0 we1 un0 ie1 re1 se1 wn0 un1 in0 rn0 sn0 wn1 in1 rn1 sn1 m1 pg0 s0 g0 s1 own0 g1 own1"
+CUT = 168
+QE1 = "V"
+EARLY = "q0 q1 z7 z0 l0 z6 z1 l1 z2 l2 l7 z3 d1 d0 g0 l3 z4 e1 z5 e0"
+LAST = "A0 own0 A1 new0 at0 A2 q0 A3 at1 q1 x0 A4 V5 gifts0 x1 y0 y1 z0 z1 at2 f0 g0 A6 A7 x2 f1 y2 g1 z2 at3 f2 x3 g2 y3 z3 clocks0 f3 g3"
+ORDER = ("pg0 ue0 fb0 qn0 we0 un0 wn0 in0 v0 ie0 ue1 v1 qn1 v2 early0 we1 rn0 gifts0 re0 un1 sn0 wn1 early1 se0 ie1 in1 m0 l0 re1 s0 rn1 "
+         "se1 l1 sn1 g0 m1 oo0 l2 own0 a0 l3 oo1 s1 b0 g1 c0 own1 clock0 d0 a1 hi0 b1 lo0 c1 by0 new0 dq0 d1 by1 hi1 lo1 meta0")
+FIRST = ("ue0 const0 put0 fb0 qn0 pg0 l0 we0 ie0 we1 qn1 ue1 early0 re0 wn0 un0 in0 wn1 hot0 ie1 un1 rn0 l1 early1 se0 re1 sn0 in1 l2 rn1 "
+         "se1 sn1 l3 s0 hot1 meta0 g0 a0 s1 clock0 b0 g1 c0 a1 d0 b1 hi0 c1 lo0 d1 dq0 hi1 lo1 new0")
 F32, BF, I32, U16 = "float32", "bfloat16", "int32", "uint16"
 
 
@@ -21,28 +26,33 @@ def _sb(n, d=F32):
 SCRATCH = {
     "PD": ("psum", [128, 1024], F32), "PN": ("psum", [128, 1024], F32), "PF": ("psum", [128, 1024], F32),
     "P6": ("psum", [128, 512], F32), "P7": ("psum", [128, 512], F32),
-    "QL": _sb(QLW), "WN": _sb(W + CAP, BF), "PR": _sb(V, BF), "PG": _sb(192, BF), "pm": _sb(64, BF), "cst": _sb(8, BF),
-    "erim": _sb(16), "rl": _sb(48), "alist": _sb(16, U16), "LW": _sb(W, BF), "SW": _sb(W, BF), "GG": _sb(3840, BF),
-    "TI": _sb(V, I32), "TB": _sb(V, BF), "qb": _sb(2 * V, BF), "thr": _sb(8),
+    "QL": _sb(QLW), "WM": _sb(W, BF), "PR": _sb(V, BF), "PG": _sb(192, BF), "pm": _sb(64, BF), "cst": _sb(8, BF),
+    "erim": _sb(32), "rl": _sb(32), "alist": _sb(16, U16), "LW": _sb(W, BF), "SW": _sb(W, BF), "GG": _sb(3840, BF),
+    "TI": _sb(V, I32), "qb": _sb(2 * V, BF), "thr": _sb(8),
     "pt": _sb(240, I32), "rm": _sb(16, I32), "i1": _sb(240, I32), "i2": _sb(240, I32), "i3": _sb(240, I32), "i4": _sb(16, I32),
     "f1": _sb(240), "f2": _sb(240), "b1": _sb(240, BF), "b2": _sb(240, BF), "FW": _sb(960, BF),
-    "colw": _sb(240, U16), "leftb": _sb(240, BF),
+    "colw": _sb(240, U16), "colk": _sb(240, U16), "leftb": _sb(240, BF),
     "pc": _sb(8, I32), "cc": _sb(64), "rowj": _sb(256), "j16": _sb(256), "QG": _sb(256), "QP": _sb(256), "OH": _sb(16), "OQ": _sb(4),
-    "lohi": _sb(16), "J2": _sb(256), "JM": _sb(256, BF), "MT": _sb(144 * 40, BF), "BI": _sb(2048, BF),
+    "lohi": _sb(24), "J2": _sb(256), "JM": _sb(384, BF), "MT": _sb(144 * 45, BF), "BI": _sb(2048, BF),
     "yrow": _sb(256, BF), "yfor": _sb(192, BF), "eperm": _sb(V), "dneg": _sb(64), "R16": _sb(256), "R4": _sb(240),
-    "ones": _sb(64), "dum": _sb(256), "c16": _sb(240),
+    "ones": _sb(128), "rows": _sb(432),
     "rime": _sb(16, U16), "krim": _sb(16, BF), "slist": _sb(48, U16), "glist": _sb(16, U16),
-    "mn": _sb(240), "ncn": _sb(64), "inl": _sb(64, BF), "x1": _sb(64), "x2": _sb(64), "pos": _sb(64, U16),
+    "mn": _sb(240), "can": _sb(64), "ncn": _sb(64), "inl": _sb(64, BF), "x1": _sb(64), "x2": _sb(64), "pos": _sb(64, U16),
     "CW": _sb(1216), "CX": _sb(1216), "sc": _sb(512), "el": _sb(16, U16), "nl": _sb(64, U16), "mo": _sb(256, U16),
-    "dyn": _sb(256, BF), "sta": _sb(256, BF), "qe": _sb(512), "sm": _sb(512), "fb": _sb(256, BF),
-    "qn": _sb(2048), "ue": _sb(1024), "un": _sb(1024), "ie": _sb(1024), "inn": _sb(1024), "mm": _sb(1024), "oo": _sb(1024),
-    "qa": _sb(1024), "ab": _sb(256), "bits": _sb(512, BF), "inv": _sb(512), "dq": _sb(256),
-    "sa": _sb(192 * 7, BF), "la": _sb(576 * 7, BF), "sb": _sb(384 * 6), "lb": _sb(384 * 6), "sg": _sb(192 * 7), "lg": _sb(192 * 7),
-    "MM": _sb(3840), "ymo": _sb(V), "yto": _sb(V), "ml": _sb(240, U16),
+    "dyn": _sb(256, BF), "sta": _sb(256, BF), "mine": _sb(256, BF), "qe": _sb(512), "sm": _sb(128, BF), "fb": _sb(768, BF),
+    "FX": _sb(4096), "ie": _sb(1024), "inn": _sb(1024), "mm": _sb(1024), "oo": _sb(1024),
+    "qa": _sb(768), "bits": _sb(512, BF), "dq": _sb(256),
+    "sa": _sb(448 * 6, BF), "la": _sb(576 * 6, BF), "se": _sb(192 * 7, BF), "le": _sb(576 * 7, BF),
+    "sb": _sb(384 * 6), "lb": _sb(384 * 6), "sg": _sb(192 * 7), "lg": _sb(192 * 7),
+    "WI": _sb(V, BF), "WC": _sb(V, BF), "IR": _sb(384, BF), "oneb": _sb(480, BF), "SG": _sb(480, BF), "row2": _sb(256, BF),
+    "HH": _sb(256), "neg": _sb(128, BF), "BW": _sb(384, BF), "away": _sb(512), "lose": _sb(512, BF), "CC": _sb(960, BF),
+    "tie": _sb(192, BF),
+    "ml": _sb(240, U16),
 }
 NDMA = 20
 SEMAPHORES = (["cV", "cA", "cP", "cG"] + ["d%d" % i for i in range(NDMA)]
-              + ["%s%d" % (s, r) for s in ("ra", "rb", "rg", "ta", "tb", "tg") for r in range(RO + 1)])
+              + ["%s%d" % (s, r) for s in ("re", "rb", "rg", "te", "ta", "tb", "tg") for r in range(RO + 1)]
+              + ["ra%d_%d" % (r, s) for r in range(1, RO) for s in range(4)])
 PSUM = ("PD", "PN", "PF", "P6", "P7")
 
 
@@ -142,16 +152,23 @@ def rank_program(g, core, T, topo):
         return
     N = len(T.cores)
     add, dma, emit = _builder(g, T)
+    place = {"Q0": ("QL", CAP, W), "Q1": ("QL", S + CAP, W), "N0": ("QL", 0, CAP), "N1": ("QL", S, CAP),
+             "qn": ("FX", 0, 2048), "ue": ("FX", 2048, 1024), "un": ("FX", 3072, 1024), "MM": ("FX", 0, 3840),
+             "ymo": ("ie", 0, V), "yto": ("inn", 0, V)}
 
-    def a(name, lo=0, hi=None, step=1):
-        if name == "WM":
-            name, lo, hi = "WN", lo + CAP, (W if hi is None else hi) + CAP
+    def a(name, lo=0, hi=None, step=1, p0=0, p1=128):
+        if name in place:
+            name, o, n = place[name]
+            lo, hi = lo + o, (n if hi is None else hi) + o
         if hi is None:
             hi = T[name].shape[1]
         if step == 1:
-            return (T[name][:, lo:hi], (name, lo, hi))
+            return (T[name][p0:p1, lo:hi], (name, lo, hi))
         last = lo + (hi - lo - 1) // step * step
-        return (T[name][:, lo:last + 1:step], (name, lo, last + 1, step))
+        return (T[name][p0:p1, lo:last + 1:step], (name, lo, last + 1, step))
+
+    def top(b, name, lo, hi):
+        return a(name, lo, hi, 1, 0, B * (b + 1))
 
     def ind(win, off):
         return (win[0].indirect(off[0]), win[1], off[1])
@@ -222,8 +239,11 @@ def rank_program(g, core, T, topo):
             add("G", lambda: g.iota(out[0], pattern, base, cm), [], [out[1]])
 
     ADD, SUB, MUL, MAX, MIN = ALU.add, ALU.subtract, ALU.mult, ALU.max, ALU.min
-    EQ, GT, LE, LT = ALU.is_equal, ALU.is_gt, ALU.is_le, ALU.is_lt
+    EQ, GT, GE, LE, LT = ALU.is_equal, ALU.is_gt, ALU.is_ge, ALU.is_le, ALU.is_lt
     SHR, AND = ALU.arith_shift_right, ALU.bitwise_and
+
+    def pick(out, in_, pattern, base):
+        add("G", lambda: g.affine_select(out[0], in_[0], pattern, EQ, 0.0, base, 1), rd(in_), [out[1]])
 
     def split(src):
         peers = [(src + d) % N for d in range(1, N)]
@@ -233,28 +253,35 @@ def rank_program(g, core, T, topo):
         parts = [eng[0:q], eng[q:3 * q], eng[3 * q:4 * q]]
         return {p: parts[i] for i, p in enumerate(peers)}
 
-    def send(kind, r, width, c0, c1):
+    def count(s):
+        return sum([len(x) for x in split(s).values()])
+
+    def spray(kind, r, src):
+        mask = 0
+        for part in split(rank).values():
+            for e in part:
+                mask |= 1 << e
+        land, ids, dsts = "l" + kind, [], []
+        for d in range(1, N):
+            rid, pid, _ = topo.addr(T.cores[(rank + d) % N])
+            ids.append(DstId(rid=rid, pnc=pid))
+            do = 576 * r + (N - d - 1) * 192
+            dsts.append(T[land][:, do:do + 192])
+        sem = "re%d" % r if kind == "e" else "ra%d_%d" % (r, rank)
+        ls = "t%s%d" % (kind, r)
+        tr = RemoteDMATransfer(dst_ids=ids, dma_engine_mask=mask, remote_sem=T.sem[sem], srcs=[src[0]], dsts=dsts)
+        add("G", lambda: g.remote_dma_fused([tr], local_sem=T.sem[ls]), [src[1]], [], (ls, count(rank)))
+        if kind == "e":
+            add("X", None, [], [(land, 576 * r, 576 * r + 576)], (sem, sum([count(s) for s in range(N) if s != rank])))
+            return
+        for d in range(1, N):
+            s, o = (rank + d) % N, 576 * r + 192 * (d - 1)
+            add("X", None, [], [(land, o, o + 192)], ("ra%d_%d" % (r, s), count(s)))
+
+    def send(kind, r, width):
         sbuf, lbuf = "s" + kind, "l" + kind
         base = r * 3 * width
         mine = split(rank)
-        if kind == "a":
-            mask, n = 0, 0
-            for p in mine:
-                for e in mine[p]:
-                    mask |= 1 << e
-                    n += 1
-            ids, dsts = [], []
-            for d in range(1, N):
-                rid, pid, _ = topo.addr(T.cores[(rank + d) % N])
-                ids.append(DstId(rid=rid, pnc=pid))
-                do = 3 * base + (N - d - 1) * 192
-                dsts.append(T.la[:, do:do + 192])
-            tr = RemoteDMATransfer(dst_ids=ids, dma_engine_mask=mask, remote_sem=T.sem["ra%d" % r],
-                                   srcs=[T.sa[:, base:base + 192]], dsts=dsts)
-            add("G", lambda: g.remote_dma_fused([tr], local_sem=T.sem["ta%d" % r]), [("sa", base, base + 192)], [], ("ta%d" % r, n))
-            got = sum([sum([len(x) for x in split(s).values()]) for s in range(N) if s != rank])
-            add("X", None, [], [("la", 3 * base, 3 * base + 576)], ("ra%d" % r, got))
-            return
         trs, n = [], 0
         for d in range(1, N):
             p = (rank + d) % N
@@ -267,14 +294,14 @@ def rank_program(g, core, T, topo):
             do = base + (N - d - 1) * width
             trs.append(RemoteDMATransfer(dst_ids=[DstId(rid=rid, pnc=pid)], dma_engine_mask=mask,
                                          remote_sem=T.sem["r%s%d" % (kind, r)],
-                                         src=T[sbuf][:, so + c0:so + c1], dst=T[lbuf][:, do + c0:do + c1]))
+                                         src=T[sbuf][:, so:so + width], dst=T[lbuf][:, do:do + width]))
         ls = "t%s%d" % (kind, r)
         add("G", lambda: g.remote_dma_fused(trs, local_sem=T.sem[ls]), [(sbuf, base, base + 3 * width)], [], (ls, n))
         got = sum([len(split(s)[rank]) for s in range(N) if s != rank])
         add("X", None, [], [(lbuf, base, base + 3 * width)], ("r%s%d" % (kind, r), got))
 
-    def shift(name, d):
-        return a(name, 16, 144) if rank < (rank + d) % N else a(name, 112, 240)
+    def shift(name, d, o=0):
+        return a(name, o + 16, o + 144) if rank < (rank + d) % N else a(name, o + 112, o + 240)
 
     col = {}
 
@@ -299,47 +326,71 @@ def rank_program(g, core, T, topo):
     def oq(j):
         return a("OQ", j, j + 1)
 
-    def weights(*chains):
+    def bi(i):
+        return a("BI", 128 * i, 128 * i + 128)
+
+    def weights(*chains, eng="A"):
         for i in range(max([len(ch[2]) for ch in chains])):
             for (name, first, terms) in chains:
-                if i < len(terms):
+                if i < len(terms) and eng == "A":
                     act(c(name), terms[i][0], AF.Identity, first if i == 0 else c(name), float(terms[i][1]))
+                elif i < len(terms):
+                    ts(c(name), terms[i][0], float(terms[i][1]), MUL, first if i == 0 else c(name), ADD)
 
     def scaled(out, base, w):
         act(out, base, AF.Copy, None, w)
 
-    def take_meta(r):
+    def rim(r):
+        return a("sa", 448 * r + CAP, 448 * r + 448)
+
+    def mine_of(land, r, d):
+        s = 576 * r + 192 * (d - 1) + 64 * (N - d - 1)
+        return a(land, s, s + 64)
+
+    def take_meta(r, P):
         for d in range(1, N):
             o = 64 * (d - 1)
-            s = 576 * r + 192 * (d - 1) + 64 * (N - d - 1)
-            group(a("P7", o, o + 64), [(shift("JM", d), a("la", s, s + 64)),
-                                       (sl("NY"), a("yfor", o, o + 64))])
-        act(a("WM", V, V + FP), a("P7", 0, 192))
+            keep = [(a("JM", 256, 384) if r == 1 else a("JM", 0, 128), a("WM", V + o, V + o + 64))] if r else []
+            group(a(P, o, o + 64), keep + [(sl("NY"), a("yfor", o, o + 64)), (shift("JM", d), mine_of("le", r, d))])
+
+    def put_meta(P):
+        act(a("WM", V, V + FP), a(P, 0, 192))
 
     def take_data(r):
         for f in range(2):
             for d in range(1, N):
-                s = 384 * r + 128 * (d - 1) + 64 * f
-                mm(a("PN", 192 * f + 64 * (d - 1), 192 * f + 64 * d), shift("J2", d), a("lb", s, s + 64))
+                s = 384 * r + 128 * (d - 1)
+                src = a("lb", s + f, s + 128, 2) if r else a("lb", s + 64 * f, s + 64 * f + 64)
+                mm(a("PN", 192 * f + 64 * (d - 1), 192 * f + 64 * d), shift("J2", d), src)
 
     def put_data():
         for f in range(2):
-            act(a("QL", W * f + V, W * f + V + FP), a("PN", 192 * f, 192 * f + 192))
+            act(a("Q%d" % f, V, V + FP), a("PN", 192 * f, 192 * f + 192))
 
-    def take_gifts(r, P="P6"):
+    def take_gifts(r, P="P6", o=64):
         for d in range(1, N):
             s = 192 * r + 64 * (d - 1)
-            mm(a(P, 64 * (d - 1), 64 * d), shift("J2", d), a("lg", s, s + 64))
+            mm(a(P, o + 64 * (d - 1), o + 64 * d), shift("J2", d), a("lg", s, s + 64))
 
-    def put_gifts(r, P="P6"):
-        act(a("QL", LOG + R * r + 512, LOG + R * r + 704), a(P, 0, 192))
+    def put_gifts(r, P="P6", o=64):
+        act(a("QL", LOG + R * r + 512, LOG + R * r + 704), a(P, o, o + 192))
 
-    def give(eng, r):
-        take(eng, a("sg", 192 * r, 192 * r + 192), ind(a("QL", LOG, LOG + R * r + 512), a("glist", 0, 12)))
-        send("g", r, 64, 0, 64)
+    def fresh(r):
+        return a("QL", LOG + R * r - 512, LOG + R * r + 512)
+
+    def rim_gifts(r):
+        act(a("f2", 0, 192) if r > 1 else a("sg", 192, 384), ind(fresh(r), a("glist", 0, 12)))
+
+    def give(r):
+        if r > 1:
+            tt(a("sg", 192 * r, 192 * r + 192), ind(a("oo"), a("glist", 0, 12)), a("f2", 0, 192), ADD)
+        send("g", r, 64)
+
+    def clocks(eng, lo, hi):
+        take(eng, a("GG", 16 * lo, 16 * hi), ind(a("WM"), a("colw", lo, hi)))
 
     def chunk(eng, j):
-        take(eng, a("GG", 480 * j, 480 * j + 480), ind(a("WM"), a("colw", 30 * j, 30 * j + 30)))
+        clocks(eng, 30 * j, 30 * j + 30)
 
     def zterm(j, start, stop):
         for i in (2 * j, 2 * j + 1):
@@ -350,190 +401,303 @@ def rank_program(g, core, T, topo):
         group(a("PF", o, o + 120), [(sl("LK", 3 - k), a("GG", 480 * j + k, 480 * j + 480, 4)) for k in range(4)]
               + [(sl("LO"), a("WM", 120 * j, 120 * j + 120))])
 
-    def quad(out, terms):
-        group(out, [(sl(nme, 12 - 4 * j), a(src, j, 256, 4)) for (nme, src) in terms for j in range(4)])
+    def keys(P, o, lo, hi):
+        for i in range(lo, hi):
+            mm(a(P, o, o + 60), sl("E", 15 - i), a("WM", 60 * i, 60 * i + 60), i == 0, i == 15)
 
-    def spread(dst, h, f):
-        for i in range(16):
-            mm(a(dst, 512 * h + i, 512 * h + 512, 16), a("BI", 128 * i, 128 * i + 128),
-               a("fb", 64 * f + 32 * h, 64 * f + 32 * h + 32))
+    def duel(r, b):
+        o, out = 448 * r + CAP + 64 * b, top(b, "PN", 512 * b, 512 * b + 128)
+        own = (a("sa", o, o + 64 * b + 64), a("BW", 256, 384))
+        tie = (a("tie", 64 * b, 128 * b + 64), a("oneb", 0, 128))
+        if b == 0:
+            group(out, [tie, own, (mine_of("la", r, 1), shift("BW", 1))])
+        else:
+            mm(out, *own, True, False)
+            for d in (3, 2):
+                mm(a("PN", 512, 640, 1, B * (d - 2), B * (d - 1)), mine_of("la", r, d), shift("BW", d), False, False)
+            mm(out, *tie, False, True)
+        for h in range(2):
+            lo = 256 * b + 128 * h
+            tt(top(b, "lose", lo, lo + 128), top(b, "PN", 512 * b, 512 * b + 128), top(b, "away", lo, lo + 128), GE)
+
+    def deliver(b):
+        for q in range(4):
+            for h in range(2):
+                lo, co = 256 * b + 128 * h + 32 * q, 480 * b + 60 * (2 * q + h)
+                mm(a("P7", 0, 60, 1, 32 * q, 32 * q + 32), top(b, "lose", lo, lo + 32), top(b, "CC", co, co + 60), False, False)
+        if b == 0:
+            keys("P7", 0, 15, 16)
+
+    def quad(out, terms, off=None):
+        group(out, [(sl(nme, 12 - 4 * j), a(src, j, 256, 4)) for (nme, src) in terms for j in range(4)]
+              + ([(sl("OFF"), off)] if off else []))
+
+    def spread(dst, h, src, o=0):
+        for k in range(4):
+            mm(a(dst, 512 * h + k, 512 * h + 512, 4), bi(8 + k), a(src, o + 128 * h, o + 128 * h + 128))
 
     TIT = [("TI1", 0, 1), ("TI2", 0, 1)]
     add("V", lambda: g.vector.memset(T.TI[:], 0), [], [("TI", 0, V)] + TIT)
     dma("S", T.rm[:, 0:12], T.rim[:], [], [("rm", 0, 12)])
     dma("S", T.pt[:], T.port[:], [], [("pt", 0, 240)])
     dma("S", T.TI[0:128:16, :], T.t0[:], [], [("TI", 0, V)])
-    dma("A", T.TI[1:128:16, :], T.d0[:], [], [TIT[0]])
-    dma("S", T.TI[2:128:16, :], T.d0[:], [], [TIT[1]])
+    dma("A", T.TI[5:128:16, :], T.d0[:], [], [TIT[0]])
+    dma("S", T.TI[6:128:16, :], T.d0[:], [], [TIT[1]])
     dma("S", T.thr[:, 0:1], T.th[:], [], [("thr", 0, 1)])
     iota(a("pc", 0, 1), [[0, 1]], 0, 1, False)
     iota(a("rowj"), [[1, 256]], 0, 0)
     dma("S", T.qb[:, 0:V], T.q0[:], [], [("qb", 0, V)])
     dma("S", T.qb[:, V:2 * V], T.q1[:], [], [("qb", V, 2 * V)])
-    iota(a("yfor"), [[1, 48], [0, 4]], 128, 0)
-    iota(a("QL", V, W), [[0, W - V]], 0, 0)
+    for f, n in enumerate((16, 4, 2)):
+        iota(a("rows", 144 * f, 144 * f + 144), [[1, 144 // n], [0, n]], 0, 0)
+    iota(a("j16"), [[0, 16], [1, 16]], 0, 0)
+    iota(a("QL", CAP + V, S + CAP), [[0, S - V]], 0, 0)
     ts(a("pc", 1, 2), a("pc", 0, 1), 15, AND)
     ts(a("pc", 2, 3), a("pc", 0, 1), 3, AND)
     ts(a("pc", 3, 4), a("pc", 0, 1), 12, AND)
-    for nme in ("p", "lane", "k", "q4"):
+    ts(a("pc", 4, 5), a("pc", 0, 1), 1, AND)
+    ts(a("pc", 5, 6), a("pc", 0, 1), 4, SHR)
+    for nme in ("p", "lane", "k", "q4", "odd", "g"):
         c(nme)
-    cp(a("cc", 0, 4), a("pc", 0, 4))
+    cp(a("cc", 0, 6), a("pc", 0, 6))
     ms(a("WM", V, W), 0.0)
     ts(a("OH"), a("rowj", 0, 16), c("lane"), EQ)
     ts(a("OQ"), a("rowj", 0, 16, 4), c("q4"), EQ)
     ts(a("QP"), a("rowj"), c("p"), SUB)
     ts(c("k12"), c("k"), 12.0, ADD)
-    weights(("ia", -1.0, [(oh(0), 2)]), ("ib", 0.0, [(oh(1), 7), (oh(2), 10)]),
-            ("lo", 0.0, [(oh(1), 4), (oh(2), 8), (oh(3), 1), (oh(8), -128)]),
-            ("hi", 0.0, [(oh(0), 99), (oh(1), 5), (oh(2), 9), (oh(3), 1), (oh(8), 200)]),
-            ("n8", 1.0, [(oh(8), -1)]), ("wd", 0.0, [(oh(1), -2), (oh(2), -1), (oh(3), 20)]),
-            ("wA", 0.0, [(oh(4), R), (oh(8), 4)]), ("wL", 0.0, [(oh(0), -1), (oh(4), 1), (oh(8), 1)]))
-    weights(("wb", c("wd"), [(oh(0), 1)]), ("l3", 3.0, [(c("lane"), 1)]), ("l60", 1216.0, [(c("lane"), -60)]))
+    weights(("lo0", oh(3), [(oh(1), 6), (oh(2), 10), (oh(6), 2)]),
+            ("up0", oh(3), [(oh(0), 99), (oh(1), 6), (oh(2), 10), (oh(5), 2), (oh(6), 4)]),
+            ("wd", oh(5), [(oh(1), -2), (oh(2), -1), (oh(3), 20), (oh(6), 1)]),
+            ("wL", oh(4), [(oh(0), -1), (oh(8), 1)]), ("l3", 3.0, [(oh(4), 8), (oh(8), 12)]),
+            ("n8", 1.0, [(oh(8), -1)]), ("g4", 3.0, [(c("g"), 4)]), ("g8", 1.0, [(c("g"), 8)]))
+    act(a("P7", 0, 240), a("rowj", 0, 240), AF.Identity, c("lane"), 16.0)
+    weights(("wb", c("wd"), [(oh(0), 1)]), ("l60", 1216.0, [(c("lane"), -60)]), ("no0", 0.0, [(oh(0), -1)]))
     ts(a("QG"), a("QP"), c("lane"), ADD)
     ts(a("J2", 0, 128), a("QP", 0, 128), 0.0, EQ)
-    ts(a("J2", 128, 256), a("QP", 0, 128), 0.0, EQ)
     ts(a("i4", 0, 12), a("rm", 0, 12), 2, SHR)
-    ts(m("C15"), a("QG", 0, 144), 15.0, EQ)
+    ts(a("J2", 128, 256), a("QP", 0, 128), 0.0, EQ)
     cp(a("rime", 0, 12), a("i4", 0, 12))
+    ts(m("C15"), a("QG", 0, 144), 15.0, EQ)
     ts(m("P4"), a("QG", 0, 144), c("k12"), EQ)
-    ts(a("lohi", 0, 7), a("rowj", 0, 7), oh(4), MUL, c("lo"), ADD)
-    ts(a("lohi", 8, 15), a("rowj", 0, 7), oh(4), MUL, c("hi"), ADD)
-    ts(m("NY"), a("QG", 0, 144), 8.0, EQ, oh(0), MUL)
-    cp(a("f2", 0, 192), ind(a("TI"), a("rime", 0, 12)), TIT)
     ts(a("i1"), a("pt"), 2, SHR)
-    ts(a("b1", 0, 192), a("f2", 0, 192), c("ia"), MUL, c("ib"), ADD)
-    ts(a("i2"), a("pt"), -2880.0, ADD)
-    ts(a("sa", 0, 192), a("b1", 0, 192), a("lohi", 0, 1), MAX, a("lohi", 8, 9), MIN)
-    send("a", 0, 64, 0, 64)
-    for d in range(3):
-        cp(a("slist", 8 * d, 8 * d + 4), a("i4", 4 * d, 4 * d + 4))
-        ts(a("slist", 8 * d + 4, 8 * d + 8), a("i4", 4 * d, 4 * d + 4), float(W), ADD)
-    scaled(a("JM"), a("J2"), c("n8"))
-    scaled(m("E"), m("C15"), c("wb"))
+    ts(a("P6", 0, 240), a("pt"), -2880.0, ADD)
+    ts(rim(0), ind(a("TI"), a("rime", 0, 12)) + tuple(TIT), c("lo0"), MAX, c("up0"), MIN)
+    spray("e", 0, rim(0))
     for j in range(4):
         scaled(m("T%d" % j), m("P4"), oq(j))
-    act(a("c16"), a("rowj", 0, 240), AF.Identity, c("lane"), 16.0)
-    act(a("QL", 0, V), a("qb", 0, V))
-    act(a("QL", W, W + V), a("qb", V, 2 * V))
-    act(a("sb", 0, 384), ind(a("QL", 0, W + V), a("slist", 0, 24)))
-    iota(a("j16"), [[0, 16], [1, 16]], 0, 0)
-    send("b", 0, 128, 0, 128)
-    iota(a("eperm"), [[1, 60], [60, 16]], 64, 0)
-    iota(a("QL", W + V, LOG + 704), [[0, LOG + 704 - W - V]], 0, 0)
-    tt(a("i1"), a("i1"), a("i2"), MAX)
-    ts(a("b1"), a("pt"), float(4 * V + B * (N - 1 - rank)), LT, 4.0, MUL)
-    tt(a("b2"), a("pt"), a("c16"), GT)
-    cp(a("FW", 0, 240), a("i1"))
-    tt(a("b1"), a("b1"), a("b2"), MUL)
+    act(a("Q0", 0, V), a("qb", 0, V))
+    act(a("Q1", 0, V), a("qb", V, 2 * V))
+    tt(a("P6", 0, 240), a("i1"), a("P6", 0, 240), MAX)
+    tt(a("b2"), a("pt"), a("P7", 0, 240), GT)
+    ts(a("erim", 16, 28), a("P7", 0, 12), float(CAP), ADD)
+    cp(a("FW", 0, 240), a("P6", 0, 240))
+    ts(a("P7", 256, 496), a("pt"), float(4 * V + B * (N - 1 - rank)), GE, 0.5, ADD)
     ts(a("i3"), a("pt"), 3, AND)
-    ts(a("FW", 480, 720), a("b1"), -2.0, ADD)
-    tt(a("FW", 240, 480), a("i1"), a("FW", 0, 240), SUB)
+    tt(a("FW", 240, 480), a("P6", 0, 240), a("FW", 0, 240), SUB)
+    tt(a("FW", 480, 720), a("b2"), a("P7", 256, 496), SUB)
     ts(a("FW", 720, 960), a("i3"), c("k"), SUB)
+    for d in range(3):
+        cp(a("slist", 8 * d, 8 * d + 4), a("i4", 4 * d, 4 * d + 4))
+        ts(a("slist", 8 * d + 4, 8 * d + 8), a("i4", 4 * d, 4 * d + 4), float(S), ADD)
+    act(a("sb", 0, 384), ind(a("QL", CAP, S + CAP + V), a("slist", 0, 24)))
+    iota(a("yfor"), [[1, 48], [0, 4]], 128, 0)
+    send("b", 0, 128)
+    iota(a("R4"), [[0, 60], [-1000, 4]], 1000, 0)
+    iota(a("ones"), [[0, 128]], 1, 0)
+    scaled(a("JM", 0, 256), a("J2"), c("n8"))
+    scaled(m("E"), m("C15"), c("wb"))
     for h in range(2):
         for j in range(4):
             group(a("PD", 512 * h + j, 512 * h + 480, 4),
                   [(sl("T%d" % j, 12 - 4 * f), a("FW", 240 * f + 120 * h, 240 * f + 120 * h + 120)) for f in range(4)])
-    ts(a("TB"), a("TI"), c("ia"), MUL, c("ib"), ADD)
-    cp(a("colw"), a("i1"))
-    ts(a("WM", 0, V), a("TB"), a("lohi", 0, 1), MAX, a("lohi", 8, 9), MIN)
-    cp(a("SW", 0, 480), a("PD", 0, 480))
-    ts(m("x"), a("QG", 0, 144), 15.5, LT)
-    ts(sl("BD"), a("QG", 0, 128), -0.5, GT)
-    cp(a("SW", 480, 960), a("PD", 512, 992))
-    ts(m("Q"), a("QG", 0, 144), 11.5, GT)
-    tt(sl("BD"), sl("BD"), sl("x"), MUL)
-    tt(m("Q"), m("Q"), m("x"), MUL)
-    for i in range(16):
-        bi = a("BI", 128 * i, 128 * i + 128)
-        add("G", lambda bi=bi, i=i: g.affine_select(bi[0], sl("BD")[0], [[-16, 8], [0, 16]], EQ, 0.0, -i, 1),
-            rd(sl("BD")), [bi[1]])
-    weights(("wzd", oq(0), [(oh(12), -1)]), ("wdl", oq(1), [(oh(13), -1)]), ("wnd", oh(13), [(oq(1), -1)]),
-            ("wan", 0.0, [(oq(1), R), (oq(2), 4)]), ("wae", 0.0, [(oh(13), R), (oh(14), 4)]),
-            ("wnl", oq(0), [(oq(1), 1)]), ("whd", 0.0, [(oh(12), -0.5)]))
+    cp(a("colw"), a("P6", 0, 240))
+    ts(a("WM", 0, V), a("TI"), c("lo0"), MAX, c("up0"), MIN)
+    ts(sl("BD"), a("rows", 0, 128), c("g"), EQ)
+    ts(m("Q"), a("rows", 144, 288), c("g4"), EQ)
+    ts(m("NY"), a("QG", 0, 144), 8.0, EQ, oh(0), MUL)
+    add("G", lambda: g.affine_select(sl("TR")[0], sl("BD")[0], [[1, 128]], GT, 0.0, 0, -1), rd(sl("BD")), [sl("TR")[1]])
+    iota(a("eperm"), [[1, 60], [60, 16]], 64, 0)
     for k in range(4):
         scaled(m("K%d" % k), m("C15"), oh(8 + k))
-    act(a("dum"), a("rowj"), AF.Silu, 1216.0)
-    take_meta(0)
-    group(a("P6", 240, 300), [(sl("E", 15 - i), a("WM", 60 * i, 60 * i + 60)) for i in range(16)])
+    act(a("SW", 0, 480), a("PD", 0, 480))
+    act(a("SW", 480, 960), a("PD", 512, 992))
+    act(a("CX", 0, CAP), a("rowj"), AF.Silu, 1216.0)
+    keys("P6", 240, 0, 16)
     for k in range(4):
         group(a("PN", k, 240, 4), [(sl("K%d" % k, 15 - i), a("SW", 60 * i, 60 * i + 60)) for i in range(16)])
-    ts(m("y"), m("Q"), oq(3), MUL)
-    cp(m("I", 0, 128), a("J2", 0, 128))
-    tt(m("U"), m("P4"), m("y"), MAX)
-    ms(a("R4"), 0.0)
-    ms(a("ones"), 1.0)
-    ms(a("cst"), -129.0)
-    cp(a("erim", 0, 12), a("i4", 0, 12))
-    ts(sl("TR"), a("QG", 0, 128), c("lane"), GT)
-    ms(a("R4", 0, 240, 4), 1000.0)
+    take_meta(0, "P7")
     ts(m("LK"), a("QG", 0, 144), c("l3"), EQ, c("wL"), MUL)
-    tt(sl("TR"), sl("TR"), sl("x"), MUL)
-    ms(sl("LO"), 0.0)
-    ts(a("x1", 0, 8), a("QG", 0, 128, 16), 0.0, EQ)
-    for j, wv in ((0, "wb"), (1, "wb"), (2, "wb"), (3, "wb"), (15, "wb"), (12, "wd"), (13, 4), (14, 8)):
-        lo = mat["LO"] * 144
-        ts(a("MT", lo + j, lo + 128, 16), a("x1", 0, 8), c(wv) if isinstance(wv, str) else oh(wv), MUL)
+    ts(m("y"), a("QG", 0, 144), 7.0, EQ, c("no0"), MUL)
+    ts(sl("LO"), sl("Q", 12), c("wb"), MUL)
+    ts(sl("z"), sl("Q", 8), oh(0), MUL)
+    cp(m("I", 0, 128), a("J2", 0, 128))
+    tt(m("LK"), m("LK"), m("y"), ADD)
+    tt(sl("LO"), sl("LO"), sl("z"), ADD)
+    ms(a("cst"), -129.0)
     ts(a("R16"), a("j16"), c("lane"), EQ, 1.0e6, MUL)
-    ms(a("SW", V, W), 0.0)
-    ms(a("LW", V, W), 0.0)
     ts(a("dneg", 0, 60), a("rowj", 0, 60), -1.0, MUL, c("l60"), ADD)
+    for i in range(16):
+        ts(bi(i), sl("BD"), oh(i), MUL)
+    weights(("wx", 0.0, [(oq(0), 2), (oq(1), -2)]), ("wy1", 0.0, [(oq(0), -0.5), (oq(1), 0.5)]),
+            ("wy2", 0.0, [(oq(0), 0.5), (oq(1), 0.5)]), ("wnl", oq(0), [(oq(1), 1)]),
+            ("dlo", 0.0, [(oq(2), -200), (oq(3), -200)]), ("prs", oh(0), [(oh(1), 1)]), ("pb", 0.0, [(oh(0), 128), (oh(1), -127)]))
+    put_meta("P7")
 
     def late_constants():
-        act(a("CW", 0, 256), a("dum"))
-        act(a("CX", 0, 256), a("dum"))
         scaled(m("NL"), m("P4"), c("wnl"))
-        for nme, wv in (("Z", oq(0)), ("ZD", c("wzd")), ("DT", oh(12))):
-            scaled(m(nme), m("U"), wv)
+        for nme, wv in (("XM", "wx"), ("Y1", "wy1"), ("Y2", "wy2")):
+            scaled(m(nme), m("P4"), c(wv))
+        scaled(m("QD"), m("Q"), c("wd"))
+        act(a("lohi", 16, 23), a("rowj", 0, 7), AF.Identity, c("pb"), oh(2))
+
+    def rim_constants():
+        iota(a("CW", 0, CAP), [[1, CAP]], 1216, 0)
+        iota(a("SW", V, W), [[0, W - V]], 0, 0)
+        iota(a("LW", V, W), [[0, W - V]], 0, 0)
+        iota(a("QL", S + CAP + V, LOG + 704), [[0, LOG + 704 - S - CAP - V]], 0, 0)
+        iota(a("N0"), [[0, CAP]], 0, 0)
+        iota(a("yrow"), [[1, CAP]], -128, 0)
+        for b in range(2):
+            pick(a("HH", 128 * b, 128 * b + 128), a("ones"), [[-16, 8], [-1, 8], [0, 2]], -8 * b)
+        iota(a("WI"), [[1, 16], [0, 60]], 0, 0)
+        iota(a("WC"), [[0, 16], [1, 60]], 0, 0)
+        iota(a("oneb"), [[0, 480]], 1, 0)
+        pick(a("SG"), a("oneb"), [[-16, 8], [0, 60]], 0)
+        iota(a("row2", 0, 128), [[0, 4], [100, 2], [1, 16]], 0, 0)
+        iota(a("row2", 128, 256), [[0, 4], [-100, 2], [1, 16]], 100, 0)
 
     def last_constants():
-        ts(sl("NC"), a("QG", 0, 128), 0.5, GT)
-        ts(sl("y"), a("QG", 0, 128), 2.5, LT)
-        ts(sl("NM"), a("QG", 0, 128), 0.0, EQ, oh(15), MUL)
-        tt(sl("NC"), sl("NC"), sl("y"), MUL)
         ts(a("i4", 0, 12), a("rm", 0, 12), 3, AND)
-        ts(sl("DB"), sl("BD"), c("whd"), MUL)
+        ts(sl("NC"), a("rows", 289, 417), c("g8"), EQ)
         ts(c("nth"), a("thr", 0, 1), -1.0, MUL)
-        ts(a("yrow"), a("rowj"), -128.0, ADD)
-        cp(a("krim", 0, 12), a("i4", 0, 12))
+        ts(a("erim", 0, 12), a("rime", 0, 12), float(CAP), ADD)
+        ms(a("neg"), -1.0 / 128)
+        ts(a("krim", 0, 12), a("i4", 0, 12), 0.25, MUL)
+        for d in range(1, N):
+            ms(a("tie", B * (d - 1), B * d), -1.0 / 128 / 128 if rank < (rank + d) % N else 0.0)
+
+    def list_constants():
+        weights(("wy", oh(0), [(oh(1), 2048)]), ("ce0", 0.0, [(oh(1), -64)]), ("ce4", oh(2), [(oh(1), -64)]),
+                ("off", 0.0, [(c("odd"), S)]))
+        scaled(m("KY"), m("C15"), c("wy"))
+        scaled(sl("NM"), sl("C15", 15), c("wb"))
+        scaled(sl("CE0"), sl("C15", 15), c("ce0"))
+        scaled(sl("CE4"), sl("C15", 11), c("ce4"))
 
     def second_constants():
-        for nme, wv in (("DL", c("wdl")), ("ND", c("wnd")), ("AN", c("wan")), ("AE", c("wae"))):
-            scaled(m(nme), m("U"), wv)
-        scaled(m("A"), m("C15"), c("wA"))
+        weights(("winv", 0.0, [(oh(1), 0.25), (oh(2), 0.5), (oh(3), -4.75), (oh(5), -0.5), (oh(6), -0.125)]),
+                ("hi", oh(3), [(oh(0), 99), (oh(1), 5), (oh(2), 9), (oh(8), 200)]),
+                ("lo", oh(3), [(oh(1), 4), (oh(2), 8), (oh(8), -128)]),
+                ("n85", c("n8"), [(oh(3), 4)]), eng="V")
+        for h in range(3):
+            ts(a("BW", 128 * h, 128 * h + 128), sl("BD"), c("wb"), MUL, (1.0 if h == 2 else -1.0) / 64, MUL)
+        ts(a("lohi", 0, 7), a("rowj", 0, 7), oh(4), MUL, c("lo"), ADD)
+        ts(a("lohi", 8, 15), a("rowj", 0, 7), oh(4), MUL, c("hi"), ADD)
+        ts(sl("IV"), sl("BD"), c("winv"), MUL)
+        ts(a("JM", 256, 384), a("JM", 0, 128), c("n85"), MUL)
+        ts(sl("ND"), sl("C15", 15), c("wd"), MUL)
+        ts(sl("NR"), sl("C15", 11), oh(4), MUL, -1.0, MUL)
 
-    for r in range(1, RO + 1):
-        if r == 1:
-            plan = (("A", 0), ("A", 1), ("A", 2), ("A", 3), ("A", 4), ("A", 5), ("V", 7), ("A", 6))
-        else:
-            group(a("P6", 240, 300), [(sl("E", 15 - i), a("WM", 60 * i, 60 * i + 60)) for i in range(16)])
-            take_meta(r - 1)
-            plan = (("A", 0), ("A", 1), ("V", 4), ("A", 2), ("V", 5), ("A", 3), ("V", 6), ("V", 7))
-        todo = list(range(8))
-        for n, (e, j) in enumerate(plan):
-            if r > 1 and n == 7:
-                act(a("GG", 3360, 3360 + 16 * CUT), ind(a("WM"), a("colw", 210, 210 + CUT)))
-                cp(a("GG", 3360 + 16 * CUT, 3840), ind(a("WM"), a("colw", 210 + CUT, 240)))
-            else:
-                chunk(e, j)
-            zterm(j, n == 0, n == 7)
-            if r > 1 and n in (0, 1, 3):
-                lterm(todo.pop(0))
-            if r == 1 and n == 4:
-                ts(a("leftb"), a("PN", 0, 240), 0.25, MUL)
-            if n == 5:
-                mm(a("P6", 0, 240), sl("I"), a("leftb"), False, False)
+    def spare(r):
         if r == 1:
             late_constants()
-        else:
-            give("A", r - 1)
-        scan(a("mn"), a("R4"), a("P6", 0, 240), MAX, MIN)
-        tt(a("ncn", 0, 60), a("mn", 3, 240, 4), a("P6", 240, 300), LE)
-        scan(a("inl", 0, 60), a("ones", 0, 60), a("ncn", 0, 60), ADD, SUB)
-        lterm(todo.pop(0))
-        if r > 1:
+        if r == 2:
+            weights(("wan", 0.0, [(oq(2), R), (oq(3), 4)]), ("wA", 0.0, [(oh(4), R), (oh(8), 4)]), ("no4", 0.0, [(oh(4), -1)]))
+            scaled(m("QN"), m("Q"), c("no4"))
+            scaled(m("AN"), m("P4"), c("wan"))
+            scaled(m("QA"), m("Q"), c("wA"))
+            scaled(sl("OFF"), sl("I"), -8192.0)
+        if r == 3:
+            weights(*[("c%d" % k, oh(k), [(oh(4 + k), 1)]) for k in range(4)])
+            for k in range(4):
+                scaled(m("K%d" % k), m("C15"), c("c%d" % k))
+        if r == 4:
+            for k in range(4):
+                scaled(m("F%d" % k), m("C15"), oh(12 + k))
+        if r == 5:
+            scaled(m("A"), m("C15"), c("wA"))
+            scaled(sl("x"), sl("C15", 15), oh(0))
+            scaled(sl("YT"), sl("C15", 14), c("wd"))
+
+    def onehots():
+        for b in range(2):
+            o, n, P = 64 * b, 64 * b + 64, ("P6", "P7")[b]
+            for h in range(2):
+                group(top(b, P, 256 + 128 * h, 384 + 128 * h),
+                      [(a("neg", 0, n), a("row2", 128 * h, 128 * h + 128)), (a("IR", o, o + n), bi(0))])
+            group(top(b, "PF", 512 * b, 512 * b + 480), [(a("neg", 0, n), a("WC", 0, 480)), (a("IR", 192 + o, 192 + o + n), a("SG"))])
+        for b in range(2):
+            act(top(b, "away", 256 * b, 256 * b + 256), top(b, ("P6", "P7")[b], 256, 512), AF.Abs)
+        for b in range(2):
+            act(top(b, "mm", 512 * b, 512 * b + 480), top(b, "PF", 512 * b, 512 * b + 480), AF.Abs)
+        for b in range(2):
+            act(top(b, "CC", 480 * b, 480 * b + 480), top(b, "mm", 512 * b, 512 * b + 480), AF.Relu, 128.0, -128.0)
+
+    rim_constants()
+    last_constants()
+    second_constants()
+    el = a("el")
+
+    def settle(f):
+        cp(ind(a("Q%d" % f), el), a("N%d" % f))
+
+    for r in range(1, RO + 1):
+        todo = list(range(8))
+        if r == 1:
+            cp(a("leftb"), a("PN", 0, 240))
+            mm(a("P6", 0, 240), sl("I"), a("leftb"), True, False)
+            for j in range(4):
+                chunk("A", j)
+                chunk("V", 7 - j)
+                zterm(j, False, False)
+                zterm(7 - j, False, j == 3)
+                if j < 3:
+                    lterm(todo.pop(0))
+            lterm(todo.pop(0))
             act(a("LW", 0, 480), a("PF", 0, 480))
+            spare(r)
+            scan(a("mn"), a("R4"), a("P6", 0, 240), MAX, MIN)
+            tt(a("ncn", 0, 60), a("mn", 3, 240, 4), a("P6", 240, 300), LE)
+        else:
+            keys("P7", 0, 0, 15)
+            mm(a("P6", 0, 240), sl("I"), a("leftb"), True, False)
+            jc = CUT // 30
+            for j in range(jc):
+                chunk("A", j)
+            clocks("A", 30 * jc, CUT)
+            for j in range(7, jc, -1):
+                chunk("V", j)
+            clocks("V", CUT, 30 * jc + 30)
+            plan = EARLY.split()
+            for x in plan:
+                j = int(x[1])
+                if x[0] == "z":
+                    zterm(j, False, x == [y for y in plan if y[0] == "z"][-1])
+                elif x[0] == "l":
+                    lterm(j)
+                    todo.remove(j)
+                elif x[0] == "d":
+                    duel(r - 1, j)
+                elif x[0] == "q":
+                    settle(j)
+                elif x[0] == "g":
+                    give(r - 1)
+                    if r > 2:
+                        new = fresh(r - 1)
+                        dma("G", new[0], T.oo[:], [("oo", 0, 1024), new[1]], [new[1]], True)
+                else:
+                    deliver(j)
+            act(a("LW", 0, 480), a("PF", 0, 480))
+            spare(r)
+            scan(a("mn"), a("R4"), a("P6", 0, 240), MAX, MIN)
+            tt(a("ncn", 0, 60), a("mn", 3, 240, 4), a("P7", 0, 60), LE)
+        scan(a("inl", 0, 60), a("ones", 0, 60), a("ncn", 0, 60), ADD, SUB)
+        for j in todo[:3]:
+            lterm(j)
+        if len(todo) < 4:
+            act(a("LW", 480, 960), a("PF", 512, 992))
         group(a("P7", 300, 301), [(sl("I"), a("cst", 0, 1)), (sl("TR"), a("inl", 59, 60))])
-        for j in todo:
+        for j in todo[3:]:
             lterm(j)
         tt(a("x1", 0, 60), a("ncn", 0, 60), a("dneg", 0, 60), MUL)
         tt(a("x2", 0, 60), a("x1", 0, 60), a("inl", 0, 60), ADD)
@@ -541,57 +705,39 @@ def rank_program(g, core, T, topo):
         ts(a("pm", 0, 60), a("x2", 0, 60), a("P7", 300, 301), ADD, 128.0, MIN)
         for i in range(16):
             o = 512 * (i // 8) + 60 * (i % 8)
-            mm(a("PD", o, o + 60), a("BI", 128 * i, 128 * i + 128), a("pm", 0, 60))
+            mm(a("PD", o, o + 60), bi(i), a("pm", 0, 60))
         take_data(r - 1)
         cp(ind(a("CW"), a("pos", 0, SPL)), a("eperm", 0, 16 * SPL))
         act(ind(a("CX"), a("pos", SPL, 60)), a("eperm", 16 * SPL, V), AF.Silu)
-        for h in range(0 if r == 1 else 1, 2):
-            act(a("LW", 480 * h, 480 * h + 480), a("PF", 512 * h, 512 * h + 480))
+        if len(todo) > 3:
+            act(a("LW", 480, 960), a("PF", 512, 992))
         for h in range(2):
-            act(a("PR", 480 * h, 480 * h + 480), a("PD", 512 * h, 512 * h + 480))
+            act(a("PR", 480 * h, 480 * h + 480), a("PD", 512 * h, 512 * h + 480), AF.Relu, a("lohi", 16 + r, 17 + r), c("prs"))
+        if r > 1:
+            put_data()
         scan(a("sc", 256, 512), a("R16"), a("CX", 0, 256), MAX, MIN)
         scan(a("sc", 0, 256), a("R16"), a("CW", 0, 256), MAX, MIN)
         tt(a("x1", 0, 16), a("sc", 15, 256, 16), a("sc", 271, 512, 16), MIN)
-        ts(a("el"), a("x1", 0, 16), -63.75, ADD)
-        el = a("el")
+        ts(el, a("x1", 0, 16), -63.75, ADD)
+        if r < RO:
+            for win in ("CW", "CX"):
+                iota(a(win, 0, CAP), [[1, CAP]], 1216, 0)
         act(a("sta"), ind(a("SW"), el))
-        cp(a("dyn"), ind(a("LW"), el))
-        quad(a("P7", 0, 64), [("NL", "sta")])
-        quad(a("P6", 0, 64), [("Z", "dyn")])
-        quad(a("P6", 64, 128), [("ZD", "dyn")])
-        quad(a("P6", 128, 192), [("T2", "sta")])
-        quad(a("P6", 192, 256), [("DT", "dyn")])
-        cp(a("qe", 0, 256), ind(a("QL", 0, W), el))
-        cp(a("nl"), a("P7", 0, 64))
-        act(a("qe", 256, 512), ind(a("QL", W, 2 * W), el))
-        put_data()
-        if r > 1:
-            quad(a("P7", 0, 64), [("DL", "dyn")])
-            quad(a("P7", 64, 128), [("ND", "dyn")])
-            quad(a("P7", 128, 192), [("AN", "dyn"), ("T3", "sta")])
-            quad(a("P7", 192, 256), [("AE", "dyn")])
-        for h in range(2):
-            act(a("qn", 512 * h, 512 * h + 512), ind(a("QL", 0, W), a("nl", 32 * h, 32 * h + 32)))
-            act(a("qn", 1024 + 512 * h, 1536 + 512 * h), ind(a("QL", W, 2 * W), a("nl", 32 * h, 32 * h + 32)))
-        ts(a("sm", 0, 128), a("P6", 0, 128), 0.0, MAX, 0.5, MUL)
-        tt(a("sm", 128, 192), a("sm", 0, 64), a("sm", 64, 128), SUB)
-        tt(a("fb", 0, 64), a("sm", 128, 192), a("P6", 128, 192), MUL)
-        tt(a("sm", 192, 256), a("P6", 192, 256), a("sm", 128, 192), SUB)
-        tt(a("sm", 256, 320), a("P6", 0, 64), a("sm", 128, 192), SUB)
-        spread("PD", 0, 0)
-        tt(a("fb", 64, 128), a("sm", 192, 256), a("fb", 0, 64), MUL)
-        tt(a("fb", 128, 192), a("sm", 256, 320), a("fb", 0, 64), MUL)
-        ts(a("fb", 192, 256), a("P6", 128, 192), 0.25, MUL)
-        spread("PF", 0, 1)
-        spread("PD", 1, 0)
-        spread("PF", 1, 1)
-        if r > 1:
-            take_gifts(r - 1)
-        spread("PN", 0, 2)
-        spread("PN", 1, 2)
-        if r == 1:
-            last_constants()
+        ts(a("dyn"), ind(a("LW"), el), c("dlo"), MAX)
+        act(a("mine"), ind(a("WM"), el))
+        mm(a("PN", 512, 768), sl("XM", 4), a("dyn"))
+        quad(a("P6", 0, 64), [("NL", "sta")])
+        group(a("PF", 512, 768), [(sl("Y1", 4), a("dyn")), (sl("QD", 4), a("mine"))])
+        mm(a("PF", 768, 1024), sl("Y2", 4), a("dyn"))
+        cp(a("qe", 0, 256), ind(a("Q0"), el))
+        tt(a("fb", 0, 256), a("PN", 512, 768), a("sta"), MUL)
+        cp(a("nl"), a("P6", 0, 64))
+        take(QE1, a("qe", 256, 512), ind(a("Q1"), el))
+        spread("PD", 0, "fb")
+        tt(a("fb", 256, 512), a("PF", 512, 768), a("fb", 0, 256), MUL)
+        spread("PF", 0, "fb", 256)
         logw = a("QL", LOG, LOG + R * r - 512)
+
         def hf(name, h, o=0):
             return a(name, o + 512 * h, o + 512 * h + 512)
 
@@ -600,6 +746,19 @@ def rank_program(g, core, T, topo):
             if name == "ue":
                 for k in range(4):
                     tt(a("ue", lo + k, hi, 4), a("qe", 128 * h, 128 * h + 128), a("PD", lo + k, hi, 4), MUL)
+            elif name == "fb":
+                tt(a("fb", 512, 768), a("PF", 768, 1024), a("fb", 0, 256), MUL)
+                spread("PD", 1, "fb")
+                spread("PF", 1, "fb", 256)
+                if r > 1:
+                    quad(a("P7", 0, 64), [("T2", "dyn"), ("QN", "mine")])
+                spread("PN", 0, "fb", 512)
+                spread("PN", 1, "fb", 512)
+                if r > 1:
+                    take_gifts(r - 1)
+            elif name == "qn":
+                for f in range(2):
+                    act(hf("qn", h, 1024 * f), ind(a("Q%d" % f), a("nl", 32 * h, 32 * h + 32)))
             elif name == "we":
                 for k in range(4):
                     tt(a("PF", lo + k, hi, 4), a("qe", 256 + 128 * h, 384 + 128 * h), a("PF", lo + k, hi, 4), MUL)
@@ -611,7 +770,7 @@ def rank_program(g, core, T, topo):
                 act(hf("ue", h), hf("ie", h), AF.Square)
             elif name == "un":
                 tt(hf("un", h), hf("qn", h), hf("PD", h), MUL)
-                spread("PD", h, 3)
+                spread("PD", h, "sta")
             elif name == "wn":
                 tt(hf("PN", h), hf("qn", h, 1024), hf("PN", h), MUL)
             elif name == "in":
@@ -626,147 +785,179 @@ def rank_program(g, core, T, topo):
                 tt(hf("PD", h), hf("un", h), hf("PD", h), MUL)
             elif name == "pg":
                 act(a("PG"), ind(a("PR"), a("rime", 0, 12)))
-                group(a("P7", 208, 220), [(sl("K0", 15 - i), a("PG", i, 192, 16)) for i in range(16)])
+            elif name == "early":
+                if h == 0:
+                    group(a("P7", 0, 192), [(sl("ND"), rim(r - 1)), (sl("NR"), rim(r - 1)), (sl("CE0"), a("PG")), (sl("CE4"), a("PG"))])
+                else:
+                    act(a("se", 192 * r, 192 * r + 192), a("P7", 0, 192), AF.Relu)
+                    spray("e", r, a("se", 192 * r, 192 * r + 192))
             elif name == "l":
                 if h == 0:
-                    ts(a("rl", 0, 12), a("P7", 208, 220), 128.0, EQ)
+                    terms = [(sl("KY", 15 - i), a("PG", i, 192, 16)) for i in range(16)]
+                    if r < RO:
+                        group(a("P7", 192, 204), terms)
+                    group(a("P7", 204, 216), [(sl("I"), a("krim", 0, 12))] + terms)
                 elif h == 1:
-                    tt(a("rl", 16, 28), a("rl", 0, 12), a("erim", 0, 12), MUL)
+                    if r < RO:
+                        tt(a("rl", 0, 12), a("P7", 192, 204), a("erim", 0, 12), MIN)
+                        tt(a("rl", 16, 28), a("P7", 192, 204), a("erim", 16, 28), MIN)
+                    ts(a("glist", 0, 12), a("P7", 204, 216), 255.75, MIN, 4.0, MUL)
+                elif r == RO:
+                    pass
                 elif h == 2:
-                    tt(a("rl", 32, 44), a("rl", 16, 28), a("P7", 208, 220), ADD)
+                    for b in range(2):
+                        mm(a("P6", b, 24, 2), a("HH", 128 * b, 128 * b + 128), a("rl", 0, 12))
+                    cp(a("alist", 0, 12), a("rl", 16, 28))
                 else:
-                    ts(a("alist", 0, 12), a("rl", 32, 44), 128.0, ADD)
-            elif r == 1:
-                pass
+                    ts(a("slist", 0, 24), a("P6", 0, 24), c("off"), ADD)
+            elif name in "abcd":
+                chain(h, "abcd".index(name))
+            elif name == "hi":
+                ts(a("bits", 256 * h, 256 * h + 128), a("N0", 128 * h, 128 * h + 128), a("thr", 0, 1), GT)
+            elif name == "lo":
+                ts(a("bits", 256 * h + 128, 256 * h + 256), a("N0", 128 * h, 128 * h + 128), c("nth"), LT)
+            elif name == "dq":
+                tt(a("dq", 128 * h, 128 * h + 128), a("N0", 128 * h, 128 * h + 128), a("qe", 128 * h, 128 * h + 128), SUB)
+            elif name == "hot":
+                if h == 0:
+                    for f, win in enumerate(("WI", "WC")):
+                        act(a("IR", 192 * f, 192 * f + 192), ind(a(win), a("rime", 0, 12)))
+                else:
+                    onehots()
+            elif name == "const":
+                list_constants()
+            elif name == "put":
+                put_data()
+            elif name == "clock":
+                mm(a("P7", 256, 512), sl("IV"), a("mine"))
+            elif name == "meta":
+                take_meta(r, "PN")
+                put_meta("PN")
+            elif name == "new":
+                act(fresh(r), a("PD"))
+                if r == RO:
+                    rim_gifts(r)
+            elif name == "by":
+                if r == 2:
+                    pass
+                elif h == 0:
+                    group(a("PN", 512, 572), [(sl("K%d" % (r - 3), 15 - i), a("SW", i, V, 16)) for i in range(16)])
+                else:
+                    cp(a("colk", 60 * (r - 3), 60 * (r - 2)), a("PN", 512, 572))
             elif name == "v":
                 if h == 0:
-                    ts(a("sm", 320, 448), a("P7", 0, 128), 0.0, GT)
+                    act(a("sm", 0, 64), a("P7", 0, 64), AF.Relu, 1.0, -1.0)
+                    act(a("sm", 64, 128), a("P7", 0, 64), AF.Relu, 1.0, 1.0)
                 elif h == 1:
-                    tt(a("sm", 0, 128), a("sm", 320, 448), a("P7", 128, 256), MUL)
+                    quad(a("P7", 64, 128), [("AN", "dyn"), ("T3", "sta")], a("sm", 0, 64))
+                    quad(a("P7", 128, 192), [("QA", "mine")], a("sm", 64, 128))
                 else:
-                    ts(a("mo", 0, 128), a("sm", 0, 128), c("k"), ADD)
+                    ts(a("mo", 0, 128), a("P7", 64, 192), c("k"), ADD, 0.0, MAX)
             elif name == "gifts":
                 put_gifts(r - 1)
             elif name == "m":
                 act(hf("mm", h), ind(logw, a("mo", 32 * h, 32 * h + 32)))
+            elif name == "oo":
+                act(hf("oo", h), ind(logw, a("mo", 64 + 32 * h, 96 + 32 * h)))
             elif name == "own":
                 tt(hf("PF", h), hf("mm", h), hf("PD", h), SUB)
 
+        def sofar(k, h):
+            return a("N0", 128 * h, 128 * h + 128) if k == 3 else a("qa", 256 * k + 128 * h, 256 * k + 128 * h + 128)
+
         def chain(h, k):
-            o = 256 * k + 128 * h
-            tt(a("qa", o, o + 128), a("qe", 128 * h, 128 * h + 128) if k == 0 else a("qa", o - 256, o - 128),
+            tt(sofar(k, h), a("qe", 128 * h, 128 * h + 128) if k == 0 else sofar(k - 1, h),
                a("PF" if r > 1 else "PD", 512 * h + k, 512 * h + 512, 4), ADD if r > 1 else SUB)
 
-        for x in ORDER.split():
+        for x in (FIRST if r == 1 else ORDER).split():
             step(x[:-1], int(x[-1]))
-        mm(a("P6", 256, 512), sl("NM"), a("dyn"), True, False)
-        mm(a("P6", 256, 512), sl("NY"), a("yrow"), False, False)
-        mm(a("P7", 256, 512), sl("DB"), a("dyn"))
-        if r > 1:
-            act(a("oo"), ind(logw, a("mo", 64, 128)))
-        else:
-            second_constants()
-        for k in range(4):
-            chain(0, k)
-            chain(1, k)
-            if TAIL:
-                step("l", k)
-        qnew = a("qa", 768, 1024)
-        ts(a("bits", 0, 128), a("qa", 768, 896), a("thr", 0, 1), GT)
-        ts(a("bits", 128, 256), a("qa", 896, 1024), a("thr", 0, 1), GT)
-        ts(a("bits", 256, 512), qnew, c("nth"), LT)
-        mm(a("P6", 256, 512), sl("NC"), a("bits", 0, 256), False, False)
-        mm(a("P6", 256, 512), sl("NC"), a("bits", 256, 512), False, True)
-        tt(a("dq", 0, 128), a("qa", 768, 896), a("qe", 0, 128), SUB)
-        act(a("inv", 0, 256), a("P7", 256, 512), AF.Relu, 1.25)
-        act(a("inv", 256, 512), a("inv", 0, 256), AF.Identity, 0.25)
-        ts(a("WN", 0, CAP), a("P6", 256, 512), a("lohi", r, r + 1), MAX, a("lohi", 8 + r, 9 + r), MIN)
-        tt(a("dq", 128, 256), a("qa", 896, 1024), a("qe", 128, 256), SUB) if DQ else None
-        cp(a("sa", 192 * r, 192 * r + 192), ind(a("WN", 0, CAP + V), a("alist", 0, 12)))
-        send("a", r, 64, 0, 64)
-        cp(ind(a("WM"), el), a("WN", 0, CAP))
-        tt(a("dq", 128, 256), a("qa", 896, 1024), a("qe", 128, 256), SUB) if not DQ else None
-        new = a("QL", LOG + R * r - 512, LOG + R * r + 512)
-        if r < RO:
-            act(new, a("PD"))
-        if 1 < r < RO:
-            dma("G", new[0], T.oo[:], [("oo", 0, 1024), new[1]], [new[1]], True)
-        group(a("P7", 192, 204), [(sl("I"), a("krim", 0, 12))]
-              + [(sl("A", 15 - i), a("sa", 192 * r + i, 192 * r + 192, 16)) for i in range(16)])
-        cp(a("glist", 0, 12), a("P7", 192, 204))
-        if r < RO:
-            cp(ind(a("QL", 0, W), el), qnew)
-            tt(ind(a("QL", W, 2 * W), el), a("dq"), a("inv", 256, 512), MUL)
-            act(a("CW", 0, 256), a("dum"))
-            act(a("CX", 0, 256), a("dum"))
-            cp(a("sb", 384 * r, 384 * r + 384), ind(a("QL", 0, W + V), a("slist", 0, 24)))
-            send("b", r, 128, 0, 128)
-        else:
-            tt(new, a("oo"), a("PD"), ADD)
+        for h in range(2):
+            o = 128 * h
+            group(a("P6", 256 + o, 384 + o), [(sl("NM"), a("mine", o, o + 128)), (sl("NY"), a("yrow", o, o + 128)),
+                                              (sl("NC"), a("bits", 2 * o, 2 * o + 128)), (sl("NC"), a("bits", 2 * o + 128, 2 * o + 256))])
+        step("dq", 1)
+        wn = a("sa", 448 * (r - 1), 448 * (r - 1) + CAP)
+        ts(wn, a("P6", 256, 512), a("lohi", r, r + 1), MAX, a("lohi", 8 + r, 9 + r), MIN)
         if r == RO:
-            give("V", r)
-            cp(ind(a("QL", 0, W), el), qnew)
-            tt(ind(a("QL", W, 2 * W), el), a("dq"), a("inv", 256, 512), MUL)
-        if r == 1:
-            scaled(m("QA"), m("Q"), c("wA"))
-            ts(sl("x"), a("QG", 0, 128), 0.0, EQ, oh(0), MUL)
-            ts(sl("YT"), a("QG", 0, 128), 1.0, EQ, c("wd"), MUL)
-            tt(sl("YT"), sl("YT"), sl("x"), ADD)
+            give(r)
+        else:
+            tt(a("N1"), a("dq"), a("P7", 256, 512), MUL)
+        if r < RO:
+            act(rim(r), ind(a("sa", 448 * (r - 1), 448 * r), a("alist", 0, 12)))
+            spray("a", r, rim(r))
+            cp(ind(a("WM"), el), wn)
+            act(a("sb", 384 * r, 384 * r + 384), ind(a("QL", 0, S + CAP + V), a("slist", 0, 24)))
+            send("b", r, 128)
+            rim_gifts(r)
+        else:
+            cp(ind(a("WM"), el), wn)
+            tt(a("N1"), a("dq"), a("P7", 256, 512), MUL)
 
-    dma("S", T.y0[:], T.QL[:, 0:V], [("QL", 0, V)], [])
-    dma("S", T.y1[:], T.QL[:, W:W + V], [("QL", W, W + V)], [])
-    group(a("P6", 0, 240), [(sl("QA", 12 - 4 * j), a("WM", j, V, 4)) for j in range(4)])
-    act(a("f1"), a("P6", 0, 240))
-    for h in range(2):
-        mm(a("PF", 512 * h, 512 * h + 480), sl("YT"), a("WM", 480 * h, 480 * h + 480))
-        act(a("yto", 480 * h, 480 * h + 480), a("PF", 512 * h, 512 * h + 480))
-    take_meta(RO)
-    dma("S", T.yt[:, 0:V], T.yto[0:128:16, :], [("yto", 0, V)], [])
-    dma("S", T.yt[:, V:2 * V], T.yto[1:128:16, :], [("yto", 0, V)], [])
     logw = a("QL", LOG, QLW)
 
-    def address(q):
-        P, lo, hi = ("P6", "P7")[q % 2], 60 * q, 60 * q + 60
-        group(a(P, 256, 316), [(sl("I"), a("FW", 720 + lo, 720 + hi))]
-              + [(sl("A", 15 - i), a("GG", 960 * q + i, 960 * q + 960, 16)) for i in range(16)])
+    def ports(eng, j):
+        take(eng, a("GG", 480 * j, 480 * j + 480), ind(a("WM"), a("colk", 30 * j, 30 * j + 30)))
 
-    def lists(q):
-        P, lo, hi = ("P6", "P7")[q % 2], 60 * q, 60 * q + 60
-        tt(a("f2", lo, hi), a(P, 256, 316), a("f1", lo, hi), GT)
-        tt(a("mn", lo, hi), a(P, 256, 316), a("f2", lo, hi), MUL)
-        ts(a("ml", lo, hi), a("mn", lo, hi), c("k"), ADD)
+    def clocks_out():
+        for h in range(2):
+            group(a(("P6", "P7")[h], 0, 480), [(sl(x), a("WM", 480 * h, 480 * h + 480)) for x in ("x", "YT")])
+            act(a("yto", 480 * h, 480 * h + 480), a(("P6", "P7")[h], 0, 480))
+        dma("S", T.yt[:, 0:V], T.inn[0:128:16, 0:V], [a("yto")[1]], [])
+        dma("S", T.yt[:, V:2 * V], T.inn[1:128:16, 0:V], [a("yto")[1]], [])
 
-    def fetch(eng, j):
-        take(eng, a("MM", 480 * j, 480 * j + 480), ind(logw, a("ml", 30 * j, 30 * j + 30)))
+    def bank(k):
+        return a(("PN", "PF")[k // 2], 256 + 512 * (k % 2), 316 + 512 * (k % 2))
 
-    def total(q):
-        P = a("PD" if q < 2 else "PF", 512 * (q % 2), 512 * (q % 2) + 240)
-        o = 960 * q
-        tt(P, a("MM", o, o + 960, 4), a("MM", o + 1, o + 960, 4), ADD)
-        tt(P, a("MM", o + 2, o + 960, 4), P, ADD)
-        tt(a("ymo", 240 * q, 240 * q + 240), a("MM", o + 3, o + 960, 4), P, ADD)
-        dma("S", T.ym[:, 240 * q:240 * q + 240], T.ymo[:, 240 * q:240 * q + 240], [("ymo", 240 * q, 240 * q + 240)], [])
+    def facing(k):
+        for i in range(16):
+            mm(bank(k), sl("F%d" % k, 15 - i), a("SW", i, V, 16), i == 0, False)
 
-    for q in range(4):
-        chunk("A", 2 * q)
-        chunk("V", 2 * q + 1)
-        address(q)
-        if q == 2:
-            take_gifts(RO, "PN")
-            put_gifts(RO, "PN")
-        if q > 0:
-            lists(q - 1)
-    fetch("A", 0)
-    fetch("A", 1)
-    lists(3)
-    fetch("V", 2)
-    fetch("A", 3)
-    total(0)
-    fetch("A", 4)
-    total(1)
-    fetch("A", 5)
-    fetch("V", 6)
-    fetch("A", 7)
-    total(2)
-    total(3)
+    def address(k):
+        for i in range(16):
+            mm(bank(k), sl("A", 15 - i), a("GG", 960 * k + i, 960 * k + 960, 16), False, i == 15)
+
+    def lists(n, k):
+        lo, hi = 60 * k, 60 * k + 60
+        if n == 0:
+            tt(a("f2", lo, hi), bank(k), a("f1", 0, 60), GT)
+        elif n == 1:
+            tt(a("mn", lo, hi), bank(k), a("f2", lo, hi), MUL)
+        else:
+            ts(a("ml", lo, hi), a("mn", lo, hi), float(k), ADD)
+
+    def fetch(k, h):
+        src = ind(logw, a("ml", 60 * k + 30 * h, 60 * k + 30 * h + 30))
+        out = a("ymo", 480 * h, 480 * h + 480) if k == 3 else a("MM", 960 * k + 480 * h, 960 * k + 480 * h + 480)
+        if k == 0:
+            act(out, src)
+        else:
+            tt(out, src, a("MM", 960 * k - 960 + 480 * h, 960 * k - 480 + 480 * h), ADD)
+        if k == 3:
+            dma("S", T.ym[:, 480 * h:480 * h + 480], out[0], [out[1]], [])
+
+    for k in range(4):
+        facing(k)
+    group(a("P6", 0, 60), [(sl("A", 15 - i), a("WM", i, V, 16)) for i in range(16)])
+    for x in LAST.split():
+        name, j = x[:-1], int(x[-1])
+        if name in ("A", "V"):
+            ports(name, j)
+        elif name == "own":
+            act(a("f1", 0, 60), a("P6", 0, 60))
+        elif name == "new":
+            tt(fresh(RO), a("oo"), a("PD"), ADD)
+        elif name == "q":
+            settle(j)
+            dma("S", (T.y0, T.y1)[j][:], a("Q%d" % j, 0, V)[0], [a("Q%d" % j, 0, V)[1]], [])
+        elif name == "at":
+            address(j)
+        elif name in "xyz":
+            lists("xyz".index(name), j)
+        elif name == "gifts":
+            take_gifts(RO, "PD", 0)
+            put_gifts(RO, "PD", 0)
+        elif name == "clocks":
+            clocks_out()
+        else:
+            fetch(j, "fg".index(name))
     emit()

from concourse.bass import DstId, RemoteDMATransfer
from concourse.mybir import AluOpType as ALU, ActivationFunctionType as AF

V, B, FP, CAP, RO = 960, 64, 192, 256, 6
W = 1408
S = CAP + W
R = 1216
LOG = 2 * S
QLW = LOG + R * RO + 704
SPL = 32
CUT = 168
QE1 = "V"
EARLY = "q0 q1 z7 z0 l0 z6 z1 l1 z2 l2 l7 z3 d1 d0 g0 l3 z4 e1 z5 e0"
LAST = "A0 own0 A1 new0 at0 A2 q0 A3 at1 q1 x0 A4 V5 gifts0 x1 y0 y1 z0 z1 at2 f0 g0 A6 A7 x2 f1 y2 g1 z2 at3 f2 x3 g2 y3 z3 clocks0 f3 g3"
ORDER = ("pg0 ue0 fb0 qn0 we0 un0 wn0 in0 v0 ie0 ue1 v1 qn1 v2 early0 we1 rn0 gifts0 re0 un1 sn0 wn1 early1 se0 ie1 in1 m0 l0 re1 s0 rn1 "
         "se1 l1 sn1 g0 m1 oo0 l2 own0 a0 l3 oo1 s1 b0 g1 c0 own1 clock0 d0 a1 hi0 b1 lo0 c1 by0 new0 dq0 d1 by1 hi1 lo1 meta0")
FIRST = ("ue0 const0 put0 fb0 qn0 pg0 l0 we0 ie0 we1 qn1 ue1 early0 re0 wn0 un0 in0 wn1 hot0 ie1 un1 rn0 l1 early1 se0 re1 sn0 in1 l2 rn1 "
         "se1 sn1 l3 s0 hot1 meta0 g0 a0 s1 clock0 b0 g1 c0 a1 d0 b1 hi0 c1 lo0 d1 dq0 hi1 lo1 new0")
F32, BF, I32, U16 = "float32", "bfloat16", "int32", "uint16"


def _sb(n, d=F32):
    return ("sbuf", [128, n], d)


SCRATCH = {
    "PD": ("psum", [128, 1024], F32), "PN": ("psum", [128, 1024], F32), "PF": ("psum", [128, 1024], F32),
    "P6": ("psum", [128, 512], F32), "P7": ("psum", [128, 512], F32),
    "QL": _sb(QLW), "WM": _sb(W, BF), "PR": _sb(V, BF), "PG": _sb(192, BF), "pm": _sb(64, BF), "cst": _sb(8, BF),
    "erim": _sb(32), "rl": _sb(32), "alist": _sb(16, U16), "LW": _sb(W, BF), "SW": _sb(W, BF), "GG": _sb(3840, BF),
    "TI": _sb(V, I32), "qb": _sb(2 * V, BF), "thr": _sb(8),
    "pt": _sb(240, I32), "rm": _sb(16, I32), "i1": _sb(240, I32), "i2": _sb(240, I32), "i3": _sb(240, I32), "i4": _sb(16, I32),
    "f1": _sb(240), "f2": _sb(240), "b1": _sb(240, BF), "b2": _sb(240, BF), "FW": _sb(960, BF),
    "colw": _sb(240, U16), "colk": _sb(240, U16), "leftb": _sb(240, BF),
    "pc": _sb(8, I32), "cc": _sb(64), "rowj": _sb(256), "j16": _sb(256), "QG": _sb(256), "QP": _sb(256), "OH": _sb(16), "OQ": _sb(4),
    "lohi": _sb(24), "J2": _sb(256), "JM": _sb(384, BF), "MT": _sb(144 * 45, BF), "BI": _sb(2048, BF),
    "yrow": _sb(256, BF), "yfor": _sb(192, BF), "eperm": _sb(V), "dneg": _sb(64), "R16": _sb(256), "R4": _sb(240),
    "ones": _sb(128), "rows": _sb(432),
    "rime": _sb(16, U16), "krim": _sb(16, BF), "slist": _sb(48, U16), "glist": _sb(16, U16),
    "mn": _sb(240), "can": _sb(64), "ncn": _sb(64), "inl": _sb(64, BF), "x1": _sb(64), "x2": _sb(64), "pos": _sb(64, U16),
    "CW": _sb(1216), "CX": _sb(1216), "sc": _sb(512), "el": _sb(16, U16), "nl": _sb(64, U16), "mo": _sb(256, U16),
    "dyn": _sb(256, BF), "sta": _sb(256, BF), "mine": _sb(256, BF), "qe": _sb(512), "sm": _sb(128, BF), "fb": _sb(768, BF),
    "FX": _sb(4096), "ie": _sb(1024), "inn": _sb(1024), "mm": _sb(1024), "oo": _sb(1024),
    "qa": _sb(768), "bits": _sb(512, BF), "dq": _sb(256),
    "sa": _sb(448 * 6, BF), "la": _sb(576 * 6, BF), "se": _sb(192 * 7, BF), "le": _sb(576 * 7, BF),
    "sb": _sb(384 * 6), "lb": _sb(384 * 6), "sg": _sb(192 * 7), "lg": _sb(192 * 7),
    "WI": _sb(V, BF), "WC": _sb(V, BF), "IR": _sb(384, BF), "oneb": _sb(480, BF), "SG": _sb(480, BF), "row2": _sb(256, BF),
    "HH": _sb(256), "neg": _sb(128, BF), "BW": _sb(384, BF), "away": _sb(512), "lose": _sb(512, BF), "CC": _sb(960, BF),
    "tie": _sb(192, BF),
    "ml": _sb(240, U16),
}
NDMA = 20
SEMAPHORES = (["cV", "cA", "cP", "cG"] + ["d%d" % i for i in range(NDMA)]
              + ["%s%d" % (s, r) for s in ("re", "rb", "rg", "te", "ta", "tb", "tg") for r in range(RO + 1)]
              + ["ra%d_%d" % (r, s) for r in range(1, RO) for s in range(4)])
PSUM = ("PD", "PN", "PF", "P6", "P7")


def _builder(g, T):
    ops, acc, bank = [], {}, {}
    queue = {"V": g.vector, "A": g.scalar, "P": g.tensor, "G": g, "S": g.sync}
    ndma = [0]

    def add(eng, fn, reads, writes, sem=None):
        me = len(ops)
        deps = set()
        for lst, wr in ((reads, False), (writes, True)):
            for x in lst:
                name, lo, hi = x[0], x[1], x[2]
                st = x[3] if len(x) > 3 else 1
                for (l2, h2, w2, o2, s2) in acc.get(name, ()):
                    if l2 < hi and lo < h2 and (wr or w2):
                        if eng == "P" and ops[o2][0] == "P":
                            continue
                        if st > 1 and s2 == st and (lo - l2) % st != 0 and ops[o2][0] == eng:
                            continue
                        deps.add(o2)
                if name in PSUM:
                    for b in range(lo // 512, (hi - 1) // 512 + 1):
                        d = bank.setdefault((name, b), {})
                        for e2 in d:
                            if e2 != eng:
                                deps.add(d[e2])
                        d[eng] = me
        for lst, wr in ((reads, False), (writes, True)):
            for y in lst:
                name, lo, hi = y[0], y[1], y[2]
                st = y[3] if len(y) > 3 else 1
                a = acc.setdefault(name, [])
                if wr and st == 1:
                    a[:] = [x for x in a if not (lo <= x[0] and x[1] <= hi)]
                a.append((lo, hi, wr, me, st))
        ops.append((eng, fn, deps, sem))
        return me

    def dma(eng, out, in_, reads, writes, adding=False):
        name = "d%d" % ndma[0]
        ndma[0] += 1
        if adding:
            return add(eng, lambda: g.dma_start(out, in_, accum_op=ALU.add).then_inc(T.sem[name], 16), reads, writes, (name, 16))
        return add(eng, lambda: queue[eng].dma_start(out, in_).then_inc(T.sem[name], 16), reads, writes, (name, 16))

    def emit():
        need, upto = set(), {}
        for i, (eng, fn, deps, sem) in enumerate(ops):
            last, keep = {}, set()
            for d in deps:
                if ops[d][3] is None:
                    last[ops[d][0]] = max(last.get(ops[d][0], -1), d)
                else:
                    keep.add(d)
            for e in last:
                if upto.get((eng, e), -1) < last[e]:
                    upto[(eng, e)] = last[e]
                    keep.add(last[e])
            ops[i] = (eng, fn, keep if eng != "X" else set(), sem)
            need |= ops[i][2]
        cnt = {"V": 0, "A": 0, "P": 0, "G": 0}
        token, seen, final = {}, {}, {}
        for i, (eng, fn, deps, sem) in enumerate(ops):
            if eng != "X":
                want = {}
                for d in deps:
                    s, v = token[d]
                    want[s] = max(want.get(s, 0), v)
                for s in sorted(want):
                    if seen.get((eng, s), 0) < want[s]:
                        queue[eng].wait_ge(T.sem[s], want[s])
                        seen[(eng, s)] = want[s]
            if sem is not None:
                if fn is not None:
                    fn()
                token[i] = sem
                final[sem[0]] = sem[1]
            else:
                ins = fn()
                if i in need:
                    cnt[eng] += 1
                    ins.then_inc(T.sem["c" + eng], 1)
                    token[i] = ("c" + eng, cnt[eng])
                    final["c" + eng] = cnt[eng]
        for s in sorted(final):
            if max([seen.get((e, s), 0) for e in queue]) < final[s]:
                g.wait_ge(T.sem[s], final[s])

    return add, dma, emit


def rank_program(g, core, T, topo):
    rank = T.rank_of(core)
    if rank is None:
        return
    N = len(T.cores)
    add, dma, emit = _builder(g, T)
    place = {"Q0": ("QL", CAP, W), "Q1": ("QL", S + CAP, W), "N0": ("QL", 0, CAP), "N1": ("QL", S, CAP),
             "qn": ("FX", 0, 2048), "ue": ("FX", 2048, 1024), "un": ("FX", 3072, 1024), "MM": ("FX", 0, 3840),
             "ymo": ("ie", 0, V), "yto": ("inn", 0, V)}

    def a(name, lo=0, hi=None, step=1, p0=0, p1=128):
        if name in place:
            name, o, n = place[name]
            lo, hi = lo + o, (n if hi is None else hi) + o
        if hi is None:
            hi = T[name].shape[1]
        if step == 1:
            return (T[name][p0:p1, lo:hi], (name, lo, hi))
        last = lo + (hi - lo - 1) // step * step
        return (T[name][p0:p1, lo:last + 1:step], (name, lo, last + 1, step))

    def top(b, name, lo, hi):
        return a(name, lo, hi, 1, 0, B * (b + 1))

    def ind(win, off):
        return (win[0].indirect(off[0]), win[1], off[1])

    def rd(*xs):
        out = []
        for x in xs:
            if isinstance(x, tuple):
                out += list(x[1:])
        return out

    def val(x):
        return x[0] if isinstance(x, tuple) else x

    def io(out, *ins):
        if len(out) == 3:
            return rd(*ins) + [out[1], out[2]], [out[1]]
        return rd(*ins), [out[1]]

    def cp(out, in_, extra=()):
        r, w = io(out, in_)
        add("V", lambda: g.vector.tensor_copy(out[0], in_[0]), r + list(extra), w)

    def tt(out, x, y, op):
        r, w = io(out, x, y)
        add("V", lambda: g.vector.tensor_tensor(out[0], x[0], y[0], op), r, w)

    def ts(out, x, s1, op0, s2=None, op1=None):
        r, w = io(out, x, s1, s2)
        if op1 is None:
            add("V", lambda: g.vector.tensor_scalar(out[0], x[0], val(s1), None, op0), r, w)
        else:
            add("V", lambda: g.vector.tensor_scalar(out[0], x[0], val(s1), val(s2), op0, op1), r, w)

    def scan(out, d0, d1, op0, op1):
        r, w = io(out, d0, d1)
        add("V", lambda: g.vector.tensor_tensor_scan(out[0], d0[0], d1[0], 0.0, op0, op1), r, w)

    def ms(out, c):
        add("V", lambda: g.vector.memset(out[0], c), [], [out[1]])

    def act(out, in_, func=AF.Copy, bias=None, scale=None):
        r, w = io(out, in_, bias, scale)
        kw = {}
        if bias is not None:
            kw["bias"] = val(bias)
        if scale is not None:
            kw["scale"] = val(scale)
        add("A", lambda: g.scalar.activation(out[0], in_[0], func, **kw), r, w)

    def take(eng, out, in_):
        if eng == "V":
            cp(out, in_)
        else:
            act(out, in_)

    def mm(out, lhsT, rhs, start=True, stop=True):
        add("P", lambda: g.tensor.matmul(out[0], lhsT[0], rhs[0], start, stop), rd(lhsT, rhs), [out[1]])

    def group(out, terms):
        for i, (l, r) in enumerate(terms):
            mm(out, l, r, i == 0, i == len(terms) - 1)

    def iota(out, pattern, base, cm, small=True):
        if small:
            add("G", lambda: g.iota(out[0], pattern, base, cm, allow_small_or_imprecise_dtypes=True), [], [out[1]])
        else:
            add("G", lambda: g.iota(out[0], pattern, base, cm), [], [out[1]])

    ADD, SUB, MUL, MAX, MIN = ALU.add, ALU.subtract, ALU.mult, ALU.max, ALU.min
    EQ, GT, GE, LE, LT = ALU.is_equal, ALU.is_gt, ALU.is_ge, ALU.is_le, ALU.is_lt
    SHR, AND = ALU.arith_shift_right, ALU.bitwise_and

    def pick(out, in_, pattern, base):
        add("G", lambda: g.affine_select(out[0], in_[0], pattern, EQ, 0.0, base, 1), rd(in_), [out[1]])

    def split(src):
        peers = [(src + d) % N for d in range(1, N)]
        eng = [e for e in topo.engines(T.cores[src], T.cores[peers[0]])
               if all([e in topo.engines(T.cores[src], T.cores[p]) for p in peers])]
        q = len(eng) // 4
        parts = [eng[0:q], eng[q:3 * q], eng[3 * q:4 * q]]
        return {p: parts[i] for i, p in enumerate(peers)}

    def count(s):
        return sum([len(x) for x in split(s).values()])

    def spray(kind, r, src):
        mask = 0
        for part in split(rank).values():
            for e in part:
                mask |= 1 << e
        land, ids, dsts = "l" + kind, [], []
        for d in range(1, N):
            rid, pid, _ = topo.addr(T.cores[(rank + d) % N])
            ids.append(DstId(rid=rid, pnc=pid))
            do = 576 * r + (N - d - 1) * 192
            dsts.append(T[land][:, do:do + 192])
        sem = "re%d" % r if kind == "e" else "ra%d_%d" % (r, rank)
        ls = "t%s%d" % (kind, r)
        tr = RemoteDMATransfer(dst_ids=ids, dma_engine_mask=mask, remote_sem=T.sem[sem], srcs=[src[0]], dsts=dsts)
        add("G", lambda: g.remote_dma_fused([tr], local_sem=T.sem[ls]), [src[1]], [], (ls, count(rank)))
        if kind == "e":
            add("X", None, [], [(land, 576 * r, 576 * r + 576)], (sem, sum([count(s) for s in range(N) if s != rank])))
            return
        for d in range(1, N):
            s, o = (rank + d) % N, 576 * r + 192 * (d - 1)
            add("X", None, [], [(land, o, o + 192)], ("ra%d_%d" % (r, s), count(s)))

    def send(kind, r, width):
        sbuf, lbuf = "s" + kind, "l" + kind
        base = r * 3 * width
        mine = split(rank)
        trs, n = [], 0
        for d in range(1, N):
            p = (rank + d) % N
            rid, pid, _ = topo.addr(T.cores[p])
            mask = 0
            for e in mine[p]:
                mask |= 1 << e
            n += len(mine[p])
            so = base + (d - 1) * width
            do = base + (N - d - 1) * width
            trs.append(RemoteDMATransfer(dst_ids=[DstId(rid=rid, pnc=pid)], dma_engine_mask=mask,
                                         remote_sem=T.sem["r%s%d" % (kind, r)],
                                         src=T[sbuf][:, so:so + width], dst=T[lbuf][:, do:do + width]))
        ls = "t%s%d" % (kind, r)
        add("G", lambda: g.remote_dma_fused(trs, local_sem=T.sem[ls]), [(sbuf, base, base + 3 * width)], [], (ls, n))
        got = sum([len(split(s)[rank]) for s in range(N) if s != rank])
        add("X", None, [], [(lbuf, base, base + 3 * width)], ("r%s%d" % (kind, r), got))

    def shift(name, d, o=0):
        return a(name, o + 16, o + 144) if rank < (rank + d) % N else a(name, o + 112, o + 240)

    col = {}

    def c(name):
        if name not in col:
            col[name] = len(col)
        return a("cc", col[name], col[name] + 1)

    mat = {}

    def m(name, lo=0, n=144):
        if name not in mat:
            mat[name] = len(mat)
        return a("MT", mat[name] * 144 + lo, mat[name] * 144 + lo + n)

    def sl(name, lo=0):
        return m(name, lo, 128)

    def oh(j):
        return a("OH", j, j + 1)

    def oq(j):
        return a("OQ", j, j + 1)

    def bi(i):
        return a("BI", 128 * i, 128 * i + 128)

    def weights(*chains, eng="A"):
        for i in range(max([len(ch[2]) for ch in chains])):
            for (name, first, terms) in chains:
                if i < len(terms) and eng == "A":
                    act(c(name), terms[i][0], AF.Identity, first if i == 0 else c(name), float(terms[i][1]))
                elif i < len(terms):
                    ts(c(name), terms[i][0], float(terms[i][1]), MUL, first if i == 0 else c(name), ADD)

    def scaled(out, base, w):
        act(out, base, AF.Copy, None, w)

    def rim(r):
        return a("sa", 448 * r + CAP, 448 * r + 448)

    def mine_of(land, r, d):
        s = 576 * r + 192 * (d - 1) + 64 * (N - d - 1)
        return a(land, s, s + 64)

    def take_meta(r, P):
        for d in range(1, N):
            o = 64 * (d - 1)
            keep = [(a("JM", 256, 384) if r == 1 else a("JM", 0, 128), a("WM", V + o, V + o + 64))] if r else []
            group(a(P, o, o + 64), keep + [(sl("NY"), a("yfor", o, o + 64)), (shift("JM", d), mine_of("le", r, d))])

    def put_meta(P):
        act(a("WM", V, V + FP), a(P, 0, 192))

    def take_data(r):
        for f in range(2):
            for d in range(1, N):
                s = 384 * r + 128 * (d - 1)
                src = a("lb", s + f, s + 128, 2) if r else a("lb", s + 64 * f, s + 64 * f + 64)
                mm(a("PN", 192 * f + 64 * (d - 1), 192 * f + 64 * d), shift("J2", d), src)

    def put_data():
        for f in range(2):
            act(a("Q%d" % f, V, V + FP), a("PN", 192 * f, 192 * f + 192))

    def take_gifts(r, P="P6", o=64):
        for d in range(1, N):
            s = 192 * r + 64 * (d - 1)
            mm(a(P, o + 64 * (d - 1), o + 64 * d), shift("J2", d), a("lg", s, s + 64))

    def put_gifts(r, P="P6", o=64):
        act(a("QL", LOG + R * r + 512, LOG + R * r + 704), a(P, o, o + 192))

    def fresh(r):
        return a("QL", LOG + R * r - 512, LOG + R * r + 512)

    def rim_gifts(r):
        act(a("f2", 0, 192) if r > 1 else a("sg", 192, 384), ind(fresh(r), a("glist", 0, 12)))

    def give(r):
        if r > 1:
            tt(a("sg", 192 * r, 192 * r + 192), ind(a("oo"), a("glist", 0, 12)), a("f2", 0, 192), ADD)
        send("g", r, 64)

    def clocks(eng, lo, hi):
        take(eng, a("GG", 16 * lo, 16 * hi), ind(a("WM"), a("colw", lo, hi)))

    def chunk(eng, j):
        clocks(eng, 30 * j, 30 * j + 30)

    def zterm(j, start, stop):
        for i in (2 * j, 2 * j + 1):
            mm(a("P6", 0, 240), sl("E", 15 - i), a("GG", 240 * i, 240 * i + 240), start and i == 2 * j, stop and i > 2 * j)

    def lterm(j):
        o = 512 * (j // 4) + 120 * (j % 4)
        group(a("PF", o, o + 120), [(sl("LK", 3 - k), a("GG", 480 * j + k, 480 * j + 480, 4)) for k in range(4)]
              + [(sl("LO"), a("WM", 120 * j, 120 * j + 120))])

    def keys(P, o, lo, hi):
        for i in range(lo, hi):
            mm(a(P, o, o + 60), sl("E", 15 - i), a("WM", 60 * i, 60 * i + 60), i == 0, i == 15)

    def duel(r, b):
        o, out = 448 * r + CAP + 64 * b, top(b, "PN", 512 * b, 512 * b + 128)
        own = (a("sa", o, o + 64 * b + 64), a("BW", 256, 384))
        tie = (a("tie", 64 * b, 128 * b + 64), a("oneb", 0, 128))
        if b == 0:
            group(out, [tie, own, (mine_of("la", r, 1), shift("BW", 1))])
        else:
            mm(out, *own, True, False)
            for d in (3, 2):
                mm(a("PN", 512, 640, 1, B * (d - 2), B * (d - 1)), mine_of("la", r, d), shift("BW", d), False, False)
            mm(out, *tie, False, True)
        for h in range(2):
            lo = 256 * b + 128 * h
            tt(top(b, "lose", lo, lo + 128), top(b, "PN", 512 * b, 512 * b + 128), top(b, "away", lo, lo + 128), GE)

    def deliver(b):
        for q in range(4):
            for h in range(2):
                lo, co = 256 * b + 128 * h + 32 * q, 480 * b + 60 * (2 * q + h)
                mm(a("P7", 0, 60, 1, 32 * q, 32 * q + 32), top(b, "lose", lo, lo + 32), top(b, "CC", co, co + 60), False, False)
        if b == 0:
            keys("P7", 0, 15, 16)

    def quad(out, terms, off=None):
        group(out, [(sl(nme, 12 - 4 * j), a(src, j, 256, 4)) for (nme, src) in terms for j in range(4)]
              + ([(sl("OFF"), off)] if off else []))

    def spread(dst, h, src, o=0):
        for k in range(4):
            mm(a(dst, 512 * h + k, 512 * h + 512, 4), bi(8 + k), a(src, o + 128 * h, o + 128 * h + 128))

    TIT = [("TI1", 0, 1), ("TI2", 0, 1)]
    add("V", lambda: g.vector.memset(T.TI[:], 0), [], [("TI", 0, V)] + TIT)
    dma("S", T.rm[:, 0:12], T.rim[:], [], [("rm", 0, 12)])
    dma("S", T.pt[:], T.port[:], [], [("pt", 0, 240)])
    dma("S", T.TI[0:128:16, :], T.t0[:], [], [("TI", 0, V)])
    dma("A", T.TI[5:128:16, :], T.d0[:], [], [TIT[0]])
    dma("S", T.TI[6:128:16, :], T.d0[:], [], [TIT[1]])
    dma("S", T.thr[:, 0:1], T.th[:], [], [("thr", 0, 1)])
    iota(a("pc", 0, 1), [[0, 1]], 0, 1, False)
    iota(a("rowj"), [[1, 256]], 0, 0)
    dma("S", T.qb[:, 0:V], T.q0[:], [], [("qb", 0, V)])
    dma("S", T.qb[:, V:2 * V], T.q1[:], [], [("qb", V, 2 * V)])
    for f, n in enumerate((16, 4, 2)):
        iota(a("rows", 144 * f, 144 * f + 144), [[1, 144 // n], [0, n]], 0, 0)
    iota(a("j16"), [[0, 16], [1, 16]], 0, 0)
    iota(a("QL", CAP + V, S + CAP), [[0, S - V]], 0, 0)
    ts(a("pc", 1, 2), a("pc", 0, 1), 15, AND)
    ts(a("pc", 2, 3), a("pc", 0, 1), 3, AND)
    ts(a("pc", 3, 4), a("pc", 0, 1), 12, AND)
    ts(a("pc", 4, 5), a("pc", 0, 1), 1, AND)
    ts(a("pc", 5, 6), a("pc", 0, 1), 4, SHR)
    for nme in ("p", "lane", "k", "q4", "odd", "g"):
        c(nme)
    cp(a("cc", 0, 6), a("pc", 0, 6))
    ms(a("WM", V, W), 0.0)
    ts(a("OH"), a("rowj", 0, 16), c("lane"), EQ)
    ts(a("OQ"), a("rowj", 0, 16, 4), c("q4"), EQ)
    ts(a("QP"), a("rowj"), c("p"), SUB)
    ts(c("k12"), c("k"), 12.0, ADD)
    weights(("lo0", oh(3), [(oh(1), 6), (oh(2), 10), (oh(6), 2)]),
            ("up0", oh(3), [(oh(0), 99), (oh(1), 6), (oh(2), 10), (oh(5), 2), (oh(6), 4)]),
            ("wd", oh(5), [(oh(1), -2), (oh(2), -1), (oh(3), 20), (oh(6), 1)]),
            ("wL", oh(4), [(oh(0), -1), (oh(8), 1)]), ("l3", 3.0, [(oh(4), 8), (oh(8), 12)]),
            ("n8", 1.0, [(oh(8), -1)]), ("g4", 3.0, [(c("g"), 4)]), ("g8", 1.0, [(c("g"), 8)]))
    act(a("P7", 0, 240), a("rowj", 0, 240), AF.Identity, c("lane"), 16.0)
    weights(("wb", c("wd"), [(oh(0), 1)]), ("l60", 1216.0, [(c("lane"), -60)]), ("no0", 0.0, [(oh(0), -1)]))
    ts(a("QG"), a("QP"), c("lane"), ADD)
    ts(a("J2", 0, 128), a("QP", 0, 128), 0.0, EQ)
    ts(a("i4", 0, 12), a("rm", 0, 12), 2, SHR)
    ts(a("J2", 128, 256), a("QP", 0, 128), 0.0, EQ)
    cp(a("rime", 0, 12), a("i4", 0, 12))
    ts(m("C15"), a("QG", 0, 144), 15.0, EQ)
    ts(m("P4"), a("QG", 0, 144), c("k12"), EQ)
    ts(a("i1"), a("pt"), 2, SHR)
    ts(a("P6", 0, 240), a("pt"), -2880.0, ADD)
    ts(rim(0), ind(a("TI"), a("rime", 0, 12)) + tuple(TIT), c("lo0"), MAX, c("up0"), MIN)
    spray("e", 0, rim(0))
    for j in range(4):
        scaled(m("T%d" % j), m("P4"), oq(j))
    act(a("Q0", 0, V), a("qb", 0, V))
    act(a("Q1", 0, V), a("qb", V, 2 * V))
    tt(a("P6", 0, 240), a("i1"), a("P6", 0, 240), MAX)
    tt(a("b2"), a("pt"), a("P7", 0, 240), GT)
    ts(a("erim", 16, 28), a("P7", 0, 12), float(CAP), ADD)
    cp(a("FW", 0, 240), a("P6", 0, 240))
    ts(a("P7", 256, 496), a("pt"), float(4 * V + B * (N - 1 - rank)), GE, 0.5, ADD)
    ts(a("i3"), a("pt"), 3, AND)
    tt(a("FW", 240, 480), a("P6", 0, 240), a("FW", 0, 240), SUB)
    tt(a("FW", 480, 720), a("b2"), a("P7", 256, 496), SUB)
    ts(a("FW", 720, 960), a("i3"), c("k"), SUB)
    for d in range(3):
        cp(a("slist", 8 * d, 8 * d + 4), a("i4", 4 * d, 4 * d + 4))
        ts(a("slist", 8 * d + 4, 8 * d + 8), a("i4", 4 * d, 4 * d + 4), float(S), ADD)
    act(a("sb", 0, 384), ind(a("QL", CAP, S + CAP + V), a("slist", 0, 24)))
    iota(a("yfor"), [[1, 48], [0, 4]], 128, 0)
    send("b", 0, 128)
    iota(a("R4"), [[0, 60], [-1000, 4]], 1000, 0)
    iota(a("ones"), [[0, 128]], 1, 0)
    scaled(a("JM", 0, 256), a("J2"), c("n8"))
    scaled(m("E"), m("C15"), c("wb"))
    for h in range(2):
        for j in range(4):
            group(a("PD", 512 * h + j, 512 * h + 480, 4),
                  [(sl("T%d" % j, 12 - 4 * f), a("FW", 240 * f + 120 * h, 240 * f + 120 * h + 120)) for f in range(4)])
    cp(a("colw"), a("P6", 0, 240))
    ts(a("WM", 0, V), a("TI"), c("lo0"), MAX, c("up0"), MIN)
    ts(sl("BD"), a("rows", 0, 128), c("g"), EQ)
    ts(m("Q"), a("rows", 144, 288), c("g4"), EQ)
    ts(m("NY"), a("QG", 0, 144), 8.0, EQ, oh(0), MUL)
    add("G", lambda: g.affine_select(sl("TR")[0], sl("BD")[0], [[1, 128]], GT, 0.0, 0, -1), rd(sl("BD")), [sl("TR")[1]])
    iota(a("eperm"), [[1, 60], [60, 16]], 64, 0)
    for k in range(4):
        scaled(m("K%d" % k), m("C15"), oh(8 + k))
    act(a("SW", 0, 480), a("PD", 0, 480))
    act(a("SW", 480, 960), a("PD", 512, 992))
    act(a("CX", 0, CAP), a("rowj"), AF.Silu, 1216.0)
    keys("P6", 240, 0, 16)
    for k in range(4):
        group(a("PN", k, 240, 4), [(sl("K%d" % k, 15 - i), a("SW", 60 * i, 60 * i + 60)) for i in range(16)])
    take_meta(0, "P7")
    ts(m("LK"), a("QG", 0, 144), c("l3"), EQ, c("wL"), MUL)
    ts(m("y"), a("QG", 0, 144), 7.0, EQ, c("no0"), MUL)
    ts(sl("LO"), sl("Q", 12), c("wb"), MUL)
    ts(sl("z"), sl("Q", 8), oh(0), MUL)
    cp(m("I", 0, 128), a("J2", 0, 128))
    tt(m("LK"), m("LK"), m("y"), ADD)
    tt(sl("LO"), sl("LO"), sl("z"), ADD)
    ms(a("cst"), -129.0)
    ts(a("R16"), a("j16"), c("lane"), EQ, 1.0e6, MUL)
    ts(a("dneg", 0, 60), a("rowj", 0, 60), -1.0, MUL, c("l60"), ADD)
    for i in range(16):
        ts(bi(i), sl("BD"), oh(i), MUL)
    weights(("wx", 0.0, [(oq(0), 2), (oq(1), -2)]), ("wy1", 0.0, [(oq(0), -0.5), (oq(1), 0.5)]),
            ("wy2", 0.0, [(oq(0), 0.5), (oq(1), 0.5)]), ("wnl", oq(0), [(oq(1), 1)]),
            ("dlo", 0.0, [(oq(2), -200), (oq(3), -200)]), ("prs", oh(0), [(oh(1), 1)]), ("pb", 0.0, [(oh(0), 128), (oh(1), -127)]))
    put_meta("P7")

    def late_constants():
        scaled(m("NL"), m("P4"), c("wnl"))
        for nme, wv in (("XM", "wx"), ("Y1", "wy1"), ("Y2", "wy2")):
            scaled(m(nme), m("P4"), c(wv))
        scaled(m("QD"), m("Q"), c("wd"))
        act(a("lohi", 16, 23), a("rowj", 0, 7), AF.Identity, c("pb"), oh(2))

    def rim_constants():
        iota(a("CW", 0, CAP), [[1, CAP]], 1216, 0)
        iota(a("SW", V, W), [[0, W - V]], 0, 0)
        iota(a("LW", V, W), [[0, W - V]], 0, 0)
        iota(a("QL", S + CAP + V, LOG + 704), [[0, LOG + 704 - S - CAP - V]], 0, 0)
        iota(a("N0"), [[0, CAP]], 0, 0)
        iota(a("yrow"), [[1, CAP]], -128, 0)
        for b in range(2):
            pick(a("HH", 128 * b, 128 * b + 128), a("ones"), [[-16, 8], [-1, 8], [0, 2]], -8 * b)
        iota(a("WI"), [[1, 16], [0, 60]], 0, 0)
        iota(a("WC"), [[0, 16], [1, 60]], 0, 0)
        iota(a("oneb"), [[0, 480]], 1, 0)
        pick(a("SG"), a("oneb"), [[-16, 8], [0, 60]], 0)
        iota(a("row2", 0, 128), [[0, 4], [100, 2], [1, 16]], 0, 0)
        iota(a("row2", 128, 256), [[0, 4], [-100, 2], [1, 16]], 100, 0)

    def last_constants():
        ts(a("i4", 0, 12), a("rm", 0, 12), 3, AND)
        ts(sl("NC"), a("rows", 289, 417), c("g8"), EQ)
        ts(c("nth"), a("thr", 0, 1), -1.0, MUL)
        ts(a("erim", 0, 12), a("rime", 0, 12), float(CAP), ADD)
        ms(a("neg"), -1.0 / 128)
        ts(a("krim", 0, 12), a("i4", 0, 12), 0.25, MUL)
        for d in range(1, N):
            ms(a("tie", B * (d - 1), B * d), -1.0 / 128 / 128 if rank < (rank + d) % N else 0.0)

    def list_constants():
        weights(("wy", oh(0), [(oh(1), 2048)]), ("ce0", 0.0, [(oh(1), -64)]), ("ce4", oh(2), [(oh(1), -64)]),
                ("off", 0.0, [(c("odd"), S)]))
        scaled(m("KY"), m("C15"), c("wy"))
        scaled(sl("NM"), sl("C15", 15), c("wb"))
        scaled(sl("CE0"), sl("C15", 15), c("ce0"))
        scaled(sl("CE4"), sl("C15", 11), c("ce4"))

    def second_constants():
        weights(("winv", 0.0, [(oh(1), 0.25), (oh(2), 0.5), (oh(3), -4.75), (oh(5), -0.5), (oh(6), -0.125)]),
                ("hi", oh(3), [(oh(0), 99), (oh(1), 5), (oh(2), 9), (oh(8), 200)]),
                ("lo", oh(3), [(oh(1), 4), (oh(2), 8), (oh(8), -128)]),
                ("n85", c("n8"), [(oh(3), 4)]), eng="V")
        for h in range(3):
            ts(a("BW", 128 * h, 128 * h + 128), sl("BD"), c("wb"), MUL, (1.0 if h == 2 else -1.0) / 64, MUL)
        ts(a("lohi", 0, 7), a("rowj", 0, 7), oh(4), MUL, c("lo"), ADD)
        ts(a("lohi", 8, 15), a("rowj", 0, 7), oh(4), MUL, c("hi"), ADD)
        ts(sl("IV"), sl("BD"), c("winv"), MUL)
        ts(a("JM", 256, 384), a("JM", 0, 128), c("n85"), MUL)
        ts(sl("ND"), sl("C15", 15), c("wd"), MUL)
        ts(sl("NR"), sl("C15", 11), oh(4), MUL, -1.0, MUL)

    def spare(r):
        if r == 1:
            late_constants()
        if r == 2:
            weights(("wan", 0.0, [(oq(2), R), (oq(3), 4)]), ("wA", 0.0, [(oh(4), R), (oh(8), 4)]), ("no4", 0.0, [(oh(4), -1)]))
            scaled(m("QN"), m("Q"), c("no4"))
            scaled(m("AN"), m("P4"), c("wan"))
            scaled(m("QA"), m("Q"), c("wA"))
            scaled(sl("OFF"), sl("I"), -8192.0)
        if r == 3:
            weights(*[("c%d" % k, oh(k), [(oh(4 + k), 1)]) for k in range(4)])
            for k in range(4):
                scaled(m("K%d" % k), m("C15"), c("c%d" % k))
        if r == 4:
            for k in range(4):
                scaled(m("F%d" % k), m("C15"), oh(12 + k))
        if r == 5:
            scaled(m("A"), m("C15"), c("wA"))
            scaled(sl("x"), sl("C15", 15), oh(0))
            scaled(sl("YT"), sl("C15", 14), c("wd"))

    def onehots():
        for b in range(2):
            o, n, P = 64 * b, 64 * b + 64, ("P6", "P7")[b]
            for h in range(2):
                group(top(b, P, 256 + 128 * h, 384 + 128 * h),
                      [(a("neg", 0, n), a("row2", 128 * h, 128 * h + 128)), (a("IR", o, o + n), bi(0))])
            group(top(b, "PF", 512 * b, 512 * b + 480), [(a("neg", 0, n), a("WC", 0, 480)), (a("IR", 192 + o, 192 + o + n), a("SG"))])
        for b in range(2):
            act(top(b, "away", 256 * b, 256 * b + 256), top(b, ("P6", "P7")[b], 256, 512), AF.Abs)
        for b in range(2):
            act(top(b, "mm", 512 * b, 512 * b + 480), top(b, "PF", 512 * b, 512 * b + 480), AF.Abs)
        for b in range(2):
            act(top(b, "CC", 480 * b, 480 * b + 480), top(b, "mm", 512 * b, 512 * b + 480), AF.Relu, 128.0, -128.0)

    rim_constants()
    last_constants()
    second_constants()
    el = a("el")

    def settle(f):
        cp(ind(a("Q%d" % f), el), a("N%d" % f))

    for r in range(1, RO + 1):
        todo = list(range(8))
        if r == 1:
            cp(a("leftb"), a("PN", 0, 240))
            mm(a("P6", 0, 240), sl("I"), a("leftb"), True, False)
            for j in range(4):
                chunk("A", j)
                chunk("V", 7 - j)
                zterm(j, False, False)
                zterm(7 - j, False, j == 3)
                if j < 3:
                    lterm(todo.pop(0))
            lterm(todo.pop(0))
            act(a("LW", 0, 480), a("PF", 0, 480))
            spare(r)
            scan(a("mn"), a("R4"), a("P6", 0, 240), MAX, MIN)
            tt(a("ncn", 0, 60), a("mn", 3, 240, 4), a("P6", 240, 300), LE)
        else:
            keys("P7", 0, 0, 15)
            mm(a("P6", 0, 240), sl("I"), a("leftb"), True, False)
            jc = CUT // 30
            for j in range(jc):
                chunk("A", j)
            clocks("A", 30 * jc, CUT)
            for j in range(7, jc, -1):
                chunk("V", j)
            clocks("V", CUT, 30 * jc + 30)
            plan = EARLY.split()
            for x in plan:
                j = int(x[1])
                if x[0] == "z":
                    zterm(j, False, x == [y for y in plan if y[0] == "z"][-1])
                elif x[0] == "l":
                    lterm(j)
                    todo.remove(j)
                elif x[0] == "d":
                    duel(r - 1, j)
                elif x[0] == "q":
                    settle(j)
                elif x[0] == "g":
                    give(r - 1)
                    if r > 2:
                        new = fresh(r - 1)
                        dma("G", new[0], T.oo[:], [("oo", 0, 1024), new[1]], [new[1]], True)
                else:
                    deliver(j)
            act(a("LW", 0, 480), a("PF", 0, 480))
            spare(r)
            scan(a("mn"), a("R4"), a("P6", 0, 240), MAX, MIN)
            tt(a("ncn", 0, 60), a("mn", 3, 240, 4), a("P7", 0, 60), LE)
        scan(a("inl", 0, 60), a("ones", 0, 60), a("ncn", 0, 60), ADD, SUB)
        for j in todo[:3]:
            lterm(j)
        if len(todo) < 4:
            act(a("LW", 480, 960), a("PF", 512, 992))
        group(a("P7", 300, 301), [(sl("I"), a("cst", 0, 1)), (sl("TR"), a("inl", 59, 60))])
        for j in todo[3:]:
            lterm(j)
        tt(a("x1", 0, 60), a("ncn", 0, 60), a("dneg", 0, 60), MUL)
        tt(a("x2", 0, 60), a("x1", 0, 60), a("inl", 0, 60), ADD)
        ts(a("pos", 0, 60), a("x2", 0, 60), a("P7", 300, 301), ADD, 128.0, ADD)
        ts(a("pm", 0, 60), a("x2", 0, 60), a("P7", 300, 301), ADD, 128.0, MIN)
        for i in range(16):
            o = 512 * (i // 8) + 60 * (i % 8)
            mm(a("PD", o, o + 60), bi(i), a("pm", 0, 60))
        take_data(r - 1)
        cp(ind(a("CW"), a("pos", 0, SPL)), a("eperm", 0, 16 * SPL))
        act(ind(a("CX"), a("pos", SPL, 60)), a("eperm", 16 * SPL, V), AF.Silu)
        if len(todo) > 3:
            act(a("LW", 480, 960), a("PF", 512, 992))
        for h in range(2):
            act(a("PR", 480 * h, 480 * h + 480), a("PD", 512 * h, 512 * h + 480), AF.Relu, a("lohi", 16 + r, 17 + r), c("prs"))
        if r > 1:
            put_data()
        scan(a("sc", 256, 512), a("R16"), a("CX", 0, 256), MAX, MIN)
        scan(a("sc", 0, 256), a("R16"), a("CW", 0, 256), MAX, MIN)
        tt(a("x1", 0, 16), a("sc", 15, 256, 16), a("sc", 271, 512, 16), MIN)
        ts(el, a("x1", 0, 16), -63.75, ADD)
        if r < RO:
            for win in ("CW", "CX"):
                iota(a(win, 0, CAP), [[1, CAP]], 1216, 0)
        act(a("sta"), ind(a("SW"), el))
        ts(a("dyn"), ind(a("LW"), el), c("dlo"), MAX)
        act(a("mine"), ind(a("WM"), el))
        mm(a("PN", 512, 768), sl("XM", 4), a("dyn"))
        quad(a("P6", 0, 64), [("NL", "sta")])
        group(a("PF", 512, 768), [(sl("Y1", 4), a("dyn")), (sl("QD", 4), a("mine"))])
        mm(a("PF", 768, 1024), sl("Y2", 4), a("dyn"))
        cp(a("qe", 0, 256), ind(a("Q0"), el))
        tt(a("fb", 0, 256), a("PN", 512, 768), a("sta"), MUL)
        cp(a("nl"), a("P6", 0, 64))
        take(QE1, a("qe", 256, 512), ind(a("Q1"), el))
        spread("PD", 0, "fb")
        tt(a("fb", 256, 512), a("PF", 512, 768), a("fb", 0, 256), MUL)
        spread("PF", 0, "fb", 256)
        logw = a("QL", LOG, LOG + R * r - 512)

        def hf(name, h, o=0):
            return a(name, o + 512 * h, o + 512 * h + 512)

        def step(name, h):
            lo, hi = 512 * h, 512 * h + 512
            if name == "ue":
                for k in range(4):
                    tt(a("ue", lo + k, hi, 4), a("qe", 128 * h, 128 * h + 128), a("PD", lo + k, hi, 4), MUL)
            elif name == "fb":
                tt(a("fb", 512, 768), a("PF", 768, 1024), a("fb", 0, 256), MUL)
                spread("PD", 1, "fb")
                spread("PF", 1, "fb", 256)
                if r > 1:
                    quad(a("P7", 0, 64), [("T2", "dyn"), ("QN", "mine")])
                spread("PN", 0, "fb", 512)
                spread("PN", 1, "fb", 512)
                if r > 1:
                    take_gifts(r - 1)
            elif name == "qn":
                for f in range(2):
                    act(hf("qn", h, 1024 * f), ind(a("Q%d" % f), a("nl", 32 * h, 32 * h + 32)))
            elif name == "we":
                for k in range(4):
                    tt(a("PF", lo + k, hi, 4), a("qe", 256 + 128 * h, 384 + 128 * h), a("PF", lo + k, hi, 4), MUL)
            elif name == "ie":
                tt(hf("ie", h), hf("ue", h), hf("PF", h), ADD)
            elif name == "re":
                act(hf("ie", h), hf("ie", h), AF.Relu, None, 0.03125)
            elif name == "se":
                act(hf("ue", h), hf("ie", h), AF.Square)
            elif name == "un":
                tt(hf("un", h), hf("qn", h), hf("PD", h), MUL)
                spread("PD", h, "sta")
            elif name == "wn":
                tt(hf("PN", h), hf("qn", h, 1024), hf("PN", h), MUL)
            elif name == "in":
                tt(hf("inn", h), hf("un", h), hf("PN", h), ADD)
            elif name == "rn":
                act(hf("inn", h), hf("inn", h), AF.Relu, None, -0.03125)
            elif name == "sn":
                act(hf("PN", h), hf("inn", h), AF.Square)
            elif name == "s":
                tt(hf("un", h), hf("ue", h), hf("PN", h), ADD)
            elif name == "g":
                tt(hf("PD", h), hf("un", h), hf("PD", h), MUL)
            elif name == "pg":
                act(a("PG"), ind(a("PR"), a("rime", 0, 12)))
            elif name == "early":
                if h == 0:
                    group(a("P7", 0, 192), [(sl("ND"), rim(r - 1)), (sl("NR"), rim(r - 1)), (sl("CE0"), a("PG")), (sl("CE4"), a("PG"))])
                else:
                    act(a("se", 192 * r, 192 * r + 192), a("P7", 0, 192), AF.Relu)
                    spray("e", r, a("se", 192 * r, 192 * r + 192))
            elif name == "l":
                if h == 0:
                    terms = [(sl("KY", 15 - i), a("PG", i, 192, 16)) for i in range(16)]
                    if r < RO:
                        group(a("P7", 192, 204), terms)
                    group(a("P7", 204, 216), [(sl("I"), a("krim", 0, 12))] + terms)
                elif h == 1:
                    if r < RO:
                        tt(a("rl", 0, 12), a("P7", 192, 204), a("erim", 0, 12), MIN)
                        tt(a("rl", 16, 28), a("P7", 192, 204), a("erim", 16, 28), MIN)
                    ts(a("glist", 0, 12), a("P7", 204, 216), 255.75, MIN, 4.0, MUL)
                elif r == RO:
                    pass
                elif h == 2:
                    for b in range(2):
                        mm(a("P6", b, 24, 2), a("HH", 128 * b, 128 * b + 128), a("rl", 0, 12))
                    cp(a("alist", 0, 12), a("rl", 16, 28))
                else:
                    ts(a("slist", 0, 24), a("P6", 0, 24), c("off"), ADD)
            elif name in "abcd":
                chain(h, "abcd".index(name))
            elif name == "hi":
                ts(a("bits", 256 * h, 256 * h + 128), a("N0", 128 * h, 128 * h + 128), a("thr", 0, 1), GT)
            elif name == "lo":
                ts(a("bits", 256 * h + 128, 256 * h + 256), a("N0", 128 * h, 128 * h + 128), c("nth"), LT)
            elif name == "dq":
                tt(a("dq", 128 * h, 128 * h + 128), a("N0", 128 * h, 128 * h + 128), a("qe", 128 * h, 128 * h + 128), SUB)
            elif name == "hot":
                if h == 0:
                    for f, win in enumerate(("WI", "WC")):
                        act(a("IR", 192 * f, 192 * f + 192), ind(a(win), a("rime", 0, 12)))
                else:
                    onehots()
            elif name == "const":
                list_constants()
            elif name == "put":
                put_data()
            elif name == "clock":
                mm(a("P7", 256, 512), sl("IV"), a("mine"))
            elif name == "meta":
                take_meta(r, "PN")
                put_meta("PN")
            elif name == "new":
                act(fresh(r), a("PD"))
                if r == RO:
                    rim_gifts(r)
            elif name == "by":
                if r == 2:
                    pass
                elif h == 0:
                    group(a("PN", 512, 572), [(sl("K%d" % (r - 3), 15 - i), a("SW", i, V, 16)) for i in range(16)])
                else:
                    cp(a("colk", 60 * (r - 3), 60 * (r - 2)), a("PN", 512, 572))
            elif name == "v":
                if h == 0:
                    act(a("sm", 0, 64), a("P7", 0, 64), AF.Relu, 1.0, -1.0)
                    act(a("sm", 64, 128), a("P7", 0, 64), AF.Relu, 1.0, 1.0)
                elif h == 1:
                    quad(a("P7", 64, 128), [("AN", "dyn"), ("T3", "sta")], a("sm", 0, 64))
                    quad(a("P7", 128, 192), [("QA", "mine")], a("sm", 64, 128))
                else:
                    ts(a("mo", 0, 128), a("P7", 64, 192), c("k"), ADD, 0.0, MAX)
            elif name == "gifts":
                put_gifts(r - 1)
            elif name == "m":
                act(hf("mm", h), ind(logw, a("mo", 32 * h, 32 * h + 32)))
            elif name == "oo":
                act(hf("oo", h), ind(logw, a("mo", 64 + 32 * h, 96 + 32 * h)))
            elif name == "own":
                tt(hf("PF", h), hf("mm", h), hf("PD", h), SUB)

        def sofar(k, h):
            return a("N0", 128 * h, 128 * h + 128) if k == 3 else a("qa", 256 * k + 128 * h, 256 * k + 128 * h + 128)

        def chain(h, k):
            tt(sofar(k, h), a("qe", 128 * h, 128 * h + 128) if k == 0 else sofar(k - 1, h),
               a("PF" if r > 1 else "PD", 512 * h + k, 512 * h + 512, 4), ADD if r > 1 else SUB)

        for x in (FIRST if r == 1 else ORDER).split():
            step(x[:-1], int(x[-1]))
        for h in range(2):
            o = 128 * h
            group(a("P6", 256 + o, 384 + o), [(sl("NM"), a("mine", o, o + 128)), (sl("NY"), a("yrow", o, o + 128)),
                                              (sl("NC"), a("bits", 2 * o, 2 * o + 128)), (sl("NC"), a("bits", 2 * o + 128, 2 * o + 256))])
        step("dq", 1)
        wn = a("sa", 448 * (r - 1), 448 * (r - 1) + CAP)
        ts(wn, a("P6", 256, 512), a("lohi", r, r + 1), MAX, a("lohi", 8 + r, 9 + r), MIN)
        if r == RO:
            give(r)
        else:
            tt(a("N1"), a("dq"), a("P7", 256, 512), MUL)
        if r < RO:
            act(rim(r), ind(a("sa", 448 * (r - 1), 448 * r), a("alist", 0, 12)))
            spray("a", r, rim(r))
            cp(ind(a("WM"), el), wn)
            act(a("sb", 384 * r, 384 * r + 384), ind(a("QL", 0, S + CAP + V), a("slist", 0, 24)))
            send("b", r, 128)
            rim_gifts(r)
        else:
            cp(ind(a("WM"), el), wn)
            tt(a("N1"), a("dq"), a("P7", 256, 512), MUL)

    logw = a("QL", LOG, QLW)

    def ports(eng, j):
        take(eng, a("GG", 480 * j, 480 * j + 480), ind(a("WM"), a("colk", 30 * j, 30 * j + 30)))

    def clocks_out():
        for h in range(2):
            group(a(("P6", "P7")[h], 0, 480), [(sl(x), a("WM", 480 * h, 480 * h + 480)) for x in ("x", "YT")])
            act(a("yto", 480 * h, 480 * h + 480), a(("P6", "P7")[h], 0, 480))
        dma("S", T.yt[:, 0:V], T.inn[0:128:16, 0:V], [a("yto")[1]], [])
        dma("S", T.yt[:, V:2 * V], T.inn[1:128:16, 0:V], [a("yto")[1]], [])

    def bank(k):
        return a(("PN", "PF")[k // 2], 256 + 512 * (k % 2), 316 + 512 * (k % 2))

    def facing(k):
        for i in range(16):
            mm(bank(k), sl("F%d" % k, 15 - i), a("SW", i, V, 16), i == 0, False)

    def address(k):
        for i in range(16):
            mm(bank(k), sl("A", 15 - i), a("GG", 960 * k + i, 960 * k + 960, 16), False, i == 15)

    def lists(n, k):
        lo, hi = 60 * k, 60 * k + 60
        if n == 0:
            tt(a("f2", lo, hi), bank(k), a("f1", 0, 60), GT)
        elif n == 1:
            tt(a("mn", lo, hi), bank(k), a("f2", lo, hi), MUL)
        else:
            ts(a("ml", lo, hi), a("mn", lo, hi), float(k), ADD)

    def fetch(k, h):
        src = ind(logw, a("ml", 60 * k + 30 * h, 60 * k + 30 * h + 30))
        out = a("ymo", 480 * h, 480 * h + 480) if k == 3 else a("MM", 960 * k + 480 * h, 960 * k + 480 * h + 480)
        if k == 0:
            act(out, src)
        else:
            tt(out, src, a("MM", 960 * k - 960 + 480 * h, 960 * k - 480 + 480 * h), ADD)
        if k == 3:
            dma("S", T.ym[:, 480 * h:480 * h + 480], out[0], [out[1]], [])

    for k in range(4):
        facing(k)
    group(a("P6", 0, 60), [(sl("A", 15 - i), a("WM", i, V, 16)) for i in range(16)])
    for x in LAST.split():
        name, j = x[:-1], int(x[-1])
        if name in ("A", "V"):
            ports(name, j)
        elif name == "own":
            act(a("f1", 0, 60), a("P6", 0, 60))
        elif name == "new":
            tt(fresh(RO), a("oo"), a("PD"), ADD)
        elif name == "q":
            settle(j)
            dma("S", (T.y0, T.y1)[j][:], a("Q%d" % j, 0, V)[0], [a("Q%d" % j, 0, V)[1]], [])
        elif name == "at":
            address(j)
        elif name in "xyz":
            lists("xyz".index(name), j)
        elif name == "gifts":
            take_gifts(RO, "PD", 0)
            put_gifts(RO, "PD", 0)
        elif name == "clocks":
            clocks_out()
        else:
            fetch(j, "fg".index(name))
    emit()
